import numpy as np, ml_dtypes
CORES = [16,18,20,22]
N = 4
import mx_ref
BF = ml_dtypes.bfloat16
def gcols(t, e):
    v = np.concatenate([t.reshape(8, 16, -1, 4), np.zeros((8, 16, 1, 4), BF)], axis=2)
    return np.ascontiguousarray(np.stack([v[g][:, e[g]] for g in range(8)])).reshape(128, -1)
def tile(rs):
    return np.stack(rs, axis=2).reshape(128, -1).astype(BF)
def cut(t, i, w=512):
    return t[:, w * i:w * i + w]
def pick(q, e):
    c = np.concatenate([q[0].reshape(128, -1, 4), np.zeros((128, 1, 4), np.uint8)], axis=1); s = np.concatenate([q[1], np.ones((16, 1), np.uint8)], axis=1)
    return (np.ascontiguousarray(c[:, e].reshape(128, -1)), np.ascontiguousarray(s[:, e]))
def join(*qs):
    return (np.concatenate([q[0] for q in qs], axis=1), np.concatenate([q[1] for q in qs], axis=1))
def put(q, e, v):
    c, s = q[0].reshape(128, -1, 4).copy(), q[1].copy(); c[:, e] = v[0].reshape(128, -1, 4); s[:, e] = v[1]
    return (c.reshape(128, -1), s)
def pk(c, s):
    return (np.ascontiguousarray(c), mx_ref.live(s))
def emit(q):
    return q[0], q[1]
def packed(v, rng):
    q = [mx_ref.quantize(np.ascontiguousarray(v[r])) for r in range(N)]
    return np.stack([a for a, b in q]), np.stack([mx_ref.plane(b, rng) for a, b in q])
def values_of_codes():
    e, c = np.zeros((128, 128, 4), np.float32), np.zeros((128, 2, 4), np.uint8)
    e[np.arange(128), np.arange(128), 0] = 1
    c[:127, :, 0] = np.arange(256).reshape(2, 128).T[:127]
    return mx_ref.matmul(mx_ref.quantize(e.reshape(128, 512).astype(BF)), (c.reshape(128, 8), np.full((16, 2), 127, np.uint8))).T.reshape(-1).astype(np.float64)
CODE_VALUE, SCALE_VALUE = values_of_codes(), 2.0 ** (np.arange(256) - 127.0)
def decode(q):
    return (CODE_VALUE[q[0]].reshape(16, 8, -1, 4) * SCALE_VALUE[q[1]][:, None, :, None] + 0.0).reshape(128, -1).astype(np.float32)
def f(rng, *shape):
    return mx_ref.flush((rng.standard_normal(shape, dtype=np.float32) * np.exp2(rng.integers(-2, 3, shape[:-1] + (1,)))).astype(BF))
def wide(rng, *shape, cols=0):
    v = rng.standard_normal(shape, dtype=np.float32) * np.exp2(rng.integers(-12, 13, shape)).astype(np.float32)
    if cols: v *= np.repeat(np.exp2(rng.integers(-cols, cols + 1, shape[:-2] + (1, shape[-1] // 4))) * (rng.random(shape[:-2] + (1, shape[-1] // 4)) > 0.0625), 4, axis=-1).astype(np.float32)
    return mx_ref.flush(v.astype(BF))
S, C, L, Q1, Q2, R = 384, 240, 96, 13, 46, 3
def numbers_of(rng):
    return {"x": np.array(f(rng, N, 128, 4 * C)), "u": np.array(f(rng, N, 128, 512)), "v": np.array(f(rng, N, 128, 512))}
def weights(rng, w):
    c, p = packed(w, rng)
    return {"wc": c, "ws": p}
def shift(rng, mix=False):
    w = np.zeros((128, 4, 128, 4), np.float32)
    i = np.arange(128)
    first = i[i % 16 < 8]
    i = i[(i % 16 >= 8) & (i % 16 < 14)]
    for b in range(4):
        w[i, b, i, b] = -64
        w[i + 2, b, i, b] = 64
        if mix: w[(first + 16) % 128, b, first, b] = 64
    return weights(rng, np.stack([w.reshape(128, 2048).astype(BF)] * N))
def planned(rng, a, step, k, mix=False):
    d = numbers_of(rng)
    x = d["x"].astype(np.float32).reshape(N, 8, 16, C, 4)
    g = ((a[..., None] >> np.arange(8)) & 1) * 2.0 ** np.arange(8) * step
    x[:, :, 8:] = g.reshape(4, N, 8, C, 2, 4).transpose(1, 2, 0, 4, 3, 5).reshape(N, 8, 8, C, 4)
    u = d["u"].reshape(N, 128, 128, 4)
    u[:, :, ::16] = 0
    for h in range(0, 128, 16): u[:, h + 8:h + 10, h] = k.astype(np.float32).astype(BF)[:, None, None]
    return {"x": d["x"], "u": u.reshape(N, 128, 512), "v": d["v"], **shift(rng, mix)}, x
def with_x(d, x):
    d["x"] = x.astype(np.float32).reshape(N, 128, 4 * C).astype(BF)
    return d
def setup_inputs(rng):
    return {**numbers_of(rng), **weights(rng, f(rng, N, 128, 2048))}
def setup_inputs_ties(rng):
    o = rng.permutation(N)
    a = rng.integers(0, 3, (4, N, 8, C))
    a[:, o[0]] = 1
    d, x = planned(rng, a, 1.0, np.ones(N))
    x[o[1]] = 0
    s = rng.integers(0, 6, (4, 8, C))
    x[o[2], :, 8:] = 0
    for i in range(4):
        x[o[2], :, 8 + 2 * i, :, 0] = (8 + s[i]) * 2.0 ** -33
        x[o[2], :, 9 + 2 * i, :, 0] = (9 + s[i]) * 2.0 ** -33
    u = d["u"].reshape(N, 128, 128, 4)
    for h in range(0, 128, 16):
        u[o[2], h + 8, h] = BF(9 * 2.0 ** -33)
        u[o[2], h + 9, h] = BF(-2.0 ** -30)
    d["u"] = u.reshape(N, 128, 512)
    return with_x(d, x)
def setup_inputs_near(rng):
    k = (np.arange(N) + rng.integers(N)) % N < N // 2
    k = np.where(k, 2.0 ** -30, 1.0)
    d, x = planned(rng, rng.integers(0, 256, (4, N, 8, C)), 2.0 ** -23, k)
    x[:, :, :8] = (0.25 + 0.75 * rng.random((N, 8, 8, C, 4))) * rng.choice([-1.0, 1.0], (N, 8, 8, C, 4))
    x[:, :, 0] = 0
    x[:, :, 0, :, 0] = (rng.permutation(8) % 2 * 2.0 - 1.0)[None, :, None]
    x[k < 1] *= np.float32(2.0 ** -7)
    u = d["u"].reshape(N, 128, 128, 4)
    for h in range(0, 128, 16): u[:, h, h, 0] = k.astype(np.float32).astype(BF)
    d["u"] = u.reshape(N, 128, 512)
    return with_x(d, x)
def setup_inputs_huge(rng):
    d = numbers_of(rng)
    x = 2.0 ** 30 * (0.6 + 0.4 * rng.random((N, 128, C, 4)))
    c = np.stack([rng.permutation(C) % 2 * 2.0 - 1.0 for r in range(N)])
    c[rng.permutation(N) < N // 2] = 1
    x *= c[:, None, :, None]
    u = d["u"].reshape(N, 128, 128, 4)
    s = np.stack([rng.permutation(8) % 2 * 2.0 - 1.0 for r in range(N)])
    u[:, :, ::16] = (2.0 ** 30 * (1 - 0.25 * rng.random((N, 128, 8, 4))) * s[:, None, :, None]).astype(np.float32).astype(BF)
    w = np.zeros((128, 4, 128, 4), np.float32)
    i = np.arange(128)
    for b in range(4): w[i, b, i, b] = 2.0 ** -10
    return with_x({"x": d["x"], "u": u.reshape(N, 128, 512), "v": d["v"], **weights(rng, np.stack([w.reshape(128, 2048).astype(BF)] * N))}, x)
def entering(m, h, rng):
    n = S // 16
    w = np.zeros(n, int)
    rest = L
    if m < 2:
        o = rng.permutation(n // 4)
        w[4 * o[0]:4 * o[0] + 4] = Q1 - h
        rest -= 4 * (Q1 - h)
        for i in o[1:]:
            c = min(rest, Q2 - 4 * h + int(m == 1 and i == o[1]))
            w[4 * i + rng.integers(4)] = c
            rest -= c
    elif m == 2:
        a = int(rng.integers(n))
        w[a] = Q1 + 1 - h
        rest -= Q1 + 1 - h
        for i in rng.permutation(n):
            if i // 4 != a // 4:
                w[i] = min(rest, Q1 - h)
                rest -= w[i]
    elif m == 3: w[rng.integers(n)] = L
    else: w = np.bincount(rng.integers(0, n, L), minlength=n)
    return w
def setup_inputs_crowd(rng):
    n = S // 16
    leaf = np.arange(C) * S // C // 16
    a = rng.integers(0, 256, (4, N, 8, C))
    a[3] = rng.integers(100, 104, (N, 8, C))
    stay = np.ones((N, 8, C), bool)
    m = np.stack([rng.permutation(8) for r in range(N)])
    gone = [[[0], [0, 1], [int(rng.integers(1, n - 2)), n - 1]][i % 3] for i in rng.permutation(N)]
    for r in range(N):
        for g in range(8):
            a[0, r, g] = rng.permutation(C)
            k = np.full(n, L // n)
            if m[r, g] == 6:
                other = np.setdiff1d(np.arange(n), gone[r])
                k[gone[r]] = C // n
                k[rng.permutation(other)] = (L - len(gone[r]) * (C // n) + np.arange(len(other))) // len(other)
            for i in range(n):
                e = rng.permutation(np.flatnonzero(leaf == i))
                if i == 0: e = np.concatenate([[0], e[e > 0]])
                stay[r, g, e[:k[i]]] = False
    for r in range(N):
        for g in range(8):
            if m[r, g] == 4: e = np.zeros(L, int)
            elif m[r, g] == 5: e = np.full(L, C - 1)
            else:
                if m[r, g] == 6:
                    room = Q1 - np.bincount(leaf[stay[r, g]], minlength=n)
                    room[gone[r]] = 0
                    first = np.zeros(6, int)
                    if gone[r][0] > 0:
                        c = gone[r][0] - 1
                        room[[c, n - 2]] -= 2
                        i = int(np.flatnonzero(stay[r, g] & (leaf == c))[-1])
                        first = np.array([i, i, C - 1, C - 1])
                    w = np.bincount(rng.permutation(np.repeat(np.arange(n), room))[:L - len(first)], minlength=n)
                else:
                    w = entering(m[r, g], C // n - L // n, rng)
                    first = np.zeros(L - int(np.sum(w)), int)
                e = np.concatenate([first] + [rng.choice(np.flatnonzero(stay[r, g] & (leaf == i)), w[i]) for i in np.flatnonzero(w)])
            s = (r - 1) % N
            b = rng.integers(C, 256, C)
            b[~stay[s, g][a[0, s, g]]] = rng.permutation(e)
            a[1, s, g] = b
    d, x = planned(rng, a, 1.0, np.ones(N), True)
    return with_x(d, x)
def setup_inputs_spread(rng):
    d = setup_inputs(rng)
    d["x"] = wide(rng, N, 128, 4 * C, cols=6)
    return d
def check_inputs(d):
    b = []
    for k in ("x", "u", "v"):
        a = np.abs(d[k].astype(np.float32))
        if not (np.isfinite(a).all() and ((a == 0) | (a >= 2.0 ** -30) & (a <= 2.0 ** 30)).all()): b.append("a value of " + k)
    for r in range(N):
        if ((d["wc"][r] & 127) == 127).any(): b.append("a code of wc that is no number")
        with np.errstate(over="ignore"): a = np.abs(decode(pk(d["wc"][r], d["ws"][r])))
        if not ((a == 0) | (a >= 2.0 ** -30) & (a <= 2.0 ** 30)).all(): b.append("a value of W (wc, ws)")
    return b
def respread(h, key, new):
    n = np.searchsorted(key[h], new, side="right")
    leaf = np.where(n > 0, h[np.maximum(n - 1, 0)], 0) // 16
    k = np.concatenate([key[h], new])
    i = np.argsort(k, kind="stable")
    src = np.concatenate([h, S + np.arange(L)])[i]
    at = src.copy()
    lf = np.concatenate([h // 16, leaf])[i]
    count = np.bincount(lf, minlength=S // 16)
    size = np.where(count <= Q1, 16, np.where(np.repeat(np.sum(count.reshape(-1, 4), axis=1), 4) <= Q2, 64, S))
    size[np.bincount(leaf, minlength=S // 16) == 0] = 0
    for w in (16, 64, S):
        for s in range(0, S, w):
            if (size[s // 16:(s + w) // 16] == w).any():
                e = np.flatnonzero(lf * 16 // w == s // w)
                at[e] = s + np.arange(len(e)) * w // len(e)
    to, kept = np.full(S, -1), np.zeros(S, np.float32)
    to[at] = src
    kept[at] = k[i]
    return to, kept
def reference(x, u, v, wc, ws):
    qu = [mx_ref.quantize(u[r]) for r in range(N)]
    lay = [pk(wc[r], ws[r]) for r in range(N)]
    start = np.arange(C) * S // C
    now, key, held = [], [], []
    for r in range(N):
        p = mx_ref.matmul(qu[r], mx_ref.quantize(x[r]))[::16] + np.float32(0.0)
        o = np.argsort(p, axis=1, kind="stable")
        e, k = np.full((8, S), -1), np.zeros((8, S), np.float32)
        e[:, start] = o
        k[:, start] = np.take_along_axis(p, o, axis=1)
        now.append(gcols(x[r], e))
        key.append(k)
        held.append(e >= 0)
    y, ol = np.zeros((N, 128, S), np.float32), np.zeros((N, 8, S), np.float32)
    oc, osc = np.zeros((N, 128, 4 * S), np.uint8), np.zeros((N, 16, S), np.uint8)
    for t in range(R):
        made, new, border = [], [], []
        for r in range(N):
            q = mx_ref.quantize(now[r])
            made.append(tile([mx_ref.matmul(pick(lay[r], np.arange(128 * b, 128 * b + 128)), q) * np.float32(0.015625) + now[r][:, b::4].astype(np.float32) for b in range(4)]))
            p = mx_ref.matmul(qu[r], mx_ref.quantize(made[r]))[::16] + np.float32(0.0)
            o = np.argsort(np.where(held[r], p, np.float32(np.inf)), axis=1, kind="stable")[:, :L]
            new.append(np.take_along_axis(p, o, axis=1))
            np.put_along_axis(held[r], o, False, axis=1)
            border.append(mx_ref.quantize(gcols(made[r], o)))
        came = decode(join(*border)).astype(BF)
        for r in range(N):
            e = (r - 1) % N
            to, k = np.full((8, S), -1), np.zeros((8, S), np.float32)
            for g in range(8): to[g], k[g] = respread(np.flatnonzero(held[r][g]), key[r][g], new[e][g])
            now[r] = gcols(np.concatenate([made[r], cut(came, e, 4 * L)], axis=1), to)
            key[r], held[r], ol[r] = k, to >= 0, to
    for r in range(N):
        q = mx_ref.quantize(now[r])
        y[r] = mx_ref.matmul(mx_ref.quantize(v[r]), q)
        oc[r], osc[r] = emit(q)
    return {"y": y, "ol": ol, "oc": oc, "osc": osc}

@@ -1,0 +1,628 @@
+from concourse.mybir import dt, AluOpType, AxisListType, ActivationFunctionType
+
+S, C, L, Q1, Q2, R = 384, 240, 96, 13, 46, 3
+ARR, OWN = 32, 128
+BIG = 2.0 ** 90
+MAGIC = 12582912.0
+UP = 0.4921875
+NA = 6
+NM = 6
+ND = 15 - NM
+CW = 256
+X4, U8, U16, BF, F32 = "float8_e4m3fn_x4", "uint8", "uint16", "bfloat16", "float32"
+
+
+def _sb(n, d):
+    return ("sbuf", [128, n], d)
+
+
+SCRATCH = {
+    "ps": ("psum", [128, 4096], F32),
+    "xs": _sb(960, BF), "us": _sb(512, BF), "vs": _sb(512, BF),
+    "qx": _sb(240, X4), "sx": _sb(240, U8), "qu": _sb(128, X4), "su": _sb(128, U8),
+    "qu2": _sb(128, X4), "su2": _sb(128, U8), "qv": _sb(128, X4), "sv": _sb(128, U8),
+    "qw": _sb(512, X4), "sw": _sb(512, U8), "qe": _sb(512, X4), "se": _sb(512, U8),
+    "ones": _sb(512, BF), "et": _sb(2048, BF),
+    "tb": _sb(2048, BF), "fi": _sb(1536, BF), "f64": _sb(1536, BF), "ti": _sb(1536, BF), "bt": _sb(512, BF),
+    "qf": _sb(384, X4), "sf": _sb(384, U8), "qt": _sb(384, X4), "st": _sb(384, U8),
+    "qb": _sb(384, X4), "sb": _sb(384, U8), "ql": _sb(320, X4), "sl": _sb(320, U8),
+    "yo": _sb(384, F32), "olr": _sb(384, F32),
+    "iota": _sb(512, F32), "t16": _sb(384, BF), "dm": _sb(384, BF), "mx": _sb(384, BF), "rs": _sb(384, BF),
+    "rs97": _sb(97 * ND, BF), "step": _sb(240, BF), "idmap": _sb(512, F32),
+    "xrow": _sb(192, BF), "xm": _sb(192, BF), "xw": _sb(192, BF),
+    "pint": _sb(8, "int32"), "zer": _sb(240, BF),
+    "tb2": _sb(512, BF), "tf2": _sb(512, F32), "inv": _sb(288, BF),
+    "pp": _sb(512, F32), "kk": _sb(240, F32), "wm": _sb(384, F32), "wf": _sb(384, F32),
+    "cmp": _sb(240 * (15 - NA), BF), "so": _sb(120 * (15 - NA), BF), "sa": _sb(241 * NA, BF),
+    "eq": _sb(240, BF), "cs": _sb(240, BF), "ex": _sb(240, BF),
+    "lrow": _sb(256, F32), "arow": _sb(96, F32), "atr": _sb(96, F32), "ax": _sb(96, F32),
+    "kt0": _sb(512, F32), "kt1": _sb(512, F32), "krow": _sb(240, F32), "kx": _sb(240, F32),
+    "strow": _sb(240, BF), "spb": _sb(256, BF), "spe": _sb(240, BF), "spx": _sb(528, BF),
+    "e1": _sb(384, BF), "e2": _sb(384, BF), "thx": _sb(32, BF), "jk": _sb(480, BF),
+    "mso": _sb(97 * ND, BF), "mcp": _sb(97 * ND, BF), "sf2": _sb(97 * NM, F32),
+    "vv": _sb(480, F32), "isa": _sb(240, BF), "aa": _sb(256, BF),
+    "qrow": _sb(256, F32), "cum": _sb(48, F32), "xx": _sb(144, F32), "tbl": _sb(192, F32),
+    "srw": _sb(624, F32), "srx": _sb(240, F32),
+    "sm": _sb(64 * 48, F32), "u16": _sb(32 * 16, U16),
+}
+for _t in range(R):
+    SCRATCH["sk%d" % _t] = _sb(6, F32)
+    SCRATCH["lk%d" % _t] = _sb(6, F32)
+
+POOLS = {"v": 48, "a": 32, "p": 12, "g": 12}
+LOADS = ["x", "u", "v", "wc", "ws"]
+SEMAPHORES = ([e + str(i) for e in POOLS for i in range(POOLS[e])] + ["ld_" + n for n in LOADS]
+              + ["ak%d" % t for t in range(R)] + ["ab%d" % t for t in range(R)] + ["sent", "out_s", "out_a"])
+
+
+def V(name, a, b, step=1):
+    return (name, a, b, step)
+
+
+def IND(win, off):
+    return ("*", win, off)
+
+
+def rank_program(g, core, T, topo):
+    rank = T.rank_of(core)
+    if rank is None:
+        return
+    nxt = T.cores[(rank + 1) % len(T.cores)]
+    rid, pid = topo.addr(nxt)[0], topo.addr(nxt)[1]
+    mask = topo.mask(core, nxt)
+    neng = len(topo.engines(core, nxt))
+    OP, AF = AluOpType, ActivationFunctionType
+    Q = {"v": g.vector, "a": g.scalar, "p": g.tensor, "g": g, "s": g.sync}
+
+    ops = []
+    known = {e: 0 for e in Q}
+    count = {e: [] for e in POOLS}
+    acc = {}
+    waited = {}
+
+    def clash(a, b):
+        if a[0] == "ps":
+            return a[1] // 512 <= (b[2] - 1) // 512 and b[1] // 512 <= (a[2] - 1) // 512
+        if a[2] <= b[1] or b[2] <= a[1]:
+            return False
+        if a[3] > 1 and a[3] == b[3]:
+            return (a[1] - b[1]) % a[3] == 0
+        return True
+
+    def flat(vs):
+        o = []
+        for v in vs:
+            if isinstance(v, tuple):
+                o += [v[1], v[2]] if v[0] == "*" else [v]
+        return o
+
+    def wait(e, i):
+        Q[e].wait_ge(T.sem[ops[i][0]], ops[i][1])
+        waited[ops[i][0]] = max(waited.get(ops[i][0], 0), ops[i][1])
+        known[e] |= ops[i][2] | (1 << i)
+
+    def before(e, reads, writes, more=()):
+        deps = set(more)
+        use = [(v, v[0] == "ps") for v in flat(reads)] + [(v, True) for v in flat(writes)]
+        for v, w in use:
+            for (u, uw, i) in acc.get(v[0], []):
+                if (w or uw) and clash(u, v):
+                    deps.add(i)
+        for i in sorted(deps, reverse=True):
+            if not known[e] >> i & 1:
+                wait(e, i)
+        return use
+
+    def note(use, sem, val, seen):
+        i = len(ops)
+        ops.append((sem, val, seen))
+        for v, w in use:
+            lst = acc.setdefault(v[0], [])
+            if w and v[3] == 1:
+                lst[:] = [r for r in lst if not (r[0][1] >= v[1] and r[0][2] <= v[2])]
+            lst.append((v, w, i))
+        return i
+
+    def run(e, reads, writes, call):
+        n, k = len(count[e]), POOLS[e]
+        use = before(e, reads, writes, [count[e][n - k]] if n >= k else [])
+        sem = e + str(n % k)
+        call().then_inc(T.sem[sem], 1)
+        count[e].append(note(use, sem, n // k + 1, known[e]))
+
+    def ap(v):
+        if not isinstance(v, tuple):
+            return v
+        if v[0] == "*":
+            return ap(v[1]).indirect(ap(v[2]))
+        return T[v[0]][:, v[1]:v[2]] if v[3] == 1 else T[v[0]][:, v[1]:v[2]:v[3]]
+
+    def cp(out, in_):
+        r, w = ([out[2]], [out[1]]) if out[0] == "*" else ([], [out])
+        run("v", r + [in_], w, lambda: g.vector.tensor_copy(ap(out), ap(in_)))
+
+    def tt(out, a, b, op):
+        run("v", [a, b], [out], lambda: g.vector.tensor_tensor(ap(out), ap(a), ap(b), op))
+
+    def ts(out, a, s1, op0, s2=None, op1=None):
+        if s2 is None:
+            run("v", [a, s1], [out], lambda: g.vector.tensor_scalar(ap(out), ap(a), ap(s1), None, op0))
+        else:
+            run("v", [a, s1, s2], [out], lambda: g.vector.tensor_scalar(ap(out), ap(a), ap(s1), ap(s2), op0, op1))
+
+    def scan(out, d0, d1, init, op0, op1):
+        run("v", [d0, d1, init], [out],
+            lambda: g.vector.tensor_tensor_scan(ap(out), ap(d0), ap(d1), ap(init), op0, op1))
+
+    def fill(out, c):
+        run("v", [], [out], lambda: g.vector.memset(ap(out), c))
+
+    def tr(out, in_):
+        run("v", [in_], [out], lambda: g.vector.transpose(ap(out), ap(in_)))
+
+    def quant(q, s, a, b, in_):
+        run("v", [in_], [V(q, a, b), V(s, a, b)],
+            lambda: g.vector.quantize_mx(ap(V(q, a, b)), ap(V(s, a, b)), ap(in_)))
+
+    def act(out, in_, func=AF.Copy, bias=None, scale=None, accum=None):
+        kw = {}
+        if bias is not None:
+            kw["bias"] = ap(bias)
+        if scale is not None:
+            kw["scale"] = ap(scale)
+        if accum is not None:
+            kw["accum_out"] = ap(accum)
+        run("a", [in_, bias, scale], [out, accum], lambda: g.scalar.activation(ap(out), ap(in_), func, **kw))
+
+    def mm(bank, wq, ws, wa, xq, xs, a, b):
+        o = V("ps", 512 * bank, 512 * bank + b - a)
+        w, wsc, x, xsc = V(wq, wa, wa + 128), V(ws, wa, wa + 128), V(xq, a, b), V(xs, a, b)
+        run("p", [w, wsc, x, xsc], [o],
+            lambda: g.tensor.matmul_mx(ap(o), ap(w), ap(wsc), ap(x), ap(xsc), True, True))
+
+    def iota(out, pattern, base=0, cm=0):
+        run("g", [], [out], lambda: g.iota(ap(out), pattern, base, cm, allow_small_or_imprecise_dtypes=True))
+
+    def const(out, c=0):
+        iota(out, [[0, len(range(out[1], out[2], out[3]))]], c)
+
+    def load(e, name, out, dst, src):
+        use = before(e, [], [out])
+        Q[e].dma_start(dst, src).then_inc(T.sem["ld_" + name], 16)
+        note(use, "ld_" + name, 16, known[e])
+
+    total = {"sent": 0, "out_s": 0, "out_a": 0}
+
+    def store(e, dst, src, reads):
+        before(e, reads, [])
+        Q[e].dma_start(dst, src).then_inc(T.sem["out_" + e], 16)
+        total["out_" + e] += 16
+
+    def send(dst, src, reads, sem):
+        before("g", reads, [])
+        g.remote_dma(dst, src, T.sem[sem], T.sem.sent, pid, rid, mask)
+        total["sent"] += neng
+
+    def landed(writes, sem, n):
+        note([(v, True) for v in writes], sem, n * neng, 0)
+
+    def PS(bank, a, b):
+        return V("ps", 512 * bank + a, 512 * bank + b)
+
+    def TB(b, a, e):
+        return V("tb", 512 * b + a, 512 * b + e)
+
+    slots = {}
+
+    def sm(name, a=0, b=24, step=1):
+        o = 64 * slots.setdefault(name, len(slots))
+        return V("sm", o + a, o + b, step)
+
+    lists = {}
+
+    def ul(name, a, b):
+        o = 32 * lists.setdefault(name, len(lists))
+        return V("u16", o + a, o + b)
+
+    def pick(out, row, n):
+        scan(out, V("mx", 0, n), row, 0.0, OP.add, OP.min)
+
+    def segsum(out, row, n):
+        scan(out, V("rs", 0, n), row, 0.0, OP.mult, OP.add)
+
+    load("a", "u", V("us", 0, 512), T.us[:], T.u[:])
+    load("s", "x", V("xs", 0, 960), T.xs[:], T.x[:])
+    load("s", "wc", V("qw", 0, 512), T.qw[:].bitcast(dt.uint8), T.wc[:])
+    load("s", "ws", V("sw", 0, 512), T.sw[:], T.ws[:])
+    load("s", "v", V("vs", 0, 512), T.vs[:], T.v[:])
+
+    scol = sm("s", 0, 1)
+    run("g", [], [V("pint", 0, 1)], lambda: g.iota(T.pint[:, 0:1], [[0, 1]], 0, 1))
+    iota(sm("c", 0, 32), [[1, 32]])
+    iota(sm("k2", 0, 48), [[1, 2], [16, 24]])
+    fill(V("rs", 0, 384), 1.0)
+    fill(ul("dest", 14, 16), C)
+    fill(sm("beta", 0, 16), -1.0)
+    fill(sm("ra", 0, 16), 0.0)
+    ts(V("pint", 1, 2), V("pint", 0, 1), 15, OP.bitwise_and)
+    fill(V("rs", 0, 384, 16), 0.0)
+    ts(V("pint", 2, 3), V("pint", 0, 1), 4, OP.logical_shift_right)
+    ts(ul("c16", 0, 8), sm("c", 0, 8), 16.0, OP.mult)
+    segsum(V("t16", 0, 384), V("rs", 0, 384), 384)
+    cp(scol, V("pint", 1, 2))
+    tt(V("pint", 2, 3), V("pint", 2, 3), V("pint", 0, 1), OP.add)
+    ts(ul("lw", 0, 16), sm("c", 0, 16), 16.0, OP.mult, 15.0, OP.add)
+    cp(ul("c", 0, 16), sm("c", 0, 16))
+    ts(V("pint", 2, 3), V("pint", 2, 3), 1, OP.bitwise_and)
+    ts(sm("beta", 0, NA), sm("c", 0, NA), 16.0, OP.mult, -1.0, OP.add)
+    ts(V("dm", 0, 384), V("t16", 0, 384), scol, OP.is_equal)
+    ts(V("mx", 0, 384), V("t16", 0, 384), scol, OP.is_le, BIG, OP.mult)
+    ts(sm("s", 2, 3), V("pint", 2, 3), 17.0, OP.mult, scol, OP.add)
+    fill(sm("mr", 24, 32), 95.0)
+    fill(sm("m2p", 0, 8), 0.0)
+    ts(ul("tw", 0, 1), sm("s", 2, 3), 16.0, OP.mult, 511.0, OP.min)
+
+    def more_vector():
+        ts(sm("yf", 0, 48), sm("k2", 0, 48), scol, OP.add, float(C) / S, OP.mult)
+        ts(sm("k240"), sm("k2"), scol, OP.add, float(C), OP.add)
+        ts(sm("yf", 0, 48), sm("yf", 0, 48), UP, OP.add, MAGIC, OP.add)
+        ts(sm("k240m"), sm("k240"), MAGIC, OP.add)
+        ts(V("tbl", 3, 192, 4), sm("yf", 0, 48), -MAGIC, OP.add)
+        ts(ul("qlo", 0, 24), sm("yf"), -MAGIC, OP.add)
+
+    def more_gpsimd():
+        const(V("pp", 0, OWN))
+        const(V("inv", 0, 16))
+        const(V("inv", 16 + C, 288))
+        iota(V("iota", 0, 512), [[1, 512]])
+        for b in range(4):
+            const(TB(b, 0, OWN))
+        iota(V("xrow", 0, 48), [[0, 2], [4, 6], [0, 4]])
+        iota(V("xrow", 48, 96), [[0, 2], [4, 6], [0, 4]], 4)
+        iota(V("xrow", 96, 144), [[0, 2], [1, 24]])
+        const(V("xrow", 144, 160))
+        iota(V("xrow", 160, 192), [[1, 8], [0, 4]])
+        iota(sm("m4", 0, 48), [[1, 2], [0, 6], [16, 4]])
+        iota(sm("n4"), [[4, 24]])
+        iota(sm("n4", 32, 64), [[4, 32]])
+        const(V("lrow", 0, 16))
+        const(V("tf2", L, 256))
+        const(V("tf2", 384, 512))
+        const(V("step", 0, L))
+        const(V("step", L, C), 1)
+        const(V("bt", 0, 128))
+        const(V("zer", 0, C))
+        const(V("spb", 0, 256))
+        const(V("spx", S, 528), C - L)
+        const(V("ones", 0, 512), 1)
+        for b in range(4):
+            o = V("et", 512 * b, 512 * b + 512)
+            run("g", [V("ones", 0, 512)], [o],
+                lambda: g.affine_select(ap(o), T.ones[:], [[-1, 512]], OP.is_equal, 0.0, b, 4))
+        const(V("rs97", 0, 97 * ND), 1)
+        const(V("rs97", 0, 97 * ND, 97))
+        const(V("vv", 0, 480))
+        const(V("kt0", 0, ARR))
+        const(V("kt1", 0, ARR))
+        const(V("aa", C, 256), OWN - 1)
+        const(V("cum", 0, 48))
+
+    def last_gpsimd():
+        const(V("srw", 0, 624))
+        const(V("idmap", 0, ARR), -1)
+        iota(V("idmap", ARR, OWN), [[1, L]], S)
+        iota(V("idmap", OWN, 512), [[1, S]])
+
+    def ranking(K):
+        def k(a, b):
+            return V(K[0], K[1] + a, K[1] + b)
+
+        def w(j):
+            return V("wf", 16 * j + 15, 16 * j + 16)
+
+        W = C + 1
+        for j in range(NA + 1):
+            if j < NA:
+                act(V("sa", W * j, W * j + C), k(0, C), AF.Sign, bias=w(j), scale=-1.0)
+            if j > 1:
+                o = W * (j - 1)
+                act(V("sa", o, o + 16 * j - 16), V("sa", o, o + 16 * j - 16), AF.Relu, scale=-1.0,
+                    accum=sm("ra", j - 1, j))
+
+        def total_of(j):
+            o = C * (j - NA)
+            scan(V("so", o // 2, o // 2 + 120), V("cmp", o, o + 120), V("cmp", o + 120, o + C),
+                 sm("eb", j, j + 1), OP.add, OP.add)
+
+        def rest():
+            tt(V("sa", C, W * NA, W), sm("eb", 0, NA), sm("ra", 0, NA), OP.subtract)
+            for j in range(NA):
+                o = W * j
+                act(V("sa", o + 16 * j, o + W), V("sa", o + 16 * j, o + W), AF.Relu, accum=sm("rb", j, j + 1))
+
+        extra = [lambda: tt(V("eq", 0, C), IND(V("wf", 0, C), ul("lw", 0, 15)), k(0, C), OP.is_equal),
+                 lambda: segsum(V("cs", 0, C), V("eq", 0, C), C),
+                 lambda: pick(V("ex", 0, C), V("cs", 0, C), C),
+                 lambda: tt(sm("eb", 0, 15), V("ex", 15, C, 16), sm("beta", 0, 15), OP.add),
+                 rest]
+        todo = list(range(NA, 15))
+        for j in range(NA, 15):
+            o = C * (j - NA)
+            ts(V("cmp", o, o + 16 * j), k(0, 16 * j), w(j), OP.is_le)
+            ts(V("cmp", o + 16 * j, o + C), k(16 * j, C), w(j), OP.is_lt)
+            if j - NA < len(extra):
+                extra[j - NA]()
+            else:
+                total_of(todo.pop(0))
+                total_of(todo.pop(0))
+        for j in todo:
+            total_of(j)
+        cp(ul("rk", 0, NA), sm("rb", 0, NA))
+        cp(ul("rk", NA, 15), V("so", 119, 120 * (15 - NA), 120))
+        return [(0, NA, sm("rb", 0, NA)), (NA, 15, V("so", 119, 120 * (15 - NA), 120))]
+
+    def parts(e, out, b, top, lst, a, z):
+        o = V(out, 4 * a + b, 4 * z, 4)
+        if e == "v":
+            ts(o, IND(TB(b, 0, top), lst), 0.015625, OP.mult)
+        else:
+            act(o, IND(TB(b, 0, top), lst), scale=0.015625)
+
+    quant("qu", "su", 0, 128, V("us", 0, 512))
+    run("v", [V("qu", 0, 128), ul("c16", 0, 8)], [V("qu2", 0, 128)], lambda: g.vector.tensor_copy(
+        T.qu2[:, 0:128].bitcast(dt.uint32), T.qu[:, 0:128].bitcast(dt.uint32).indirect(ap(ul("c16", 0, 8)))))
+    act(V("su2", 0, 128), IND(V("su", 0, 128), ul("c16", 0, 8)))
+    quant("qx", "sx", 0, C, V("xs", 0, 960))
+    mm(0, "qu2", "su2", 0, "qx", "sx", 0, C)
+    mm(1, "qu2", "su2", 0, "qx", "sx", 0, C)
+    more_gpsimd()
+    more_vector()
+    for b in range(2):
+        act(TB(b, OWN, OWN + C), V("xs", b, 960, 4), scale=64.0)
+    tt(V("wm", 0, C), PS(0, 0, C), V("dm", 0, C), OP.mult)
+    act(V("pp", OWN, OWN + C), PS(1, 0, C))
+    segsum(V("wf", 0, C), V("wm", 0, C), C)
+    ranking(V("pp", OWN, OWN + C))
+    for b in range(2, 4):
+        act(TB(b, OWN, OWN + C), V("xs", b, 960, 4), scale=64.0)
+    cp(IND(V("inv", 16, 16 + C), ul("rk", 0, 15)), V("iota", 0, C))
+    tr(V("tb2", 0, 256), V("inv", 16, 272))
+    tr(V("tb2", 256, 512), V("inv", 0, 256))
+    ts(ul("to", 0, 16), IND(V("tb2", 0, 512), ul("tw", 0, 1)), float(OWN), OP.add)
+
+    for t in range(R):
+        first, last = t == 0, t == R - 1
+        cw = 128 if first else CW
+        top = OWN + C if t < 2 else 512
+        kt, ktn = "kt%d" % (t % 2), "kt%d" % ((t + 1) % 2)
+        ch = [(0, cw), (cw, 256 if first else S)]
+
+        def lst(c):
+            return ul("to", ch[c][0] // 16, ch[c][1] // 16)
+
+        def qf(c):
+            a, z = ch[c]
+            quant("qf", "sf", a, z, V("fi", 4 * a, 4 * z))
+            for b in range(4):
+                mm(4 * c + b, "qw", "sw", 128 * b, "qf", "sf", a, z)
+
+        def f64(c):
+            a, z = ch[c]
+            ts(V("f64", 4 * a, 4 * z), V("fi", 4 * a, 4 * z), 64.0, OP.mult)
+
+        def add(c):
+            a, z = ch[c]
+            for b in range(4):
+                tt(TB(b, OWN + a, OWN + z), PS(4 * c + b, 0, z - a), V("f64", 4 * a + b, 4 * z, 4), OP.add)
+                act(V("ti", 4 * a + b, 4 * z, 4), TB(b, OWN + a, OWN + z), scale=0.015625)
+
+        def qt(c):
+            a, z = ch[c]
+            quant("qt", "st", a, z, V("ti", 4 * a, 4 * z))
+            mm(4 * c, "qu2", "su2", 0, "qt", "st", a, z)
+            if first:
+                mm(4 * c + 1, "qu2", "su2", 0, "qt", "st", a, z)
+
+        if first:
+            for c in range(2):
+                for b in range(4):
+                    parts("va"[b % 2], "fi", b, top, lst(c), *ch[c])
+                qf(c)
+            act(V(kt, OWN, OWN + C), IND(V("pp", 0, OWN + C), ul("to", 0, 15)))
+            f64(0)
+            f64(1)
+            add(0)
+            add(1)
+            qt(0)
+            tt(V("xm", 0, 192), V("xrow", 0, 192), V("dm", 0, 192), OP.mult)
+            qt(1)
+            segsum(V("xw", 0, 192), V("xm", 0, 192), 192)
+            cp(ul("xl", 0, 12), V("xw", 15, 192, 16))
+            for c in range(2):
+                a, z = ch[c][0], min(ch[c][1], C)
+                tt(V("wm", a, z), PS(4 * c, 0, z - a), V("dm", 0, z - a), OP.mult)
+                act(V("pp", OWN + a, OWN + z), PS(4 * c + 1, 0, z - a))
+            K, ids, ptop = V("pp", OWN, OWN + C), V("iota", OWN, OWN + C), OWN + C
+        else:
+            for c in range(2):
+                for b in range(4):
+                    if (c, b) != (1, 3):
+                        parts("a", "fi", b, top, lst(c), *ch[c])
+            cp(IND(V("srw", 0, 624), ul("d2", 0, 24)), V("iota", OWN, 512))
+            parts("v", "fi", 3, top, lst(1), *ch[1])
+            qf(0)
+            f64(0)
+            qf(1)
+            add(0)
+            f64(1)
+            qt(0)
+            add(1)
+            qt(1)
+            pick(V("srx", 0, C), V("srw", 0, C), C)
+            cp(ul("ids", 0, 15), V("srx", 15, C, 16))
+            act(V("pp", OWN, OWN + cw), PS(0, 0, cw))
+            act(V("pp", OWN + cw, 512), PS(4, 0, S - cw))
+            tt(V("wm", 0, C), IND(V("pp", 0, 512), ul("ids", 0, 15)), V("dm", 0, C), OP.mult)
+            act(V("kk", 0, C), IND(V("pp", 0, 512), ul("ids", 0, 15)))
+            K, ids, ptop = V("kk", 0, C), V("srw", 0, C), 512
+        segsum(V("wf", 0, C), V("wm", 0, C), C)
+        rk = ranking(K)
+        if not first:
+            act(V(kt, OWN, 512), IND(V(ktn, 0, top), ul("to", 0, 24)))
+            act(V("krow", 0, C), IND(V(kt, 0, 512), ul("ids", 0, 15)))
+
+        cp(IND(V("lrow", 16, 16 + C), ul("rk", 0, 15)), ids)
+        act(V("strow", 0, C), IND(V("step", 0, C), ul("rk", 0, 15)))
+        for a, z, v in rk:
+            act(sm("gp", a, z), v, AF.Identity, bias=-(2 * L - 1) * BIG, scale=2 * BIG)
+        act(sm("gn", 0, 15), sm("gp", 0, 15), scale=-1.0)
+        if first:
+            act(sm("o16", 0, 2), sm("c", 0, 2), AF.Identity, bias=scol)
+            act(sm("o64", 0, 48), sm("m4", 0, 48), AF.Identity, bias=scol)
+            act(sm("o16", 0, 2), sm("o16", 0, 2), scale=1.0 / 16)
+            act(sm("o64", 0, 48), sm("o64", 0, 48), scale=1.0 / 64)
+        tr(V("tf2", 0, L), V("lrow", 16, 16 + L))
+        tr(V("tf2", 256, 384), V("lrow", 0, 128))
+        cp(ul("l", 0, 16), IND(V("tf2", 0, 512), ul("tw", 0, 1)))
+        cp(V("arow", 0, L), IND(V("pp", 0, ptop), ul("l", 0, 6)))
+        tr(V("atr", 0, L), V("arow", 0, L))
+        sk, lk = "sk%d" % t, "lk%d" % t
+        cp(V(sk, 0, 6), V("atr", 0, L, 16))
+        send(T[lk][:], T[sk][:], [V(sk, 0, 6)], "ak%d" % t)
+        for b in range(4):
+            parts("a", "bt", b, OWN + ch[1][1], ul("l", 0, 6), 32, 128)
+        scan(V("spb", 1, C + 1), V("strow", 0, C), V("zer", 0, C), 0.0, OP.add, OP.add)
+        act(V("spx", 0, S), IND(V("spb", 0, 256), ul("qlo", 0, 24)))
+        pick(V("kx", 0, C), V(kt, OWN, OWN + C) if first else V("krow", 0, C), C)
+        o = 128 * t
+        quant("qb", "sb", o, o + 128, V("bt", 0, 512))
+        a = 0 if first else 32
+        la, lz = L * t + a, L * t + 128
+        send(T.ql[:, la:lz].bitcast(dt.uint8), T.qb[:, o + a:o + 128].bitcast(dt.uint8), [V("qb", o, o + 128)], "ab%d" % t)
+        send(T.sl[:, la:lz], T.sb[:, o + a:o + 128], [V("sb", o, o + 128)], "ab%d" % t)
+        if first:
+            last_gpsimd()
+
+        pick(V("spe", 0, C), V("spb", 0, C), C)
+        tt(sm("km", 0, 15), V("kx", 15, C, 16), sm("gp", 0, 15), OP.min)
+        tt(sm("gh", 0, 15), sm("k240", 0, 15), V("spe", 15, C, 16), OP.subtract)
+        if first:
+            quant("qe", "se", 0, 512, V("et", 0, 2048))
+        if last:
+            quant("qv", "sv", 0, 128, V("vs", 0, 512))
+        tt(sm("base", 0, 15), V("spe", 15, C, 16), sm("gn", 0, 15), OP.max)
+        pick(V("thx", 0, 32), V("spx", 16, 528, 16), 32)
+        act(sm("thr", 0, 2), V("thx", 15, 32, 16), AF.Identity, bias=0.5)
+        for j in range(2):
+            act(V("jk", C * j, C * j + C), V("spb", 1, C + 1), AF.Sign, bias=sm("thr", j, j + 1), scale=-1.0,
+                accum=sm("fs", j, j + 1))
+        pick(V("e1", 0, S), V("spx", 0, S), S)
+        tt(sm("base", 0, 15), sm("base", 0, 15), sm("gh", 0, 15), OP.min)
+        pick(V("e2", 0, S), V("spx", 1, S + 1), S)
+        lo, hi = V("spx", 0, S, 16), V("spx", 16, S + 1, 16)
+        tt(sm("sc"), hi, lo, OP.subtract)
+        tt(sm("rst", 0, 24), V("e1", 15, S, 16), lo, OP.subtract)
+        tt(sm("rst", 24, 48), V("e2", 15, S, 16), lo, OP.subtract)
+        ts(sm("sc13"), sm("sc"), float(Q1), OP.max)
+        act(V("mcp", L, 97 * ND, 97), sm("base", NM, 15), AF.Identity, bias=-128.0)
+        act(V("sf2", L, 97 * NM, 97), sm("base", 0, NM))
+        ts(ul("fs", 0, 2), sm("fs", 0, 2), 0.5, OP.mult, C / 2.0, OP.add)
+
+        landed([V(lk, 0, 6)], "ak%d" % t, 1)
+        cp(V("ax", 0, L), IND(V(lk, 0, 6), ul("c", 0, 6)))
+        A = V(kt, ARR, OWN)
+        tr(A, V("ax", 0, L))
+        for j in range(NM + 2):
+            if j < NM:
+                act(V("sf2", 97 * j, 97 * j + L), A, AF.Sign, bias=sm("km", j, j + 1), scale=-1.0)
+            if j > 1:
+                o = V("sf2", 97 * j - 194, 97 * j - 97)
+                act(o, o, AF.Relu, accum=sm("ta", j - 2, j - 1))
+        h = ND - 3
+        for j in range(ND):
+            ts(V("mcp", 97 * j, 97 * j + L), A, sm("km", NM + j, NM + j + 1), OP.is_lt)
+            if j == h + 1:
+                scan(V("mso", 0, 97 * h), V("rs97", 0, 97 * h), V("mcp", 0, 97 * h), 0.0, OP.mult, OP.add)
+        scan(V("mso", 97 * h, 97 * ND), V("rs97", 97 * h, 97 * ND), V("mcp", 97 * h, 97 * ND), 0.0, OP.mult, OP.add)
+        cp(ul("dest", 0, NM), sm("ta", 0, NM))
+        ts(ul("dest", NM, 15), V("mso", L, 97 * ND, 97), 128.0, OP.add)
+        cp(IND(V("vv", 0, 480), ul("dest", 0, 15)), ids)
+        act(V("qrow", 0, 256), IND(V("iota", 0, 512), ul("dest", 0, 16)))
+        act(V("cum", 1, 33), IND(V("qrow", 0, 256), ul("fs", 0, 2)))
+        act(V("xx", 0, 144), IND(V("cum", 0, 48), ul("xl", 0, 9)), AF.Identity, bias=UP)
+        act(V("isa", 0, C), V("vv", 0, C), AF.Relu, bias=1.0, scale=-1.0)
+        landed([V("ql", la, lz), V("sl", la, lz)], "ab%d" % t, 2)
+        for b in range(4):
+            mm(b, "qe", "se", 128 * b, "ql", "sl", L * t, L * t + 128)
+
+        LO, HI, CL = V("xx", 0, 48), V("xx", 48, 96), V("xx", 96, 144)
+        tt(sm("cnt"), V("cum", 1, 25), V("cum", 0, 24), OP.subtract)
+        act(sm("y16", 0, 24), sm("cnt"), scale=sm("o16", 0, 1))
+        act(sm("y16", 24, 48), sm("cnt"), scale=sm("o16", 1, 2))
+        for b in range(4):
+            act(TB(b, ARR, OWN), PS(b, ARR, OWN), scale=64.0)
+        tt(sm("c64", 0, 48), HI, LO, OP.subtract)
+        tt(sm("big"), sm("cnt"), sm("sc13"), OP.is_gt)
+        tt(sm("has"), sm("cnt"), sm("sc"), OP.is_gt)
+        ts(sm("w3"), sm("c64"), float(Q2), OP.is_gt, 3.0, OP.mult)
+        tt(sm("m1", 0, 12), sm("big", 0, 24, 2), sm("big", 1, 24, 2), OP.max)
+        tt(V("tbl", 0, 192, 4), CL, sm("rst", 0, 48), OP.add)
+        tt(sm("w3"), sm("w3"), sm("big"), OP.mult)
+        tt(sm("m2", 0, 6), sm("m1", 0, 12, 2), sm("m1", 1, 12, 2), OP.max)
+        run("v", [sm("w3")], [sm("f3", 0, 1)],
+            lambda: g.vector.tensor_reduce(ap(sm("f3", 0, 1)), ap(sm("w3")), AxisListType.X, OP.max))
+        tt(sm("has"), sm("has"), sm("n4"), OP.add)
+        ts(sm("m2p", 0, 6), sm("m2", 0, 6), 2.0, OP.mult, sm("f3", 0, 1), OP.max)
+        tt(sm("y64", 0, 48), sm("c64", 0, 48), sm("o64", 0, 48), OP.mult)
+        tt(sm("md", 0, 32), IND(sm("m2p", 0, 8), ul("xl", 10, 12)), sm("n4", 32, 64), OP.add)
+        scan(V("aa", 0, C), V("isa", 0, C), V("zer", 0, C), float(ARR - 1), OP.add, OP.add)
+        tt(sm("mr"), sm("md"), sm("has"), OP.max)
+        tt(V("tbl", 2, 192, 4), sm("y64", 0, 48), LO, OP.add)
+        pick(sm("mw", 0, 32), sm("mr", 0, 32), 32)
+        tt(V("tbl", 1, 192, 4), sm("y16", 0, 48), CL, OP.add)
+        cp(ul("md", 0, 2), sm("mw", 15, 32, 16))
+        ts(ul("qlo", 0, 32), IND(V("tbl", 0, 96), ul("md", 0, 2)), MAGIC, OP.add, -MAGIC, OP.add)
+        act(sm("r", 0, 32), IND(V("tbl", 0, 96), ul("md", 0, 2)), AF.Identity, bias=MAGIC)
+        act(sm("rh", 0, 32), IND(V("tbl", 96, 192), ul("md", 0, 2)), AF.Identity, bias=MAGIC)
+        act(V("e1", 0, S), IND(V("aa", 0, 256), ul("qlo", 0, 24)))
+        tt(V("wm", 0, S), IND(V("vv", 0, 256), ul("qlo", 0, 24)), V("dm", 0, S), OP.mult)
+        if not last:
+            const(V("vv", 0, C))
+        tt(sm("valid"), sm("rh"), sm("r"), OP.is_gt)
+        segsum(V("wf", 0, S), V("wm", 0, S), S)
+        if not last:
+            tt(sm("d1"), sm("r"), sm("k240m"), OP.subtract)
+        pick(V("e2", 0, S), V("e1", 0, S), S)
+        if not last:
+            tt(sm("d1"), sm("d1"), sm("valid"), OP.mult)
+        tt(sm("tw"), V("wf", 15, S, 16), V("e2", 15, S, 16), OP.max)
+        if not last:
+            tt(sm("d1"), sm("d1"), sm("k240"), OP.add)
+        tt(sm("tw"), sm("tw"), sm("valid"), OP.mult)
+        cp(ul("to", 0, 24), sm("tw"))
+        if not last:
+            cp(ul("d2", 0, 24), sm("d1"))
+
+    for c in range(2):
+        a, z = (0, CW) if c == 0 else (CW, S)
+        for b in range(4):
+            parts("va"[b % 2], "fi", b, 512, ul("to", a // 16, z // 16), a, z)
+        quant("qf", "sf", a, z, V("fi", 4 * a, 4 * z))
+        mm(c, "qv", "sv", 0, "qf", "sf", a, z)
+        store("s", T.oc[:, 4 * a:4 * z], T.qf[:, a:z].bitcast(dt.uint8), [V("qf", a, z)])
+    act(V("olr", 0, S), IND(V("idmap", 0, 512), ul("to", 0, 24)))
+    cp(V("yo", 0, CW), PS(0, 0, CW))
+    cp(V("yo", CW, S), PS(1, 0, S - CW))
+    for k in range(4):
+        store("s", T.osc[4 * k:4 * k + 4, :], T.sf[32 * k:32 * k + 4, :], [V("sf", 0, S)])
+    store("a", T.ol[:], T.olr[0:128:16, :], [V("olr", 0, S)])
+    store("a", T.y[:], T.yo[:], [V("yo", 0, S)])
+
+    lastval = {}
+    for sem, val, seen in ops:
+        lastval[sem] = max(lastval.get(sem, 0), val)
+    for sem in lastval:
+        if waited.get(sem, 0) < lastval[sem]:
+            g.wait_ge(T.sem[sem], lastval[sem])
+    for sem in total:
+        g.wait_ge(T.sem[sem], total[sem])

@@ -25,24 +25,24 @@ SCRATCH = {
     "ones": _sb(512, BF), "et": _sb(2048, BF),
     "tb": _sb(2048, BF), "fi": _sb(1536, BF), "f64": _sb(1536, BF), "ti": _sb(1536, BF), "bt": _sb(512, BF),
     "qf": _sb(384, X4), "sf": _sb(384, U8), "qt": _sb(384, X4), "st": _sb(384, U8),
+    "qz": _sb(128, X4), "sz": _sb(128, U8),
     "qb": _sb(384, X4), "sb": _sb(384, U8), "ql": _sb(320, X4), "sl": _sb(320, U8),
     "yo": _sb(384, F32), "olr": _sb(384, F32),
     "iota": _sb(512, F32), "t16": _sb(384, BF), "dm": _sb(384, BF), "mx": _sb(384, BF), "rs": _sb(384, BF),
-    "rs97": _sb(97 * ND, BF), "step": _sb(240, BF), "idmap": _sb(512, F32),
-    "xrow": _sb(192, BF), "xm": _sb(192, BF), "xw": _sb(192, BF),
-    "pint": _sb(8, "int32"), "zer": _sb(240, BF),
-    "tb2": _sb(512, BF), "tf2": _sb(512, F32), "inv": _sb(288, BF),
-    "pp": _sb(512, F32), "kk": _sb(240, F32), "wm": _sb(384, F32), "wf": _sb(384, F32),
+    "rs97": _sb(97 * ND, BF), "step": _sb(240, BF), "idmap": _sb(512, F32), "xrow": _sb(224, BF),
+    "pint": _sb(8, "int32"), "zer": _sb(240, BF), "tb2": _sb(512, BF), "inv": _sb(288, BF),
+    "pp": _sb(512, F32), "kk": _sb(240, F32), "wm": _sb(240, F32), "wf": _sb(240, F32),
     "cmp": _sb(240 * (15 - NA), BF), "so": _sb(120 * (15 - NA), BF), "sa": _sb(241 * NA, BF),
     "eq": _sb(240, BF), "cs": _sb(240, BF), "ex": _sb(240, BF),
-    "lrow": _sb(256, F32), "arow": _sb(96, F32), "atr": _sb(96, F32), "ax": _sb(96, F32),
+    "lrow": _sb(256, BF), "idb": _sb(384, BF), "wb": _sb(384, BF), "wb2": _sb(384, BF),
+    "arow": _sb(96, F32), "atr": _sb(96, F32), "ax": _sb(96, F32),
     "kt0": _sb(512, F32), "kt1": _sb(512, F32), "krow": _sb(240, F32), "kx": _sb(240, F32),
     "strow": _sb(240, BF), "spb": _sb(256, BF), "spe": _sb(240, BF), "spx": _sb(528, BF),
     "e1": _sb(384, BF), "e2": _sb(384, BF), "thx": _sb(32, BF), "jk": _sb(480, BF),
     "mso": _sb(97 * ND, BF), "mcp": _sb(97 * ND, BF), "sf2": _sb(97 * NM, F32),
-    "vv": _sb(480, F32), "isa": _sb(240, BF), "aa": _sb(256, BF),
-    "qrow": _sb(256, F32), "cum": _sb(48, F32), "xx": _sb(144, F32), "tbl": _sb(192, F32),
-    "srw": _sb(624, F32), "srx": _sb(240, F32),
+    "vv": _sb(480, BF), "isa": _sb(240, BF), "aa": _sb(256, BF),
+    "qrow": _sb(256, F32), "cum": _sb(48, F32), "xx": _sb(144, F32), "tbl": _sb(384, F32),
+    "srw": _sb(624, BF), "srx": _sb(240, BF),
     "sm": _sb(64 * 48, F32), "u16": _sb(32 * 16, U16),
 }
 for _t in range(R):
@@ -52,7 +52,7 @@ for _t in range(R):
 POOLS = {"v": 48, "a": 32, "p": 12, "g": 12}
 LOADS = ["x", "u", "v", "wc", "ws"]
 SEMAPHORES = ([e + str(i) for e in POOLS for i in range(POOLS[e])] + ["ld_" + n for n in LOADS]
-              + ["ak%d" % t for t in range(R)] + ["ab%d" % t for t in range(R)] + ["sent", "out_s", "out_a"])
+              + ["ak%d" % t for t in range(R)] + ["ab%d" % t for t in range(R)] + ["apad", "sent", "out_s", "out_a"])
 
 
 def V(name, a, b, step=1):
@@ -230,6 +230,11 @@ def rank_program(g, core, T, topo):
     def segsum(out, row, n):
         scan(out, V("rs", 0, n), row, 0.0, OP.mult, OP.add)
 
+    def turned(out, row, n, more):
+        tr(V("tb2", 0, n), V(row, 16, 16 + n))
+        tr(V("tb2", 256, 256 + min(n + 32, 256)), V(row, 0, min(n + 32, 256)))
+        ts(out, IND(V("tb2", 0, 512), ul("tw", 0, 1)), more, OP.add)
+
     load("a", "u", V("us", 0, 512), T.us[:], T.u[:])
     load("s", "x", V("xs", 0, 960), T.xs[:], T.x[:])
     load("s", "wc", V("qw", 0, 512), T.qw[:].bitcast(dt.uint8), T.wc[:])
@@ -241,7 +246,7 @@ def rank_program(g, core, T, topo):
     iota(sm("c", 0, 32), [[1, 32]])
     iota(sm("k2", 0, 48), [[1, 2], [16, 24]])
     fill(V("rs", 0, 384), 1.0)
-    fill(ul("dest", 14, 16), C)
+    fill(V("bt", 0, 512), 0.0)
     fill(sm("beta", 0, 16), -1.0)
     fill(sm("ra", 0, 16), 0.0)
     ts(V("pint", 1, 2), V("pint", 0, 1), 15, OP.bitwise_and)
@@ -258,8 +263,7 @@ def rank_program(g, core, T, topo):
     ts(V("dm", 0, 384), V("t16", 0, 384), scol, OP.is_equal)
     ts(V("mx", 0, 384), V("t16", 0, 384), scol, OP.is_le, BIG, OP.mult)
     ts(sm("s", 2, 3), V("pint", 2, 3), 17.0, OP.mult, scol, OP.add)
-    fill(sm("mr", 24, 32), 95.0)
-    fill(sm("m2p", 0, 8), 0.0)
+    quant("qz", "sz", 0, 128, V("bt", 0, 512))
     ts(ul("tw", 0, 1), sm("s", 2, 3), 16.0, OP.mult, 511.0, OP.min)
 
     def more_vector():
@@ -267,7 +271,6 @@ def rank_program(g, core, T, topo):
         ts(sm("k240"), sm("k2"), scol, OP.add, float(C), OP.add)
         ts(sm("yf", 0, 48), sm("yf", 0, 48), UP, OP.add, MAGIC, OP.add)
         ts(sm("k240m"), sm("k240"), MAGIC, OP.add)
-        ts(V("tbl", 3, 192, 4), sm("yf", 0, 48), -MAGIC, OP.add)
         ts(ul("qlo", 0, 24), sm("yf"), -MAGIC, OP.add)
 
     def more_gpsimd():
@@ -277,35 +280,46 @@ def rank_program(g, core, T, topo):
         iota(V("iota", 0, 512), [[1, 512]])
         for b in range(4):
             const(TB(b, 0, OWN))
-        iota(V("xrow", 0, 48), [[0, 2], [4, 6], [0, 4]])
-        iota(V("xrow", 48, 96), [[0, 2], [4, 6], [0, 4]], 4)
-        iota(V("xrow", 96, 144), [[0, 2], [1, 24]])
-        const(V("xrow", 144, 160))
-        iota(V("xrow", 160, 192), [[1, 8], [0, 4]])
-        iota(sm("m4", 0, 48), [[1, 2], [0, 6], [16, 4]])
-        iota(sm("n4"), [[4, 24]])
-        iota(sm("n4", 32, 64), [[4, 32]])
-        const(V("lrow", 0, 16))
-        const(V("tf2", L, 256))
-        const(V("tf2", 384, 512))
-        const(V("step", 0, L))
-        const(V("step", L, C), 1)
-        const(V("bt", 0, 128))
-        const(V("zer", 0, C))
-        const(V("spb", 0, 256))
-        const(V("spx", S, 528), C - L)
+        send(T.ql[:, 0:32].bitcast(dt.uint8), T.qz[:, 0:32].bitcast(dt.uint8), [V("qz", 0, 128)], "apad")
+        send(T.sl[:, 0:32], T.sz[:, 0:32], [V("sz", 0, 128)], "apad")
+        landed([V("ql", 0, 32), V("sl", 0, 32)], "apad", 2)
         const(V("ones", 0, 512), 1)
         for b in range(4):
             o = V("et", 512 * b, 512 * b + 512)
             run("g", [V("ones", 0, 512)], [o],
                 lambda: g.affine_select(ap(o), T.ones[:], [[-1, 512]], OP.is_equal, 0.0, b, 4))
+        iota(V("idb", 0, S), [[1, S]], OWN - 256)
+        const(V("lrow", 0, 16))
+        const(V("step", 0, L))
+        const(V("step", L, C), 1)
+        iota(sm("m4", 0, 48), [[1, 2], [0, 6], [16, 4]])
+        const(V("zer", 0, C))
+        const(V("spb", 0, 256))
+        const(V("spx", S, 528), C - L)
+        const(V("xrow", 0, 16))
+        iota(V("xrow", 16, 64), [[0, 2], [4, 6], [0, 4]])
+        iota(V("xrow", 64, 112), [[0, 2], [4, 6], [0, 4]], 4)
+        iota(V("xrow", 112, 160), [[0, 2], [1, 24]])
+        const(V("xrow", 160, 176))
+        iota(V("xrow", 176, 224), [[4, 12], [0, 4]], 3)
+        iota(sm("n4"), [[4, 24]])
+        const(sm("hz2", 24, 32), 95)
+        const(sm("any", 24, 32))
+        const(sm("rs4"), 1)
+        const(sm("rs4", 0, 24, 4))
         const(V("rs97", 0, 97 * ND), 1)
         const(V("rs97", 0, 97 * ND, 97))
-        const(V("vv", 0, 480))
         const(V("kt0", 0, ARR))
         const(V("kt1", 0, ARR))
-        const(V("aa", C, 256), OWN - 1)
+        const(V("aa", C, 256), OWN - 257)
         const(V("cum", 0, 48))
+        const(V("qrow", C, 256), C)
+
+    def more_scalar():
+        act(V("vv", 0, C), V("rs", 0, C), AF.Identity, bias=-256.0, scale=0.0)
+        act(V("vv", C, 480), V("rs", 0, C), AF.Identity, bias=-256.0, scale=0.0)
+        for b in range(4):
+            act(V("tbl", 192 + b, 384, 4), sm("yf", 0, 48), AF.Identity, bias=-MAGIC)
 
     def last_gpsimd():
         const(V("srw", 0, 624))
@@ -385,10 +399,9 @@ def rank_program(g, core, T, topo):
     ranking(V("pp", OWN, OWN + C))
     for b in range(2, 4):
         act(TB(b, OWN, OWN + C), V("xs", b, 960, 4), scale=64.0)
+    more_scalar()
     cp(IND(V("inv", 16, 16 + C), ul("rk", 0, 15)), V("iota", 0, C))
-    tr(V("tb2", 0, 256), V("inv", 16, 272))
-    tr(V("tb2", 256, 512), V("inv", 0, 256))
-    ts(ul("to", 0, 16), IND(V("tb2", 0, 512), ul("tw", 0, 1)), float(OWN), OP.add)
+    turned(ul("to", 0, 16), "inv", 256, float(OWN))
 
     for t in range(R):
         first, last = t == 0, t == R - 1
@@ -434,32 +447,30 @@ def rank_program(g, core, T, topo):
             add(0)
             add(1)
             qt(0)
-            tt(V("xm", 0, 192), V("xrow", 0, 192), V("dm", 0, 192), OP.mult)
             qt(1)
-            segsum(V("xw", 0, 192), V("xm", 0, 192), 192)
-            cp(ul("xl", 0, 12), V("xw", 15, 192, 16))
+            quant("qe", "se", 0, 256, V("et", 0, 1024))
             for c in range(2):
                 a, z = ch[c][0], min(ch[c][1], C)
                 tt(V("wm", a, z), PS(4 * c, 0, z - a), V("dm", 0, z - a), OP.mult)
                 act(V("pp", OWN + a, OWN + z), PS(4 * c + 1, 0, z - a))
-            K, ids, ptop = V("pp", OWN, OWN + C), V("iota", OWN, OWN + C), OWN + C
+            K, ids, ptop = V("pp", OWN, OWN + C), V("idb", 0, C), OWN + C
         else:
             for c in range(2):
                 for b in range(4):
                     if (c, b) != (1, 3):
                         parts("a", "fi", b, top, lst(c), *ch[c])
-            cp(IND(V("srw", 0, 624), ul("d2", 0, 24)), V("iota", OWN, 512))
+            cp(IND(V("srw", 0, 624), ul("d2", 0, 24)), V("idb", 0, S))
             parts("v", "fi", 3, top, lst(1), *ch[1])
             qf(0)
             f64(0)
             qf(1)
             add(0)
             f64(1)
+            pick(V("srx", 0, C), V("srw", 0, C), C)
             qt(0)
             add(1)
             qt(1)
-            pick(V("srx", 0, C), V("srw", 0, C), C)
-            cp(ul("ids", 0, 15), V("srx", 15, C, 16))
+            ts(ul("ids", 0, 15), V("srx", 15, C, 16), 256.0, OP.add)
             act(V("pp", OWN, OWN + cw), PS(0, 0, cw))
             act(V("pp", OWN + cw, 512), PS(4, 0, S - cw))
             tt(V("wm", 0, C), IND(V("pp", 0, 512), ul("ids", 0, 15)), V("dm", 0, C), OP.mult)
@@ -481,9 +492,7 @@ def rank_program(g, core, T, topo):
             act(sm("o64", 0, 48), sm("m4", 0, 48), AF.Identity, bias=scol)
             act(sm("o16", 0, 2), sm("o16", 0, 2), scale=1.0 / 16)
             act(sm("o64", 0, 48), sm("o64", 0, 48), scale=1.0 / 64)
-        tr(V("tf2", 0, L), V("lrow", 16, 16 + L))
-        tr(V("tf2", 256, 384), V("lrow", 0, 128))
-        cp(ul("l", 0, 16), IND(V("tf2", 0, 512), ul("tw", 0, 1)))
+        turned(ul("l", 0, 16), "lrow", L, 256.0)
         cp(V("arow", 0, L), IND(V("pp", 0, ptop), ul("l", 0, 6)))
         tr(V("atr", 0, L), V("arow", 0, L))
         sk, lk = "sk%d" % t, "lk%d" % t
@@ -496,10 +505,9 @@ def rank_program(g, core, T, topo):
         pick(V("kx", 0, C), V(kt, OWN, OWN + C) if first else V("krow", 0, C), C)
         o = 128 * t
         quant("qb", "sb", o, o + 128, V("bt", 0, 512))
-        a = 0 if first else 32
-        la, lz = L * t + a, L * t + 128
-        send(T.ql[:, la:lz].bitcast(dt.uint8), T.qb[:, o + a:o + 128].bitcast(dt.uint8), [V("qb", o, o + 128)], "ab%d" % t)
-        send(T.sl[:, la:lz], T.sb[:, o + a:o + 128], [V("sb", o, o + 128)], "ab%d" % t)
+        la, lz = L * t + 32, L * t + 128
+        send(T.ql[:, la:lz].bitcast(dt.uint8), T.qb[:, o + 32:o + 128].bitcast(dt.uint8), [V("qb", o, o + 128)], "ab%d" % t)
+        send(T.sl[:, la:lz], T.sb[:, o + 32:o + 128], [V("sb", o, o + 128)], "ab%d" % t)
         if first:
             last_gpsimd()
 
@@ -507,7 +515,7 @@ def rank_program(g, core, T, topo):
         tt(sm("km", 0, 15), V("kx", 15, C, 16), sm("gp", 0, 15), OP.min)
         tt(sm("gh", 0, 15), sm("k240", 0, 15), V("spe", 15, C, 16), OP.subtract)
         if first:
-            quant("qe", "se", 0, 512, V("et", 0, 2048))
+            quant("qe", "se", 256, 512, V("et", 1024, 2048))
         if last:
             quant("qv", "sv", 0, 128, V("vs", 0, 512))
         tt(sm("base", 0, 15), V("spe", 15, C, 16), sm("gn", 0, 15), OP.max)
@@ -526,6 +534,8 @@ def rank_program(g, core, T, topo):
         ts(sm("sc13"), sm("sc"), float(Q1), OP.max)
         act(V("mcp", L, 97 * ND, 97), sm("base", NM, 15), AF.Identity, bias=-128.0)
         act(V("sf2", L, 97 * NM, 97), sm("base", 0, NM))
+        if first:
+            turned(ul("xl", 0, 16), "xrow", 192, 0.0)
         ts(ul("fs", 0, 2), sm("fs", 0, 2), 0.5, OP.mult, C / 2.0, OP.add)
 
         landed([V(lk, 0, 6)], "ak%d" % t, 1)
@@ -547,10 +557,10 @@ def rank_program(g, core, T, topo):
         cp(ul("dest", 0, NM), sm("ta", 0, NM))
         ts(ul("dest", NM, 15), V("mso", L, 97 * ND, 97), 128.0, OP.add)
         cp(IND(V("vv", 0, 480), ul("dest", 0, 15)), ids)
-        act(V("qrow", 0, 256), IND(V("iota", 0, 512), ul("dest", 0, 16)))
+        act(V("qrow", 0, C), IND(V("iota", 0, 512), ul("dest", 0, 15)))
         act(V("cum", 1, 33), IND(V("qrow", 0, 256), ul("fs", 0, 2)))
         act(V("xx", 0, 144), IND(V("cum", 0, 48), ul("xl", 0, 9)), AF.Identity, bias=UP)
-        act(V("isa", 0, C), V("vv", 0, C), AF.Relu, bias=1.0, scale=-1.0)
+        act(V("isa", 0, C), V("vv", 0, C), AF.Relu, bias=-255.0, scale=-1.0)
         landed([V("ql", la, lz), V("sl", la, lz)], "ab%d" % t, 2)
         for b in range(4):
             mm(b, "qe", "se", 128 * b, "ql", "sl", L * t, L * t + 128)
@@ -564,44 +574,44 @@ def rank_program(g, core, T, topo):
         tt(sm("c64", 0, 48), HI, LO, OP.subtract)
         tt(sm("big"), sm("cnt"), sm("sc13"), OP.is_gt)
         tt(sm("has"), sm("cnt"), sm("sc"), OP.is_gt)
-        ts(sm("w3"), sm("c64"), float(Q2), OP.is_gt, 3.0, OP.mult)
-        tt(sm("m1", 0, 12), sm("big", 0, 24, 2), sm("big", 1, 24, 2), OP.max)
-        tt(V("tbl", 0, 192, 4), CL, sm("rst", 0, 48), OP.add)
+        tt(sm("y64", 0, 48), sm("c64", 0, 48), sm("o64", 0, 48), OP.mult)
+        scan(sm("any"), sm("rs4"), sm("big"), 0.0, OP.mult, OP.max)
+        tt(sm("hz"), sm("has"), sm("n4"), OP.add)
+        ts(sm("w3"), sm("c64"), float(Q2), OP.is_gt, 192.0, OP.mult)
+        tt(V("tbl", 1, 192, 4), sm("y64", 0, 48), LO, OP.add)
+        act(V("tbl", 3, 192, 4), V("tbl", 1, 192, 4))
+        tt(sm("hz2"), sm("hz"), sm("has"), OP.add)
         tt(sm("w3"), sm("w3"), sm("big"), OP.mult)
-        tt(sm("m2", 0, 6), sm("m1", 0, 12, 2), sm("m1", 1, 12, 2), OP.max)
+        tt(V("tbl", 0, 192, 4), CL, sm("rst", 0, 48), OP.add)
+        tt(sm("mr", 0, 32), IND(sm("any", 0, 32), ul("xl", 10, 12)), sm("hz2", 0, 32), OP.add)
         run("v", [sm("w3")], [sm("f3", 0, 1)],
             lambda: g.vector.tensor_reduce(ap(sm("f3", 0, 1)), ap(sm("w3")), AxisListType.X, OP.max))
-        tt(sm("has"), sm("has"), sm("n4"), OP.add)
-        ts(sm("m2p", 0, 6), sm("m2", 0, 6), 2.0, OP.mult, sm("f3", 0, 1), OP.max)
-        tt(sm("y64", 0, 48), sm("c64", 0, 48), sm("o64", 0, 48), OP.mult)
-        tt(sm("md", 0, 32), IND(sm("m2p", 0, 8), ul("xl", 10, 12)), sm("n4", 32, 64), OP.add)
-        scan(V("aa", 0, C), V("isa", 0, C), V("zer", 0, C), float(ARR - 1), OP.add, OP.add)
-        tt(sm("mr"), sm("md"), sm("has"), OP.max)
-        tt(V("tbl", 2, 192, 4), sm("y64", 0, 48), LO, OP.add)
         pick(sm("mw", 0, 32), sm("mr", 0, 32), 32)
-        tt(V("tbl", 1, 192, 4), sm("y16", 0, 48), CL, OP.add)
-        cp(ul("md", 0, 2), sm("mw", 15, 32, 16))
-        ts(ul("qlo", 0, 32), IND(V("tbl", 0, 96), ul("md", 0, 2)), MAGIC, OP.add, -MAGIC, OP.add)
-        act(sm("r", 0, 32), IND(V("tbl", 0, 96), ul("md", 0, 2)), AF.Identity, bias=MAGIC)
-        act(sm("rh", 0, 32), IND(V("tbl", 96, 192), ul("md", 0, 2)), AF.Identity, bias=MAGIC)
+        tt(V("tbl", 2, 192, 4), sm("y16", 0, 48), CL, OP.add)
+        ts(ul("md", 0, 2), sm("mw", 15, 32, 16), sm("f3", 0, 1), OP.add)
+        scan(V("aa", 0, C), V("isa", 0, C), V("zer", 0, C), float(ARR - 257), OP.add, OP.add)
+        ts(ul("qlo", 0, 32), IND(V("tbl", 0, 288), ul("md", 0, 2)), MAGIC, OP.add, -MAGIC, OP.add)
+        act(sm("r", 0, 32), IND(V("tbl", 0, 288), ul("md", 0, 2)), AF.Identity, bias=MAGIC)
+        act(sm("rh", 0, 32), IND(V("tbl", 96, 384), ul("md", 0, 2)), AF.Identity, bias=MAGIC)
         act(V("e1", 0, S), IND(V("aa", 0, 256), ul("qlo", 0, 24)))
-        tt(V("wm", 0, S), IND(V("vv", 0, 256), ul("qlo", 0, 24)), V("dm", 0, S), OP.mult)
+        tt(V("wb", 0, S), IND(V("vv", 0, 256), ul("qlo", 0, 24)), V("dm", 0, S), OP.mult)
         if not last:
-            const(V("vv", 0, C))
+            const(V("vv", 0, C), -256)
         tt(sm("valid"), sm("rh"), sm("r"), OP.is_gt)
-        segsum(V("wf", 0, S), V("wm", 0, S), S)
+        segsum(V("wb2", 0, S), V("wb", 0, S), S)
+        act(sm("cap"), sm("valid"), AF.Identity, bias=-256.0, scale=1024.0)
         if not last:
-            tt(sm("d1"), sm("r"), sm("k240m"), OP.subtract)
+            act(sm("gap"), sm("valid"), AF.Identity, bias=BIG, scale=-BIG)
         pick(V("e2", 0, S), V("e1", 0, S), S)
+        tt(sm("tw"), V("wb2", 15, S, 16), V("e2", 15, S, 16), OP.max)
         if not last:
-            tt(sm("d1"), sm("d1"), sm("valid"), OP.mult)
-        tt(sm("tw"), V("wf", 15, S, 16), V("e2", 15, S, 16), OP.max)
+            tt(sm("d1"), sm("r"), sm("gap"), OP.max)
+        tt(sm("tw"), sm("tw"), sm("cap"), OP.min)
         if not last:
-            tt(sm("d1"), sm("d1"), sm("k240"), OP.add)
-        tt(sm("tw"), sm("tw"), sm("valid"), OP.mult)
-        cp(ul("to", 0, 24), sm("tw"))
+            tt(sm("d1"), sm("d1"), sm("k240m"), OP.min)
+        ts(ul("to", 0, 24), sm("tw"), 256.0, OP.add)
         if not last:
-            cp(ul("d2", 0, 24), sm("d1"))
+            ts(ul("d2", 0, 24), sm("d1"), -MAGIC, OP.add)
 
     for c in range(2):
         a, z = (0, CW) if c == 0 else (CW, S)

@@ -5,10 +5,19 @@ ARR, OWN = 32, 128
 BIG = 2.0 ** 90
 MAGIC = 12582912.0
 UP = 0.4921875
+OFF = 200.0
 NA = 6
-NM = 6
+NM = 7
 ND = 15 - NM
 CW = 256
+WAKE, DMA, GATHER, SCATTER = 190, 2300, 1.56, 3.8
+PASSES = 3
+LOG = []
+HOOK = []
+LAYER = "s g0 q0 g1 f0 q1 a0 f1 a1 t0 t1"
+ENG = dict(g0="va", g1="va", f0="v", f1="v", t0="a", t1="a", kk="a")
+AFTER = "leavers arrive stays base signs list B less"
+NSC = 3
 X4, U8, U16, BF, F32 = "float8_e4m3fn_x4", "uint8", "uint16", "bfloat16", "float32"
 
 
@@ -22,37 +31,40 @@ SCRATCH = {
     "qx": _sb(240, X4), "sx": _sb(240, U8), "qu": _sb(128, X4), "su": _sb(128, U8),
     "qu2": _sb(128, X4), "su2": _sb(128, U8), "qv": _sb(128, X4), "sv": _sb(128, U8),
     "qw": _sb(512, X4), "sw": _sb(512, U8), "qe": _sb(512, X4), "se": _sb(512, U8),
-    "ones": _sb(512, BF), "et": _sb(2048, BF),
-    "tb": _sb(2048, BF), "fi": _sb(1536, BF), "f64": _sb(1536, BF), "ti": _sb(1536, BF), "bt": _sb(512, BF),
+    "ones": _sb(512, BF), "et": _sb(2048, BF), "tb0": _sb(2048, BF), "tb1": _sb(2048, BF),
+    "fi": _sb(1536, BF), "f64": _sb(1536, BF), "ti": _sb(1536, BF), "bt": _sb(512, BF),
     "qf": _sb(384, X4), "sf": _sb(384, U8), "qt": _sb(384, X4), "st": _sb(384, U8),
-    "qz": _sb(128, X4), "sz": _sb(128, U8),
-    "qb": _sb(384, X4), "sb": _sb(384, U8), "ql": _sb(320, X4), "sl": _sb(320, U8),
+    "qb": _sb(384, X4), "sb": _sb(384, U8), "ql": _sb(416, X4), "sl": _sb(416, U8),
     "yo": _sb(384, F32), "olr": _sb(384, F32),
     "iota": _sb(512, F32), "t16": _sb(384, BF), "dm": _sb(384, BF), "mx": _sb(384, BF), "rs": _sb(384, BF),
-    "rs97": _sb(97 * ND, BF), "step": _sb(240, BF), "idmap": _sb(512, F32), "xrow": _sb(224, BF),
-    "pint": _sb(8, "int32"), "zer": _sb(240, BF), "tb2": _sb(512, BF), "inv": _sb(288, BF),
-    "pp": _sb(512, F32), "kk": _sb(240, F32), "wm": _sb(240, F32), "wf": _sb(240, F32),
+    "nd": _sb(240, BF), "step": _sb(240, BF), "idmap": _sb(512, F32), "xrow": _sb(256, BF), "xr": _sb(256, BF),
+    "pint": _sb(8, "int32"), "zer": _sb(240, BF), "ta": _sb(512, BF), "tc": _sb(512, BF), "inv": _sb(288, BF),
+    "pp": _sb(512, F32), "kk": _sb(256, F32), "wm": _sb(240, F32), "wf": _sb(240, F32),
+    "ptr": _sb(256, F32), "pax": _sb(256, F32), "prow": _sb(256, F32),
     "cmp": _sb(240 * (15 - NA), BF), "so": _sb(120 * (15 - NA), BF), "sa": _sb(241 * NA, BF),
-    "eq": _sb(240, BF), "cs": _sb(240, BF), "ex": _sb(240, BF),
+    "eq": _sb(240, BF), "ex": _sb(240, BF),
     "lrow": _sb(256, BF), "idb": _sb(384, BF), "wb": _sb(384, BF), "wb2": _sb(384, BF),
     "arow": _sb(96, F32), "atr": _sb(96, F32), "ax": _sb(96, F32),
     "kt0": _sb(512, F32), "kt1": _sb(512, F32), "krow": _sb(240, F32), "kx": _sb(240, F32),
-    "strow": _sb(240, BF), "spb": _sb(256, BF), "spe": _sb(240, BF), "spx": _sb(528, BF),
-    "e1": _sb(384, BF), "e2": _sb(384, BF), "thx": _sb(32, BF), "jk": _sb(480, BF),
-    "mso": _sb(97 * ND, BF), "mcp": _sb(97 * ND, BF), "sf2": _sb(97 * NM, F32),
-    "vv": _sb(480, BF), "isa": _sb(240, BF), "aa": _sb(256, BF),
-    "qrow": _sb(256, F32), "cum": _sb(48, F32), "xx": _sb(144, F32), "tbl": _sb(384, F32),
+    "strow": _sb(240, BF), "spb": _sb(256, BF), "spe": _sb(240, BF), "sxx": _sb(80, F32),
+    "e1": _sb(384, BF), "e2": _sb(384, BF), "zz": _sb(400, BF),
+    "mso": _sb(120 * ND, BF), "mcp": _sb(240 * ND, BF), "sf2": _sb(241 * NM, F32),
+    "vv": _sb(480, BF), "isa": _sb(240, BF), "aa": _sb(240, BF), "sq": _sb(256, BF),
+    "qrow": _sb(240, BF), "suf": _sb(256, BF), "xx": _sb(176, F32), "tbl": _sb(384, F32),
     "srw": _sb(624, BF), "srx": _sb(240, BF),
     "sm": _sb(64 * 48, F32), "u16": _sb(32 * 16, U16),
 }
 for _t in range(R):
+    SCRATCH["sp%d" % _t] = _sb(16, F32)
+    SCRATCH["lp%d" % _t] = _sb(16, F32)
+for _t in range(R - 1):
     SCRATCH["sk%d" % _t] = _sb(6, F32)
     SCRATCH["lk%d" % _t] = _sb(6, F32)
 
 POOLS = {"v": 48, "a": 32, "p": 12, "g": 12}
 LOADS = ["x", "u", "v", "wc", "ws"]
 SEMAPHORES = ([e + str(i) for e in POOLS for i in range(POOLS[e])] + ["ld_" + n for n in LOADS]
-              + ["ak%d" % t for t in range(R)] + ["ab%d" % t for t in range(R)] + ["apad", "sent", "out_s", "out_a"])
+              + [n + str(t) for n in ("ap", "ak", "ab") for t in range(R)] + ["sent", "out_s", "out_a"])
 
 
 def V(name, a, b, step=1):
@@ -74,7 +86,8 @@ def rank_program(g, core, T, topo):
     OP, AF = AluOpType, ActivationFunctionType
     Q = {"v": g.vector, "a": g.scalar, "p": g.tensor, "g": g, "s": g.sync}
 
-    ops = []
+    prog = []
+    ops = {}
     known = {e: 0 for e in Q}
     count = {e: [] for e in POOLS}
     acc = {}
@@ -96,75 +109,152 @@ def rank_program(g, core, T, topo):
                 o += [v[1], v[2]] if v[0] == "*" else [v]
         return o
 
-    def wait(e, i):
-        Q[e].wait_ge(T.sem[ops[i][0]], ops[i][1])
-        waited[ops[i][0]] = max(waited.get(ops[i][0], 0), ops[i][1])
-        known[e] |= ops[i][2] | (1 << i)
-
-    def before(e, reads, writes, more=()):
+    def note(ways, reads, writes, kind="", lag=0, more=()):
         deps = set(more)
         use = [(v, v[0] == "ps") for v in flat(reads)] + [(v, True) for v in flat(writes)]
         for v, w in use:
             for (u, uw, i) in acc.get(v[0], []):
                 if (w or uw) and clash(u, v):
                     deps.add(i)
-        for i in sorted(deps, reverse=True):
-            if not known[e] >> i & 1:
-                wait(e, i)
-        return use
-
-    def note(use, sem, val, seen):
-        i = len(ops)
-        ops.append((sem, val, seen))
+        i = len(prog)
+        prog.append(({e: (c, int(n)) for e, (c, n) in ways.items()}, deps, kind, lag))
         for v, w in use:
             lst = acc.setdefault(v[0], [])
-            if w and v[3] == 1:
+            if w and abs(v[3]) == 1:
                 lst[:] = [r for r in lst if not (r[0][1] >= v[1] and r[0][2] <= v[2])]
             lst.append((v, w, i))
         return i
 
-    def run(e, reads, writes, call):
-        n, k = len(count[e]), POOLS[e]
-        use = before(e, reads, writes, [count[e][n - k]] if n >= k else [])
-        sem = e + str(n % k)
-        call().then_inc(T.sem[sem], 1)
-        count[e].append(note(use, sem, n // k + 1, known[e]))
+    def size(v):
+        return 16 * size(v[2]) if v[0] == "*" else len(range(v[1], v[2], abs(v[3])))
+
+    def cycles(e, out, ins, rate=None):
+        vs = [v for v in [out] + ins if isinstance(v, tuple)]
+        n = max(size(v) for v in vs)
+        if out[0] == "*":
+            return 60 + SCATTER * n
+        if any(v[0] == "*" for v in vs):
+            return 60 + GATHER * n
+        if rate is None:
+            rate = 0.5 if e == "v" and all(SCRATCH[v[0]][2] in (BF, U16) for v in vs if size(v) > 1) else 1.0
+        return max(64, rate * n)
+
+    def run(e, reads, writes, call, cost):
+        note({e: (call, cost)}, reads, writes)
+
+    def order():
+        n = len(prog)
+        if HOOK:
+            return HOOK[0](prog)
+        users = [[] for _ in range(n)]
+        for i in range(n):
+            for d in prog[i][1]:
+                users[d].append(i)
+
+        def lay(seq, back):
+            busy = {e: [] for e in list(Q) + ["-"]}
+            span = {}
+            for i in seq:
+                if back:
+                    at = prog[i][3] + max([span[u][1] + WAKE for u in users[i]], default=0)
+                else:
+                    at = max([span[d][1] + prog[d][3] + WAKE for d in prog[i][1]], default=0)
+                best = None
+                for e, (_, c) in prog[i][0].items():
+                    b, k = busy[e], len(busy[e])
+                    while k and b[k - 1][1] > at:
+                        k -= 1
+                    a = at
+                    while k < len(b) and b[k][0] < a + c:
+                        a = max(a, b[k][1])
+                        k += 1
+                    if best is None or (a + c, c) < best[0]:
+                        best = ((a + c, c), a, e, k)
+                (end, c), a, e, k = best
+                busy[e].insert(k, (a, end))
+                span[i] = (a, end, e)
+            return span
+
+        seq = list(range(n))
+        best = None
+        for _ in range(PASSES):
+            span = lay(seq, False)
+            end = max(span[i][1] + prog[i][3] for i in range(n))
+            LOG.append(end)
+            if best is None or end < best[0]:
+                best = (end, span)
+            back = lay(sorted(range(n), key=lambda i: (-span[i][1] - prog[i][3], -i)), True)
+            seq = sorted(range(n), key=lambda i: (-back[i][1], i))
+        span = best[1]
+        return [(i, span[i][2]) for i in sorted(range(n), key=lambda i: (span[i][0], i))]
+
+    def wait(e, i):
+        Q[e].wait_ge(T.sem[ops[i][0]], ops[i][1])
+        waited[ops[i][0]] = max(waited.get(ops[i][0], 0), ops[i][1])
+        known[e] |= ops[i][2] | (1 << i)
+
+    def issue():
+        place = {}
+        for i, e in order():
+            place[i] = len(place)
+            ways, deps, kind, lag = prog[i]
+            if e == "-":
+                ops[i] = (kind[0], kind[1], 0)
+                continue
+            if not kind:
+                n, k = len(count[e]), POOLS[e]
+                deps = set(deps) | set([count[e][n - k]] if n >= k else [])
+            for d in sorted(deps, key=place.get, reverse=True):
+                if not known[e] >> d & 1:
+                    wait(e, d)
+            if not kind:
+                ways[e][0]().then_inc(T.sem[e + str(n % k)], 1)
+                ops[i] = (e + str(n % k), n // k + 1, known[e])
+                count[e].append(i)
+            else:
+                ways[e][0]()
+                if kind[1]:
+                    ops[i] = (kind[0], kind[1], known[e])
 
     def ap(v):
         if not isinstance(v, tuple):
             return v
         if v[0] == "*":
             return ap(v[1]).indirect(ap(v[2]))
+        if v[3] == -1:
+            return T[v[0]][:, v[2] - 1:(v[1] - 1 if v[1] else None):-1]
         return T[v[0]][:, v[1]:v[2]] if v[3] == 1 else T[v[0]][:, v[1]:v[2]:v[3]]
 
     def cp(out, in_):
         r, w = ([out[2]], [out[1]]) if out[0] == "*" else ([], [out])
-        run("v", r + [in_], w, lambda: g.vector.tensor_copy(ap(out), ap(in_)))
+        run("v", r + [in_], w, lambda: g.vector.tensor_copy(ap(out), ap(in_)), cycles("v", out, [in_]))
 
     def tt(out, a, b, op):
-        run("v", [a, b], [out], lambda: g.vector.tensor_tensor(ap(out), ap(a), ap(b), op))
+        run("v", [a, b], [out], lambda: g.vector.tensor_tensor(ap(out), ap(a), ap(b), op),
+            cycles("v", out, [a, b], 1.0 if "ps" in (a[0], b[0]) else 2.0))
+
+    def ts_way(out, a, s1, op0, s2=None, op1=None):
+        more = (None, op0) if s2 is None else (ap(s2), op0, op1)
+        return lambda: g.vector.tensor_scalar(ap(out), ap(a), ap(s1), *more), cycles("v", out, [a])
 
     def ts(out, a, s1, op0, s2=None, op1=None):
-        if s2 is None:
-            run("v", [a, s1], [out], lambda: g.vector.tensor_scalar(ap(out), ap(a), ap(s1), None, op0))
-        else:
-            run("v", [a, s1, s2], [out], lambda: g.vector.tensor_scalar(ap(out), ap(a), ap(s1), ap(s2), op0, op1))
+        note({"v": ts_way(out, a, s1, op0, s2, op1)}, [a, s1, s2], [out])
 
     def scan(out, d0, d1, init, op0, op1):
         run("v", [d0, d1, init], [out],
-            lambda: g.vector.tensor_tensor_scan(ap(out), ap(d0), ap(d1), ap(init), op0, op1))
+            lambda: g.vector.tensor_tensor_scan(ap(out), ap(d0), ap(d1), ap(init), op0, op1), cycles("v", out, [d0, d1]))
 
     def fill(out, c):
-        run("v", [], [out], lambda: g.vector.memset(ap(out), c))
+        run("v", [], [out], lambda: g.vector.memset(ap(out), c), cycles("v", out, []))
 
     def tr(out, in_):
-        run("v", [in_], [out], lambda: g.vector.transpose(ap(out), ap(in_)))
+        run("v", [in_], [out], lambda: g.vector.transpose(ap(out), ap(in_)), cycles("v", out, [in_]))
 
     def quant(q, s, a, b, in_):
         run("v", [in_], [V(q, a, b), V(s, a, b)],
-            lambda: g.vector.quantize_mx(ap(V(q, a, b)), ap(V(s, a, b)), ap(in_)))
+            lambda: g.vector.quantize_mx(ap(V(q, a, b)), ap(V(s, a, b)), ap(in_)), 14 + (b - a))
 
-    def act(out, in_, func=AF.Copy, bias=None, scale=None, accum=None):
+    def act_way(out, in_, func=AF.Copy, bias=None, scale=None, accum=None):
         kw = {}
         if bias is not None:
             kw["bias"] = ap(bias)
@@ -172,56 +262,73 @@ def rank_program(g, core, T, topo):
             kw["scale"] = ap(scale)
         if accum is not None:
             kw["accum_out"] = ap(accum)
-        run("a", [in_, bias, scale], [out, accum], lambda: g.scalar.activation(ap(out), ap(in_), func, **kw))
+        return (lambda: g.scalar.activation(ap(out), ap(in_), func, **kw),
+                cycles("a", out, [in_]) + (24 if accum else 0))
+
+    def act(out, in_, func=AF.Copy, bias=None, scale=None, accum=None):
+        note({"a": act_way(out, in_, func, bias, scale, accum)}, [in_, bias, scale], [out, accum])
+
+    def lin(out, in_, scale=1.0, bias=None, on="av"):
+        ways = {}
+        for e in on:
+            if e == "a":
+                ways[e] = act_way(out, in_, AF.Copy if bias is None else AF.Identity, bias, scale)
+            else:
+                ways[e] = ts_way(out, in_, scale, OP.mult, bias, None if bias is None else OP.add)
+        note(ways, [in_, bias, scale], [out])
 
     def mm(bank, wq, ws, wa, xq, xs, a, b):
         o = V("ps", 512 * bank, 512 * bank + b - a)
         w, wsc, x, xsc = V(wq, wa, wa + 128), V(ws, wa, wa + 128), V(xq, a, b), V(xs, a, b)
         run("p", [w, wsc, x, xsc], [o],
-            lambda: g.tensor.matmul_mx(ap(o), ap(w), ap(wsc), ap(x), ap(xsc), True, True))
+            lambda: g.tensor.matmul_mx(ap(o), ap(w), ap(wsc), ap(x), ap(xsc), True, True), 1.2 * (b - a + 16))
 
     def iota(out, pattern, base=0, cm=0):
-        run("g", [], [out], lambda: g.iota(ap(out), pattern, base, cm, allow_small_or_imprecise_dtypes=True))
+        run("g", [], [out], lambda: g.iota(ap(out), pattern, base, cm, allow_small_or_imprecise_dtypes=True),
+            150 + 2 * size(out))
 
     def const(out, c=0):
         iota(out, [[0, len(range(out[1], out[2], out[3]))]], c)
 
-    def load(e, name, out, dst, src):
-        use = before(e, [], [out])
-        Q[e].dma_start(dst, src).then_inc(T.sem["ld_" + name], 16)
-        note(use, "ld_" + name, 16, known[e])
+    def load(e, name, out, dst, src, lag, more=()):
+        return note({e: (lambda: Q[e].dma_start(dst, src).then_inc(T.sem["ld_" + name], 16), 50)}, [], [out],
+                    ("ld_" + name, 16), lag, more)
 
     total = {"sent": 0, "out_s": 0, "out_a": 0}
 
-    def store(e, dst, src, reads):
-        before(e, reads, [])
-        Q[e].dma_start(dst, src).then_inc(T.sem["out_" + e], 16)
+    def store(e, dst, src, reads, lag=DMA):
+        note({e: (lambda: Q[e].dma_start(dst, src).then_inc(T.sem["out_" + e], 16), 50)}, reads, [], ("out", 0), lag)
         total["out_" + e] += 16
 
+    sends = {}
+
     def send(dst, src, reads, sem):
-        before("g", reads, [])
-        g.remote_dma(dst, src, T.sem[sem], T.sem.sent, pid, rid, mask)
+        i = note({"g": (lambda: g.remote_dma(dst, src, T.sem[sem], T.sem.sent, pid, rid, mask), 330)}, reads, [],
+                 ("sent", 0), DMA if sends else 2 * DMA)
+        sends.setdefault(sem, []).append(i)
         total["sent"] += neng
 
-    def landed(writes, sem, n):
-        note([(v, True) for v in writes], sem, n * neng, 0)
+    def landed(writes, sem):
+        note({"-": (None, 0)}, [], writes, (sem, len(sends[sem]) * neng), -WAKE, sends[sem])
 
     def PS(bank, a, b):
         return V("ps", 512 * bank + a, 512 * bank + b)
 
-    def TB(b, a, e):
-        return V("tb", 512 * b + a, 512 * b + e)
+    def TB(t, b, a, e):
+        return V("tb%d" % (t % 2), 512 * b + a, 512 * b + e)
 
     slots = {}
 
     def sm(name, a=0, b=24, step=1):
         o = 64 * slots.setdefault(name, len(slots))
+        assert len(slots) <= 48
         return V("sm", o + a, o + b, step)
 
     lists = {}
 
     def ul(name, a, b):
         o = 32 * lists.setdefault(name, len(lists))
+        assert len(lists) <= 16
         return V("u16", o + a, o + b)
 
     def pick(out, row, n):
@@ -230,19 +337,19 @@ def rank_program(g, core, T, topo):
     def segsum(out, row, n):
         scan(out, V("rs", 0, n), row, 0.0, OP.mult, OP.add)
 
-    def turned(out, row, n, more):
-        tr(V("tb2", 0, n), V(row, 16, 16 + n))
-        tr(V("tb2", 256, 256 + min(n + 32, 256)), V(row, 0, min(n + 32, 256)))
-        ts(out, IND(V("tb2", 0, 512), ul("tw", 0, 1)), more, OP.add)
+    def turned(out, row, n, more, via):
+        tr(V(via, 0, n), V(row, 16, 16 + n))
+        tr(V(via, 256, 256 + min(n + 32, 256)), V(row, 0, min(n + 32, 256)))
+        ts(out, IND(V(via, 0, 512), ul("tw", 0, 1)), more, OP.add)
 
-    load("a", "u", V("us", 0, 512), T.us[:], T.u[:])
-    load("s", "x", V("xs", 0, 960), T.xs[:], T.x[:])
-    load("s", "wc", V("qw", 0, 512), T.qw[:].bitcast(dt.uint8), T.wc[:])
-    load("s", "ws", V("sw", 0, 512), T.sw[:], T.ws[:])
-    load("s", "v", V("vs", 0, 512), T.vs[:], T.v[:])
+    load("a", "u", V("us", 0, 512), T.us[:], T.u[:], 2700)
+    x_in = load("s", "x", V("xs", 0, 960), T.xs[:], T.x[:], 3500)
+    load("s", "wc", V("qw", 0, 512), T.qw[:].bitcast(dt.uint8), T.wc[:], 3500, [x_in])
+    load("s", "ws", V("sw", 0, 512), T.sw[:], T.ws[:], 3500, [x_in])
+    load("s", "v", V("vs", 0, 512), T.vs[:], T.v[:], 4000, [x_in])
 
     scol = sm("s", 0, 1)
-    run("g", [], [V("pint", 0, 1)], lambda: g.iota(T.pint[:, 0:1], [[0, 1]], 0, 1))
+    run("g", [], [V("pint", 0, 1)], lambda: g.iota(T.pint[:, 0:1], [[0, 1]], 0, 1), 150)
     iota(sm("c", 0, 32), [[1, 32]])
     iota(sm("k2", 0, 48), [[1, 2], [16, 24]])
     fill(V("rs", 0, 384), 1.0)
@@ -261,71 +368,74 @@ def rank_program(g, core, T, topo):
     ts(V("pint", 2, 3), V("pint", 2, 3), 1, OP.bitwise_and)
     ts(sm("beta", 0, NA), sm("c", 0, NA), 16.0, OP.mult, -1.0, OP.add)
     ts(V("dm", 0, 384), V("t16", 0, 384), scol, OP.is_equal)
+    ts(V("nd", 0, C), V("t16", 0, C), scol, OP.not_equal)
     ts(V("mx", 0, 384), V("t16", 0, 384), scol, OP.is_le, BIG, OP.mult)
     ts(sm("s", 2, 3), V("pint", 2, 3), 17.0, OP.mult, scol, OP.add)
-    quant("qz", "sz", 0, 128, V("bt", 0, 512))
+    quant("ql", "sl", 0, 128, V("bt", 0, 512))
     ts(ul("tw", 0, 1), sm("s", 2, 3), 16.0, OP.mult, 511.0, OP.min)
 
-    def more_vector():
-        ts(sm("yf", 0, 48), sm("k2", 0, 48), scol, OP.add, float(C) / S, OP.mult)
-        ts(sm("k240"), sm("k2"), scol, OP.add, float(C), OP.add)
-        ts(sm("yf", 0, 48), sm("yf", 0, 48), UP, OP.add, MAGIC, OP.add)
-        ts(sm("k240m"), sm("k240"), MAGIC, OP.add)
-        ts(ul("qlo", 0, 24), sm("yf"), -MAGIC, OP.add)
-
-    def more_gpsimd():
-        const(V("pp", 0, OWN))
+    def constants():
         const(V("inv", 0, 16))
         const(V("inv", 16 + C, 288))
         iota(V("iota", 0, 512), [[1, 512]])
-        for b in range(4):
-            const(TB(b, 0, OWN))
-        send(T.ql[:, 0:32].bitcast(dt.uint8), T.qz[:, 0:32].bitcast(dt.uint8), [V("qz", 0, 128)], "apad")
-        send(T.sl[:, 0:32], T.sz[:, 0:32], [V("sz", 0, 128)], "apad")
-        landed([V("ql", 0, 32), V("sl", 0, 32)], "apad", 2)
-        const(V("ones", 0, 512), 1)
-        for b in range(4):
-            o = V("et", 512 * b, 512 * b + 512)
-            run("g", [V("ones", 0, 512)], [o],
-                lambda: g.affine_select(ap(o), T.ones[:], [[-1, 512]], OP.is_equal, 0.0, b, 4))
+        const(V("tb0", 0, 2048, 512))
+        const(V("tb1", 0, 2048, 512))
+        const(V("xrow", 0, 256), 33)
+        for o in (16, 40):
+            iota(V("xrow", o + 4, o + 24), [[4, 5], [0, 4]], 4)
+            iota(V("xrow", o + 48, o + 72), [[4, 6], [0, 4]], 4)
+            const(V("xrow", o + 68, o + 72), 32)
+            iota(V("xrow", o + 97, o + 120), [[1, 23]], 1)
+        iota(V("xrow", 160, 184), [[1, 24]], 1)
+        const(V("xrow", 183, 184), 32)
+        iota(V("xrow", 208, 240), [[4, 8], [0, 4]], 3)
+        iota(sm("r", 32, 34), [[1, 2]], int(MAGIC) + C)
+        const(V("xr", 0, 256))
+        const(V("tc", 0, 512))
         iota(V("idb", 0, S), [[1, S]], OWN - 256)
         const(V("lrow", 0, 16))
         const(V("step", 0, L))
         const(V("step", L, C), 1)
-        iota(sm("m4", 0, 48), [[1, 2], [0, 6], [16, 4]])
         const(V("zer", 0, C))
-        const(V("spb", 0, 256))
-        const(V("spx", S, 528), C - L)
-        const(V("xrow", 0, 16))
-        iota(V("xrow", 16, 64), [[0, 2], [4, 6], [0, 4]])
-        iota(V("xrow", 64, 112), [[0, 2], [4, 6], [0, 4]], 4)
-        iota(V("xrow", 112, 160), [[0, 2], [1, 24]])
-        const(V("xrow", 160, 176))
-        iota(V("xrow", 176, 224), [[4, 12], [0, 4]], 3)
+        const(V("spb", 0, 256), -int(OFF))
+        const(V("kk", C, 256))
+        const(V("kt0", 0, 1))
+        const(V("kt1", 0, 1))
+        iota(sm("m4", 0, 48), [[1, 2], [0, 6], [16, 4]])
         iota(sm("n4"), [[4, 24]])
         const(sm("hz2", 24, 32), 95)
         const(sm("any", 24, 32))
         const(sm("rs4"), 1)
         const(sm("rs4", 0, 24, 4))
-        const(V("rs97", 0, 97 * ND), 1)
-        const(V("rs97", 0, 97 * ND, 97))
-        const(V("kt0", 0, ARR))
-        const(V("kt1", 0, ARR))
-        const(V("aa", C, 256), OWN - 257)
-        const(V("cum", 0, 48))
-        const(V("qrow", C, 256), C)
-
-    def more_scalar():
-        act(V("vv", 0, C), V("rs", 0, C), AF.Identity, bias=-256.0, scale=0.0)
-        act(V("vv", C, 480), V("rs", 0, C), AF.Identity, bias=-256.0, scale=0.0)
+        const(V("sq", C, 256))
+        const(V("suf", C, C + 1), C)
+        const(V("suf", C + 1, 256))
+        const(V("zz", S, 400), C)
+        const(V("ones", 0, 512), 1)
         for b in range(4):
-            act(V("tbl", 192 + b, 384, 4), sm("yf", 0, 48), AF.Identity, bias=-MAGIC)
+            o = V("et", 512 * b, 512 * b + 512)
+            run("g", [V("ones", 0, 512)], [o],
+                lambda o=o, b=b: g.affine_select(ap(o), T.ones[:], [[-1, 512]], OP.is_equal, 0.0, b, 4), 1200)
+        ts(sm("yf", 0, 48), sm("k2", 0, 48), scol, OP.add, float(C) / S, OP.mult)
+        ts(sm("k240"), sm("k2"), scol, OP.add, float(C), OP.add)
+        ts(sm("yf", 0, 48), sm("yf", 0, 48), UP, OP.add, MAGIC, OP.add)
+        lin(sm("k240m"), sm("k240"), bias=MAGIC)
+        ts(ul("qlo", 0, 24), sm("yf"), -MAGIC, OP.add)
+        for a in (0, C):
+            lin(V("vv", a, a + C), V("rs", 0, C), 0.0, -256.0)
+        for b in range(4):
+            lin(V("tbl", 192 + b, 384, 4), sm("yf", 0, 48), bias=-MAGIC)
+        lin(sm("r", 0, 24), sm("yf", 0, 24))
+        lin(sm("k40", 0, 15), sm("k240", 0, 15), bias=-2 * OFF)
+        lin(sm("o16", 0, 2), sm("c", 0, 2), bias=scol)
+        lin(sm("o16", 0, 2), sm("o16", 0, 2), 1.0 / 16)
+        lin(sm("o64", 0, 48), sm("m4", 0, 48), bias=scol)
+        lin(sm("o64", 0, 48), sm("o64", 0, 48), 1.0 / 64)
+        turned(ul("xc", 0, 16), "xrow", 224, 0.0, "tc")
 
-    def last_gpsimd():
-        const(V("srw", 0, 624))
-        const(V("idmap", 0, ARR), -1)
-        iota(V("idmap", ARR, OWN), [[1, L]], S)
-        iota(V("idmap", OWN, 512), [[1, S]])
+    def leaf_lists():
+        lin(V("xr", 16, 192), IND(sm("r", 0, 64), ul("xc", 0, 11)), bias=-MAGIC)
+        turned(ul("xl", 0, 16), "xr", 192, 0.0, "tc")
 
     def ranking(K):
         def k(a, b):
@@ -335,73 +445,49 @@ def rank_program(g, core, T, topo):
             return V("wf", 16 * j + 15, 16 * j + 16)
 
         W = C + 1
-        for j in range(NA + 1):
-            if j < NA:
-                act(V("sa", W * j, W * j + C), k(0, C), AF.Sign, bias=w(j), scale=-1.0)
-            if j > 1:
-                o = W * (j - 1)
-                act(V("sa", o, o + 16 * j - 16), V("sa", o, o + 16 * j - 16), AF.Relu, scale=-1.0,
-                    accum=sm("ra", j - 1, j))
-
-        def total_of(j):
-            o = C * (j - NA)
-            scan(V("so", o // 2, o // 2 + 120), V("cmp", o, o + 120), V("cmp", o + 120, o + C),
-                 sm("eb", j, j + 1), OP.add, OP.add)
-
-        def rest():
-            tt(V("sa", C, W * NA, W), sm("eb", 0, NA), sm("ra", 0, NA), OP.subtract)
-            for j in range(NA):
-                o = W * j
-                act(V("sa", o + 16 * j, o + W), V("sa", o + 16 * j, o + W), AF.Relu, accum=sm("rb", j, j + 1))
-
-        extra = [lambda: tt(V("eq", 0, C), IND(V("wf", 0, C), ul("lw", 0, 15)), k(0, C), OP.is_equal),
-                 lambda: segsum(V("cs", 0, C), V("eq", 0, C), C),
-                 lambda: pick(V("ex", 0, C), V("cs", 0, C), C),
-                 lambda: tt(sm("eb", 0, 15), V("ex", 15, C, 16), sm("beta", 0, 15), OP.add),
-                 rest]
-        todo = list(range(NA, 15))
+        tt(V("eq", 0, C), IND(V("wf", 0, C), ul("lw", 0, 15)), k(0, C), OP.is_equal)
+        scan(V("ex", 0, C, -1), V("nd", 0, C, -1), V("eq", 0, C, -1), 0.0, OP.mult, OP.add)
+        tt(sm("eb", 0, 15), V("ex", 0, C, 16), sm("beta", 0, 15), OP.add)
+        for j in range(NA - 1, -1, -1):
+            act(V("sa", W * j, W * j + C), k(0, C), AF.Sign, bias=w(j), scale=-1.0)
+        for j in range(NA - 1, 0, -1):
+            act(V("sa", W * j, W * j + 16 * j), V("sa", W * j, W * j + 16 * j), AF.Relu, scale=-1.0,
+                accum=sm("ra", j, j + 1))
+        tt(V("sa", C, W * NA, W), sm("eb", 0, NA), sm("ra", 0, NA), OP.subtract)
+        for j in range(NA):
+            o = W * j
+            act(V("sa", o + 16 * j, o + W), V("sa", o + 16 * j, o + W), AF.Relu, accum=sm("rb", j, j + 1))
         for j in range(NA, 15):
             o = C * (j - NA)
             ts(V("cmp", o, o + 16 * j), k(0, 16 * j), w(j), OP.is_le)
             ts(V("cmp", o + 16 * j, o + C), k(16 * j, C), w(j), OP.is_lt)
-            if j - NA < len(extra):
-                extra[j - NA]()
-            else:
-                total_of(todo.pop(0))
-                total_of(todo.pop(0))
-        for j in todo:
-            total_of(j)
-        cp(ul("rk", 0, NA), sm("rb", 0, NA))
+        for j in range(NA, 15):
+            o = C * (j - NA)
+            scan(V("so", o // 2, o // 2 + 120), V("cmp", o, o + 120), V("cmp", o + 120, o + C),
+                 sm("eb", j, j + 1), OP.add, OP.add)
         cp(ul("rk", NA, 15), V("so", 119, 120 * (15 - NA), 120))
+        cp(ul("rk", 0, NA), sm("rb", 0, NA))
         return [(0, NA, sm("rb", 0, NA)), (NA, 15, V("so", 119, 120 * (15 - NA), 120))]
 
-    def parts(e, out, b, top, lst, a, z):
-        o = V(out, 4 * a + b, 4 * z, 4)
-        if e == "v":
-            ts(o, IND(TB(b, 0, top), lst), 0.015625, OP.mult)
-        else:
-            act(o, IND(TB(b, 0, top), lst), scale=0.015625)
+    def parts(e, t, out, b, top, lst, a, z):
+        lin(V(out, 4 * a + b, 4 * z, 4), IND(TB(t, b, 0, top), lst), 0.015625, on=e)
 
     quant("qu", "su", 0, 128, V("us", 0, 512))
     run("v", [V("qu", 0, 128), ul("c16", 0, 8)], [V("qu2", 0, 128)], lambda: g.vector.tensor_copy(
-        T.qu2[:, 0:128].bitcast(dt.uint32), T.qu[:, 0:128].bitcast(dt.uint32).indirect(ap(ul("c16", 0, 8)))))
+        T.qu2[:, 0:128].bitcast(dt.uint32), T.qu[:, 0:128].bitcast(dt.uint32).indirect(ap(ul("c16", 0, 8)))), 260)
     act(V("su2", 0, 128), IND(V("su", 0, 128), ul("c16", 0, 8)))
     quant("qx", "sx", 0, C, V("xs", 0, 960))
     mm(0, "qu2", "su2", 0, "qx", "sx", 0, C)
     mm(1, "qu2", "su2", 0, "qx", "sx", 0, C)
-    more_gpsimd()
-    more_vector()
-    for b in range(2):
-        act(TB(b, OWN, OWN + C), V("xs", b, 960, 4), scale=64.0)
     tt(V("wm", 0, C), PS(0, 0, C), V("dm", 0, C), OP.mult)
     act(V("pp", OWN, OWN + C), PS(1, 0, C))
     segsum(V("wf", 0, C), V("wm", 0, C), C)
     ranking(V("pp", OWN, OWN + C))
-    for b in range(2, 4):
-        act(TB(b, OWN, OWN + C), V("xs", b, 960, 4), scale=64.0)
-    more_scalar()
+    constants()
     cp(IND(V("inv", 16, 16 + C), ul("rk", 0, 15)), V("iota", 0, C))
-    turned(ul("to", 0, 16), "inv", 256, float(OWN))
+    turned(ul("to", 0, 16), "inv", 256, float(OWN), "ta")
+    for b in range(4):
+        lin(TB(0, b, OWN, OWN + C), V("xs", b, 960, 4), 64.0)
 
     for t in range(R):
         first, last = t == 0, t == R - 1
@@ -410,8 +496,9 @@ def rank_program(g, core, T, topo):
         kt, ktn = "kt%d" % (t % 2), "kt%d" % ((t + 1) % 2)
         ch = [(0, cw), (cw, 256 if first else S)]
 
-        def lst(c):
-            return ul("to", ch[c][0] // 16, ch[c][1] // 16)
+        def gather(c):
+            for b in range(4):
+                parts(ENG["g%d" % c], t, "fi", b, top, ul("to", ch[c][0] // 16, ch[c][1] // 16), *ch[c])
 
         def qf(c):
             a, z = ch[c]
@@ -421,13 +508,13 @@ def rank_program(g, core, T, topo):
 
         def f64(c):
             a, z = ch[c]
-            ts(V("f64", 4 * a, 4 * z), V("fi", 4 * a, 4 * z), 64.0, OP.mult)
+            lin(V("f64", 4 * a, 4 * z), V("fi", 4 * a, 4 * z), 64.0, on=ENG["f%d" % c])
 
         def add(c):
             a, z = ch[c]
             for b in range(4):
-                tt(TB(b, OWN + a, OWN + z), PS(4 * c + b, 0, z - a), V("f64", 4 * a + b, 4 * z, 4), OP.add)
-                act(V("ti", 4 * a + b, 4 * z, 4), TB(b, OWN + a, OWN + z), scale=0.015625)
+                tt(TB(t + 1, b, OWN + a, OWN + z), PS(4 * c + b, 0, z - a), V("f64", 4 * a + b, 4 * z, 4), OP.add)
+                lin(V("ti", 4 * a + b, 4 * z, 4), TB(t + 1, b, OWN + a, OWN + z), 0.015625, on=ENG["t%d" % c])
 
         def qt(c):
             a, z = ch[c]
@@ -435,201 +522,203 @@ def rank_program(g, core, T, topo):
             mm(4 * c, "qu2", "su2", 0, "qt", "st", a, z)
             if first:
                 mm(4 * c + 1, "qu2", "su2", 0, "qt", "st", a, z)
+                n = min(z, C) - a
+                tt(V("wm", a, a + n), PS(4 * c, 0, n), V("dm", 0, n), OP.mult)
+            lin(V("pp", OWN + a, OWN + z), PS(4 * c + first, 0, z - a))
+
+        def held(c):
+            if not first:
+                for a in range(0, 24, 24 // NSC):
+                    z = a + 24 // NSC
+                    cp(IND(V("srw", 0, 624), ul("d2", a, z)), V("idb", 16 * a, 16 * z))
+                pick(V("srx", 0, C), V("srw", 0, C), C)
+                ts(ul("ids", 0, 15), V("srx", 15, C, 16), 256.0, OP.add)
+
+        def keys():
+            if first:
+                lin(V(kt, OWN, OWN + C), IND(V("pp", 0, OWN + C), ul("to", 0, 15)))
+                pick(V("kx", 0, C), V(kt, OWN, OWN + C), C)
+            else:
+                lk = "lk%d" % (t - 1)
+                landed([V(lk, 0, 6)], "ak%d" % (t - 1))
+                lin(V("ax", 0, L), IND(V(lk, 0, 6), ul("c", 0, 6)))
+                tr(V(ktn, ARR, OWN), V("ax", 0, L))
+                lin(V(kt, OWN, 512), IND(V(ktn, 0, top), ul("to", 0, 24)))
+                lin(V("krow", 0, C), IND(V(kt, 0, 512), ul("ids", 0, 15)))
+                pick(V("kx", 0, C), V("krow", 0, C), C)
 
         if first:
-            for c in range(2):
-                for b in range(4):
-                    parts("va"[b % 2], "fi", b, top, lst(c), *ch[c])
-                qf(c)
-            act(V(kt, OWN, OWN + C), IND(V("pp", 0, OWN + C), ul("to", 0, 15)))
-            f64(0)
-            f64(1)
-            add(0)
-            add(1)
-            qt(0)
-            qt(1)
-            quant("qe", "se", 0, 256, V("et", 0, 1024))
-            for c in range(2):
-                a, z = ch[c][0], min(ch[c][1], C)
-                tt(V("wm", a, z), PS(4 * c, 0, z - a), V("dm", 0, z - a), OP.mult)
-                act(V("pp", OWN + a, OWN + z), PS(4 * c + 1, 0, z - a))
+            keys()
+        steps = {"g": gather, "q": qf, "f": f64, "a": add, "t": qt, "s": held}
+        for s in LAYER.split():
+            steps[s[0]](int(s[1:] or 0))
+        if first:
             K, ids, ptop = V("pp", OWN, OWN + C), V("idb", 0, C), OWN + C
         else:
-            for c in range(2):
-                for b in range(4):
-                    if (c, b) != (1, 3):
-                        parts("a", "fi", b, top, lst(c), *ch[c])
-            cp(IND(V("srw", 0, 624), ul("d2", 0, 24)), V("idb", 0, S))
-            parts("v", "fi", 3, top, lst(1), *ch[1])
-            qf(0)
-            f64(0)
-            qf(1)
-            add(0)
-            f64(1)
-            pick(V("srx", 0, C), V("srw", 0, C), C)
-            qt(0)
-            add(1)
-            qt(1)
-            ts(ul("ids", 0, 15), V("srx", 15, C, 16), 256.0, OP.add)
-            act(V("pp", OWN, OWN + cw), PS(0, 0, cw))
-            act(V("pp", OWN + cw, 512), PS(4, 0, S - cw))
             tt(V("wm", 0, C), IND(V("pp", 0, 512), ul("ids", 0, 15)), V("dm", 0, C), OP.mult)
-            act(V("kk", 0, C), IND(V("pp", 0, 512), ul("ids", 0, 15)))
+            lin(V("kk", 0, C), IND(V("pp", 0, 512), ul("ids", 0, 15)), on=ENG["kk"])
             K, ids, ptop = V("kk", 0, C), V("srw", 0, C), 512
         segsum(V("wf", 0, C), V("wm", 0, C), C)
+
+        sp, lp = "sp%d" % t, "lp%d" % t
+        tr(V("ptr", 0, 256), V(K[0], K[1], K[1] + 256))
+        lin(V(sp, 0, 16), V("ptr", 0, 256, 16))
+        send(T[lp][:], T[sp][:], [V(sp, 0, 16)], "ap%d" % t)
         rk = ranking(K)
         if not first:
-            act(V(kt, OWN, 512), IND(V(ktn, 0, top), ul("to", 0, 24)))
-            act(V("krow", 0, C), IND(V(kt, 0, 512), ul("ids", 0, 15)))
+            keys()
+        leaf_lists()
 
-        cp(IND(V("lrow", 16, 16 + C), ul("rk", 0, 15)), ids)
-        act(V("strow", 0, C), IND(V("step", 0, C), ul("rk", 0, 15)))
-        for a, z, v in rk:
-            act(sm("gp", a, z), v, AF.Identity, bias=-(2 * L - 1) * BIG, scale=2 * BIG)
-        act(sm("gn", 0, 15), sm("gp", 0, 15), scale=-1.0)
-        if first:
-            act(sm("o16", 0, 2), sm("c", 0, 2), AF.Identity, bias=scol)
-            act(sm("o64", 0, 48), sm("m4", 0, 48), AF.Identity, bias=scol)
-            act(sm("o16", 0, 2), sm("o16", 0, 2), scale=1.0 / 16)
-            act(sm("o64", 0, 48), sm("o64", 0, 48), scale=1.0 / 64)
-        turned(ul("l", 0, 16), "lrow", L, 256.0)
-        cp(V("arow", 0, L), IND(V("pp", 0, ptop), ul("l", 0, 6)))
-        tr(V("atr", 0, L), V("arow", 0, L))
-        sk, lk = "sk%d" % t, "lk%d" % t
-        cp(V(sk, 0, 6), V("atr", 0, L, 16))
-        send(T[lk][:], T[sk][:], [V(sk, 0, 6)], "ak%d" % t)
-        for b in range(4):
-            parts("a", "bt", b, OWN + ch[1][1], ul("l", 0, 6), 32, 128)
-        scan(V("spb", 1, C + 1), V("strow", 0, C), V("zer", 0, C), 0.0, OP.add, OP.add)
-        act(V("spx", 0, S), IND(V("spb", 0, 256), ul("qlo", 0, 24)))
-        pick(V("kx", 0, C), V(kt, OWN, OWN + C) if first else V("krow", 0, C), C)
+        W = C + 1
         o = 128 * t
-        quant("qb", "sb", o, o + 128, V("bt", 0, 512))
-        la, lz = L * t + 32, L * t + 128
-        send(T.ql[:, la:lz].bitcast(dt.uint8), T.qb[:, o + 32:o + 128].bitcast(dt.uint8), [V("qb", o, o + 128)], "ab%d" % t)
-        send(T.sl[:, la:lz], T.sb[:, o + 32:o + 128], [V("sb", o, o + 128)], "ab%d" % t)
-        if first:
-            last_gpsimd()
+        la, lz = 128 + L * t, 128 + L * t + L
 
-        pick(V("spe", 0, C), V("spb", 0, C), C)
-        tt(sm("km", 0, 15), V("kx", 15, C, 16), sm("gp", 0, 15), OP.min)
-        tt(sm("gh", 0, 15), sm("k240", 0, 15), V("spe", 15, C, 16), OP.subtract)
-        if first:
-            quant("qe", "se", 256, 512, V("et", 1024, 2048))
-        if last:
-            quant("qv", "sv", 0, 128, V("vs", 0, 512))
-        tt(sm("base", 0, 15), V("spe", 15, C, 16), sm("gn", 0, 15), OP.max)
-        pick(V("thx", 0, 32), V("spx", 16, 528, 16), 32)
-        act(sm("thr", 0, 2), V("thx", 15, 32, 16), AF.Identity, bias=0.5)
-        for j in range(2):
-            act(V("jk", C * j, C * j + C), V("spb", 1, C + 1), AF.Sign, bias=sm("thr", j, j + 1), scale=-1.0,
-                accum=sm("fs", j, j + 1))
-        pick(V("e1", 0, S), V("spx", 0, S), S)
-        tt(sm("base", 0, 15), sm("base", 0, 15), sm("gh", 0, 15), OP.min)
-        pick(V("e2", 0, S), V("spx", 1, S + 1), S)
-        lo, hi = V("spx", 0, S, 16), V("spx", 16, S + 1, 16)
-        tt(sm("sc"), hi, lo, OP.subtract)
-        tt(sm("rst", 0, 24), V("e1", 15, S, 16), lo, OP.subtract)
-        tt(sm("rst", 24, 48), V("e2", 15, S, 16), lo, OP.subtract)
-        ts(sm("sc13"), sm("sc"), float(Q1), OP.max)
-        act(V("mcp", L, 97 * ND, 97), sm("base", NM, 15), AF.Identity, bias=-128.0)
-        act(V("sf2", L, 97 * NM, 97), sm("base", 0, NM))
-        if first:
-            turned(ul("xl", 0, 16), "xrow", 192, 0.0)
-        ts(ul("fs", 0, 2), sm("fs", 0, 2), 0.5, OP.mult, C / 2.0, OP.add)
+        def key(j):
+            return V("kx", 16 * j + 15, 16 * j + 16)
 
-        landed([V(lk, 0, 6)], "ak%d" % t, 1)
-        cp(V("ax", 0, L), IND(V(lk, 0, 6), ul("c", 0, 6)))
-        A = V(kt, ARR, OWN)
-        tr(A, V("ax", 0, L))
-        for j in range(NM + 2):
-            if j < NM:
-                act(V("sf2", 97 * j, 97 * j + L), A, AF.Sign, bias=sm("km", j, j + 1), scale=-1.0)
-            if j > 1:
-                o = V("sf2", 97 * j - 194, 97 * j - 97)
-                act(o, o, AF.Relu, accum=sm("ta", j - 2, j - 1))
-        h = ND - 3
-        for j in range(ND):
-            ts(V("mcp", 97 * j, 97 * j + L), A, sm("km", NM + j, NM + j + 1), OP.is_lt)
-            if j == h + 1:
-                scan(V("mso", 0, 97 * h), V("rs97", 0, 97 * h), V("mcp", 0, 97 * h), 0.0, OP.mult, OP.add)
-        scan(V("mso", 97 * h, 97 * ND), V("rs97", 97 * h, 97 * ND), V("mcp", 97 * h, 97 * ND), 0.0, OP.mult, OP.add)
-        cp(ul("dest", 0, NM), sm("ta", 0, NM))
-        ts(ul("dest", NM, 15), V("mso", L, 97 * ND, 97), 128.0, OP.add)
-        cp(IND(V("vv", 0, 480), ul("dest", 0, 15)), ids)
-        act(V("qrow", 0, C), IND(V("iota", 0, 512), ul("dest", 0, 15)))
-        act(V("cum", 1, 33), IND(V("qrow", 0, 256), ul("fs", 0, 2)))
-        act(V("xx", 0, 144), IND(V("cum", 0, 48), ul("xl", 0, 9)), AF.Identity, bias=UP)
-        act(V("isa", 0, C), V("vv", 0, C), AF.Relu, bias=-255.0, scale=-1.0)
-        landed([V("ql", la, lz), V("sl", la, lz)], "ab%d" % t, 2)
-        for b in range(4):
-            mm(b, "qe", "se", 128 * b, "ql", "sl", L * t, L * t + 128)
+        def leavers():
+            cp(IND(V("lrow", 16, 16 + C), ul("rk", 0, 15)), ids)
+
+        def arrive():
+            landed([V(lp, 0, 16)], "ap%d" % t)
+            lin(V("pax", 0, 256), IND(V(lp, 0, 16), ul("c", 0, 16)))
+            tr(V("prow", 0, 256), V("pax", 0, 256))
+
+        def stays():
+            lin(V("strow", 0, C), IND(V("step", 0, C), ul("rk", 0, 15)))
+            scan(V("spb", 1, C + 1), V("strow", 0, C), V("zer", 0, C), -OFF, OP.add, OP.add)
+            pick(V("spe", 0, C), V("spb", 0, C), C)
+
+        def base():
+            for a, z, v in rk:
+                lin(sm("gn", a, z), v, -2 * BIG, (2 * L - 1) * BIG)
+            tt(sm("gh", 0, 15), sm("k40", 0, 15), V("spe", 15, C, 16), OP.subtract)
+            tt(sm("base", 0, 15), V("spe", 15, C, 16), sm("gn", 0, 15), OP.max)
+            tt(sm("base", 0, 15), sm("base", 0, 15), sm("gh", 0, 15), OP.min)
+            lin(V("sf2", C, W * NM, W), sm("base", 0, NM), bias=OFF)
+            lin(sm("cap96", 0, NM), sm("base", 0, NM), bias=OFF + L)
+            lin(sm("cap96", NM, 15), sm("base", NM, 15), bias=float(L))
+
+        def signs():
+            for j in range(NM):
+                act(V("sf2", W * j, W * j + C), V("prow", 0, C), AF.Sign, bias=key(j), scale=-1.0)
+            for j in range(NM):
+                act(V("sf2", W * j, W * j + W), V("sf2", W * j, W * j + W), AF.Relu, accum=sm("ta", j, j + 1))
+
+        def less():
+            for j in range(ND):
+                ts(V("mcp", C * j, C * j + C), V("prow", 0, C), key(NM + j), OP.is_lt)
+            for j in range(ND):
+                scan(V("mso", 120 * j, 120 * j + 120), V("mcp", C * j, C * j + 120), V("mcp", C * j + 120, C * j + C),
+                     sm("base", NM + j, NM + j + 1), OP.add, OP.add)
+
+        def send_b():
+            for b in range(4):
+                parts("av", t + 1, "bt", b, OWN + ch[1][1], ul("l", 0, 6), 32, 128)
+            quant("qb", "sb", o, o + 128, V("bt", 0, 512))
+            send(T.ql[:, la:lz].bitcast(dt.uint8), T.qb[:, o + 32:o + 128].bitcast(dt.uint8), [V("qb", o, o + 128)],
+                 "ab%d" % t)
+            send(T.sl[:, la:lz], T.sb[:, o + 32:o + 128], [V("sb", o, o + 128)], "ab%d" % t)
+
+        steps = {"leavers": leavers, "arrive": arrive, "stays": stays, "base": base, "signs": signs, "less": less,
+                 "list": lambda: turned(ul("l", 0, 16), "lrow", L, 256.0, "ta"), "B": send_b}
+        for s in AFTER.split():
+            steps[s]()
+        tt(sm("dd", 0, NM), sm("ta", 0, NM), sm("cap96", 0, NM), OP.min)
+        tt(sm("dd", NM, 15), V("mso", 119, 120 * ND, 120), sm("cap96", NM, 15), OP.min)
+        cp(ul("dest", 0, NM), sm("dd", 0, NM))
+        ts(ul("dest", NM, 15), sm("dd", NM, 15), OFF, OP.add)
+
+        lin(V("qrow", 0, C), IND(V("iota", 0, 512), ul("dest", 0, 15)), on="a")
+        cp(IND(V("vv", 0, 480), ul("dest", 0, 8)), V(ids[0], 0, 128))
+        scan(V("suf", 0, C, -1), V("zer", 0, C), V("qrow", 0, C, -1), float(C), OP.add, OP.min)
+        lin(V("xx", 96, 176), IND(V("suf", 0, 256), ul("xl", 6, 11)), bias=UP)
+        lin(V("xx", 0, 96), IND(V("suf", 0, 256), ul("xl", 0, 6)), bias=UP)
+        cp(IND(V("vv", 0, 480), ul("dest", 8, 15)), V(ids[0], 128, C))
+        lin(V("zz", 0, S), IND(V("suf", 0, 256), ul("qlo", 0, 24)), on="a")
+        lin(V("sxx", 0, 80), IND(V("spb", 0, 256), ul("xl", 6, 11)))
 
         LO, HI, CL = V("xx", 0, 48), V("xx", 48, 96), V("xx", 96, 144)
-        tt(sm("cnt"), V("cum", 1, 25), V("cum", 0, 24), OP.subtract)
-        act(sm("y16", 0, 24), sm("cnt"), scale=sm("o16", 0, 1))
-        act(sm("y16", 24, 48), sm("cnt"), scale=sm("o16", 1, 2))
-        for b in range(4):
-            act(TB(b, ARR, OWN), PS(b, ARR, OWN), scale=64.0)
+        tt(sm("sc"), V("sxx", 48, 72), V("sxx", 0, 24), OP.subtract)
+        ts(sm("sc13"), sm("sc"), float(Q1), OP.max)
+        tt(sm("cnt"), V("xx", 144, 168), V("xx", 96, 120), OP.subtract)
         tt(sm("c64", 0, 48), HI, LO, OP.subtract)
         tt(sm("big"), sm("cnt"), sm("sc13"), OP.is_gt)
         tt(sm("has"), sm("cnt"), sm("sc"), OP.is_gt)
-        tt(sm("y64", 0, 48), sm("c64", 0, 48), sm("o64", 0, 48), OP.mult)
+        ts(sm("w3"), sm("c64"), float(Q2), OP.is_gt, 192.0, OP.mult)
         scan(sm("any"), sm("rs4"), sm("big"), 0.0, OP.mult, OP.max)
         tt(sm("hz"), sm("has"), sm("n4"), OP.add)
-        ts(sm("w3"), sm("c64"), float(Q2), OP.is_gt, 192.0, OP.mult)
-        tt(V("tbl", 1, 192, 4), sm("y64", 0, 48), LO, OP.add)
-        act(V("tbl", 3, 192, 4), V("tbl", 1, 192, 4))
-        tt(sm("hz2"), sm("hz"), sm("has"), OP.add)
         tt(sm("w3"), sm("w3"), sm("big"), OP.mult)
-        tt(V("tbl", 0, 192, 4), CL, sm("rst", 0, 48), OP.add)
-        tt(sm("mr", 0, 32), IND(sm("any", 0, 32), ul("xl", 10, 12)), sm("hz2", 0, 32), OP.add)
+        tt(sm("hz2"), sm("hz"), sm("has"), OP.add)
+        tt(sm("mr", 0, 32), IND(sm("any", 0, 32), ul("xc", 12, 14)), sm("hz2", 0, 32), OP.add)
         run("v", [sm("w3")], [sm("f3", 0, 1)],
-            lambda: g.vector.tensor_reduce(ap(sm("f3", 0, 1)), ap(sm("w3")), AxisListType.X, OP.max))
+            lambda: g.vector.tensor_reduce(ap(sm("f3", 0, 1)), ap(sm("w3")), AxisListType.X, OP.max), 64)
         pick(sm("mw", 0, 32), sm("mr", 0, 32), 32)
-        tt(V("tbl", 2, 192, 4), sm("y16", 0, 48), CL, OP.add)
         ts(ul("md", 0, 2), sm("mw", 15, 32, 16), sm("f3", 0, 1), OP.add)
+        pick(V("e1", 0, S), V("zz", 0, S), S)
+        pick(V("e2", 0, S), V("zz", 1, S + 1), S)
+        lin(V("tbl", 0, 96, 4), V("e1", 15, S, 16))
+        lin(V("tbl", 96, 192, 4), V("e2", 15, S, 16))
+        tt(sm("y64", 0, 48), sm("c64", 0, 48), sm("o64", 0, 48), OP.mult)
+        tt(V("tbl", 1, 192, 4), sm("y64", 0, 48), LO, OP.add)
+        lin(V("tbl", 3, 192, 4), V("tbl", 1, 192, 4))
+        lin(sm("y16", 0, 24), sm("cnt"), sm("o16", 0, 1))
+        lin(sm("y16", 24, 48), sm("cnt"), sm("o16", 1, 2))
+        tt(V("tbl", 2, 192, 4), sm("y16", 0, 48), CL, OP.add)
+        act(V("isa", 0, C), V("vv", 0, C), AF.Relu, bias=-255.0, scale=-1.0)
         scan(V("aa", 0, C), V("isa", 0, C), V("zer", 0, C), float(ARR - 257), OP.add, OP.add)
+        tt(V("sq", 0, C), V("vv", 0, C), V("aa", 0, C), OP.max)
         ts(ul("qlo", 0, 32), IND(V("tbl", 0, 288), ul("md", 0, 2)), MAGIC, OP.add, -MAGIC, OP.add)
-        act(sm("r", 0, 32), IND(V("tbl", 0, 288), ul("md", 0, 2)), AF.Identity, bias=MAGIC)
-        act(sm("rh", 0, 32), IND(V("tbl", 96, 384), ul("md", 0, 2)), AF.Identity, bias=MAGIC)
-        act(V("e1", 0, S), IND(V("aa", 0, 256), ul("qlo", 0, 24)))
-        tt(V("wb", 0, S), IND(V("vv", 0, 256), ul("qlo", 0, 24)), V("dm", 0, S), OP.mult)
-        if not last:
-            const(V("vv", 0, C), -256)
-        tt(sm("valid"), sm("rh"), sm("r"), OP.is_gt)
+        lin(sm("r", 0, 32), IND(V("tbl", 0, 288), ul("md", 0, 2)), bias=MAGIC, on="a")
+        lin(sm("rh", 0, 32), IND(V("tbl", 96, 384), ul("md", 0, 2)), bias=MAGIC, on="a")
+        tt(V("wb", 0, S), IND(V("sq", 0, 256), ul("qlo", 0, 24)), V("dm", 0, S), OP.mult)
         segsum(V("wb2", 0, S), V("wb", 0, S), S)
-        act(sm("cap"), sm("valid"), AF.Identity, bias=-256.0, scale=1024.0)
-        if not last:
-            act(sm("gap"), sm("valid"), AF.Identity, bias=BIG, scale=-BIG)
-        pick(V("e2", 0, S), V("e1", 0, S), S)
-        tt(sm("tw"), V("wb2", 15, S, 16), V("e2", 15, S, 16), OP.max)
-        if not last:
-            tt(sm("d1"), sm("r"), sm("gap"), OP.max)
-        tt(sm("tw"), sm("tw"), sm("cap"), OP.min)
-        if not last:
-            tt(sm("d1"), sm("d1"), sm("k240m"), OP.min)
+        tt(sm("gap"), sm("rh"), sm("r"), OP.is_le)
+        lin(sm("gap"), sm("gap"), BIG)
+        tt(sm("tw"), V("wb2", 15, S, 16), sm("gap"), OP.subtract)
         ts(ul("to", 0, 24), sm("tw"), 256.0, OP.add)
         if not last:
+            tt(sm("d1"), sm("r"), sm("gap"), OP.max)
+            tt(sm("d1"), sm("d1"), sm("k240m"), OP.min)
             ts(ul("d2", 0, 24), sm("d1"), -MAGIC, OP.add)
+
+        if first:
+            quant("qe", "se", 0, 256, V("et", 0, 1024))
+            quant("qe", "se", 256, 512, V("et", 1024, 2048))
+            const(V("srw", 0, 624))
+            const(V("idmap", 0, ARR), -1)
+            iota(V("idmap", ARR, OWN), [[1, L]], S)
+            iota(V("idmap", OWN, 512), [[1, S]])
+            quant("qv", "sv", 0, 128, V("vs", 0, 512))
+        landed([V("ql", la, lz), V("sl", la, lz)], "ab%d" % t)
+        for b in range(4):
+            mm(b, "qe", "se", 128 * b, "ql", "sl", la - 32, lz)
+            lin(TB(t + 1, b, ARR, OWN), PS(b, ARR, OWN), 64.0)
+        if not last:
+            const(V("vv", 0, C), -256)
+            sk = "sk%d" % t
+            lin(V("arow", 0, L), IND(V("pp", 0, ptop), ul("l", 0, 6)))
+            tr(V("atr", 0, L), V("arow", 0, L))
+            lin(V(sk, 0, 6), V("atr", 0, L, 16))
+            send(T["lk%d" % t][:], T[sk][:], [V(sk, 0, 6)], "ak%d" % t)
 
     for c in range(2):
         a, z = (0, CW) if c == 0 else (CW, S)
         for b in range(4):
-            parts("va"[b % 2], "fi", b, 512, ul("to", a // 16, z // 16), a, z)
+            parts("va", R, "fi", b, 512, ul("to", a // 16, z // 16), a, z)
         quant("qf", "sf", a, z, V("fi", 4 * a, 4 * z))
         mm(c, "qv", "sv", 0, "qf", "sf", a, z)
-        store("s", T.oc[:, 4 * a:4 * z], T.qf[:, a:z].bitcast(dt.uint8), [V("qf", a, z)])
-    act(V("olr", 0, S), IND(V("idmap", 0, 512), ul("to", 0, 24)))
-    cp(V("yo", 0, CW), PS(0, 0, CW))
-    cp(V("yo", CW, S), PS(1, 0, S - CW))
+        lin(V("yo", a, z), PS(c, 0, z - a))
+        store("sa"[c], T.y[:, a:z], T.yo[:, a:z], [V("yo", a, z)], DMA + 4 * (z - a))
+        store("s", T.oc[:, 4 * a:4 * z], T.qf[:, a:z].bitcast(dt.uint8), [V("qf", a, z)], DMA + 4 * (z - a))
+    lin(V("olr", 0, S), IND(V("idmap", 0, 512), ul("to", 0, 24)))
     for k in range(4):
         store("s", T.osc[4 * k:4 * k + 4, :], T.sf[32 * k:32 * k + 4, :], [V("sf", 0, S)])
     store("a", T.ol[:], T.olr[0:128:16, :], [V("olr", 0, S)])
-    store("a", T.y[:], T.yo[:], [V("yo", 0, S)])
 
+    issue()
     lastval = {}
-    for sem, val, seen in ops:
+    for sem, val, seen in ops.values():
         lastval[sem] = max(lastval.get(sem, 0), val)
     for sem in lastval:
         if waited.get(sem, 0) < lastval[sem]:

@@ -7,17 +7,25 @@ MAGIC = 12582912.0
 UP = 0.4921875
 OFF = 200.0
 NA = 6
-NM = 7
+NM = 6
 ND = 15 - NM
 CW = 256
-WAKE, DMA, GATHER, SCATTER = 190, 2300, 1.56, 3.8
-PASSES = 3
+WAKE = 160
+DMA = 2600
+GATHER, SCATTER = 1.56, 3.8
+PASSES = 1500
+SEED = 1
+PLAN = []
+OUTS = [(0, 192), (192, 384)]
 LOG = []
 HOOK = []
 LAYER = "s g0 q0 g1 f0 q1 a0 f1 a1 t0 t1"
 ENG = dict(g0="va", g1="va", f0="v", f1="v", t0="a", t1="a", kk="a")
-AFTER = "leavers arrive stays base signs list B less"
-NSC = 3
+AFTER = "arrive stays base signs less"
+NSC = 1
+SPARE = 300
+HI = 112
+TAIL = [(0, 24)]
 X4, U8, U16, BF, F32 = "float8_e4m3fn_x4", "uint8", "uint16", "bfloat16", "float32"
 
 
@@ -32,9 +40,8 @@ SCRATCH = {
     "qu2": _sb(128, X4), "su2": _sb(128, U8), "qv": _sb(128, X4), "sv": _sb(128, U8),
     "qw": _sb(512, X4), "sw": _sb(512, U8), "qe": _sb(512, X4), "se": _sb(512, U8),
     "ones": _sb(512, BF), "et": _sb(2048, BF), "tb0": _sb(2048, BF), "tb1": _sb(2048, BF),
-    "fi": _sb(1536, BF), "f64": _sb(1536, BF), "ti": _sb(1536, BF), "bt": _sb(512, BF),
-    "qf": _sb(384, X4), "sf": _sb(384, U8), "qt": _sb(384, X4), "st": _sb(384, U8),
-    "qb": _sb(384, X4), "sb": _sb(384, U8), "ql": _sb(416, X4), "sl": _sb(416, U8),
+    "fi": _sb(1536, BF), "f64": _sb(1536, BF), "ti": _sb(1536, BF), "df": _sb(2048, BF),
+    "qf": _sb(384, X4), "sf": _sb(384, U8),
     "yo": _sb(384, F32), "olr": _sb(384, F32),
     "iota": _sb(512, F32), "t16": _sb(384, BF), "dm": _sb(384, BF), "mx": _sb(384, BF), "rs": _sb(384, BF),
     "nd": _sb(240, BF), "step": _sb(240, BF), "idmap": _sb(512, F32), "xrow": _sb(256, BF), "xr": _sb(256, BF),
@@ -50,13 +57,18 @@ SCRATCH = {
     "e1": _sb(384, BF), "e2": _sb(384, BF), "zz": _sb(400, BF),
     "mso": _sb(120 * ND, BF), "mcp": _sb(240 * ND, BF), "sf2": _sb(241 * NM, F32),
     "vv": _sb(480, BF), "isa": _sb(240, BF), "aa": _sb(240, BF), "sq": _sb(256, BF),
-    "qrow": _sb(240, BF), "suf": _sb(256, BF), "xx": _sb(176, F32), "tbl": _sb(384, F32),
+    "qrow": _sb(240, BF), "suf": _sb(256, BF), "tbl": _sb(448, F32),
     "srw": _sb(624, BF), "srx": _sb(240, BF),
     "sm": _sb(64 * 48, F32), "u16": _sb(32 * 16, U16),
 }
 for _t in range(R):
     SCRATCH["sp%d" % _t] = _sb(16, F32)
     SCRATCH["lp%d" % _t] = _sb(16, F32)
+    SCRATCH["lo%d" % _t] = _sb(16, U16)
+    SCRATCH["ll%d" % _t] = _sb(16, U16)
+    for _q, _s in (("qt", "st"), ("ql", "sl")):
+        SCRATCH[_q + str(_t)] = _sb(384, X4)
+        SCRATCH[_s + str(_t)] = _sb(384, U8)
 for _t in range(R - 1):
     SCRATCH["sk%d" % _t] = _sb(6, F32)
     SCRATCH["lk%d" % _t] = _sb(6, F32)
@@ -64,7 +76,7 @@ for _t in range(R - 1):
 POOLS = {"v": 48, "a": 32, "p": 12, "g": 12}
 LOADS = ["x", "u", "v", "wc", "ws"]
 SEMAPHORES = ([e + str(i) for e in POOLS for i in range(POOLS[e])] + ["ld_" + n for n in LOADS]
-              + [n + str(t) for n in ("ap", "ak", "ab") for t in range(R)] + ["sent", "out_s", "out_a"])
+              + [n + str(t) for n in ("ap", "ak", "ab", "al") for t in range(R)] + ["sent", "out_s", "out_a"])
 
 
 def V(name, a, b, step=1):
@@ -100,6 +112,9 @@ def rank_program(g, core, T, topo):
             return False
         if a[3] > 1 and a[3] == b[3]:
             return (a[1] - b[1]) % a[3] == 0
+        if a[3] > 1 >= b[3] or b[3] > 1 >= a[3]:
+            s, r = (a, b) if a[3] > 1 else (b, a)
+            return any(r[1] <= c < r[2] for c in range(s[1], s[2], s[3]))
         return True
 
     def flat(vs):
@@ -168,25 +183,41 @@ def rank_program(g, core, T, topo):
                     while k < len(b) and b[k][0] < a + c:
                         a = max(a, b[k][1])
                         k += 1
-                    if best is None or (a + c, c) < best[0]:
-                        best = ((a + c, c), a, e, k)
-                (end, c), a, e, k = best
+                    late = a + c + (SPARE if e == "v" else 0)
+                    if best is None or late < best[0]:
+                        best = (late, a + c, a, e, k)
+                late, end, a, e, k = best
                 busy[e].insert(k, (a, end))
                 span[i] = (a, end, e)
             return span
 
-        seq = list(range(n))
-        best = None
-        for _ in range(PASSES):
+        def close(seq):
             span = lay(seq, False)
-            end = max(span[i][1] + prog[i][3] for i in range(n))
-            LOG.append(end)
-            if best is None or end < best[0]:
-                best = (end, span)
             back = lay(sorted(range(n), key=lambda i: (-span[i][1] - prog[i][3], -i)), True)
-            seq = sorted(range(n), key=lambda i: (-back[i][1], i))
-        span = best[1]
-        return [(i, span[i][2]) for i in sorted(range(n), key=lambda i: (span[i][0], i))]
+            span = lay(sorted(range(n), key=lambda i: (-back[i][1], i)), False)
+            return max(span[i][1] + prog[i][3] for i in range(n)), span
+
+        if not PLAN:
+            now = best = close(list(range(n)))
+            x = [SEED]
+
+            def unit():
+                x[0] = (x[0] * 1103515245 + 12345) % 2 ** 31
+                return x[0] / 2 ** 31
+
+            for k in range(PASSES):
+                a, far, wide = unit() * now[0], (300, 1000, 2500)[k % 3], (2000, 5000, 10000)[k // 3 % 3]
+                at = {}
+                for i in range(n):
+                    s = now[1][i][0]
+                    s += far * (unit() - 0.5) if a <= s < a + wide else 0
+                    at[i] = max([s] + [at[j] for j in prog[i][1]])
+                new = close(sorted(range(n), key=lambda i: (at[i], i)))
+                now = new if new[0] <= now[0] + 30 else now
+                best = new if new[0] < best[0] else best
+            LOG.append(best[0])
+            PLAN.extend((i, best[1][i][2]) for i in sorted(range(n), key=lambda i: (best[1][i][0], i)))
+        return PLAN
 
     def wait(e, i):
         Q[e].wait_ge(T.sem[ops[i][0]], ops[i][1])
@@ -205,7 +236,7 @@ def rank_program(g, core, T, topo):
                 n, k = len(count[e]), POOLS[e]
                 deps = set(deps) | set([count[e][n - k]] if n >= k else [])
             for d in sorted(deps, key=place.get, reverse=True):
-                if not known[e] >> d & 1:
+                if d in ops and not known[e] >> d & 1:
                     wait(e, d)
             if not kind:
                 ways[e][0]().then_inc(T.sem[e + str(n % k)], 1)
@@ -302,11 +333,12 @@ def rank_program(g, core, T, topo):
 
     sends = {}
 
-    def send(dst, src, reads, sem):
-        i = note({"g": (lambda: g.remote_dma(dst, src, T.sem[sem], T.sem.sent, pid, rid, mask), 330)}, reads, [],
-                 ("sent", 0), DMA if sends else 2 * DMA)
+    def send(dst, src, reads, sem, behind=(), more=0):
+        i = note({"g": (lambda: g.remote_dma(dst, src, T.sem[sem], T.sem.sent, pid, rid, mask),
+                        330 if sends else 330 + DMA)}, reads, [], ("sent", 0), DMA + more, behind)
         sends.setdefault(sem, []).append(i)
         total["sent"] += neng
+        return i
 
     def landed(writes, sem):
         note({"-": (None, 0)}, [], writes, (sem, len(sends[sem]) * neng), -WAKE, sends[sem])
@@ -337,9 +369,9 @@ def rank_program(g, core, T, topo):
     def segsum(out, row, n):
         scan(out, V("rs", 0, n), row, 0.0, OP.mult, OP.add)
 
-    def turned(out, row, n, more, via):
-        tr(V(via, 0, n), V(row, 16, 16 + n))
-        tr(V(via, 256, 256 + min(n + 32, 256)), V(row, 0, min(n + 32, 256)))
+    def turned(out, row, n, more, via, o=0):
+        tr(V(via, 0, n), V(row, o + 16, o + 16 + n))
+        tr(V(via, 256, 256 + min(n + 32, 256)), V(row, o, o + min(n + 32, 256)))
         ts(out, IND(V(via, 0, 512), ul("tw", 0, 1)), more, OP.add)
 
     load("a", "u", V("us", 0, 512), T.us[:], T.u[:], 2700)
@@ -351,9 +383,8 @@ def rank_program(g, core, T, topo):
     scol = sm("s", 0, 1)
     run("g", [], [V("pint", 0, 1)], lambda: g.iota(T.pint[:, 0:1], [[0, 1]], 0, 1), 150)
     iota(sm("c", 0, 32), [[1, 32]])
-    iota(sm("k2", 0, 48), [[1, 2], [16, 24]])
+    iota(sm("k2", 0, 56), [[1, 2], [16, 28]])
     fill(V("rs", 0, 384), 1.0)
-    fill(V("bt", 0, 512), 0.0)
     fill(sm("beta", 0, 16), -1.0)
     fill(sm("ra", 0, 16), 0.0)
     ts(V("pint", 1, 2), V("pint", 0, 1), 15, OP.bitwise_and)
@@ -371,7 +402,6 @@ def rank_program(g, core, T, topo):
     ts(V("nd", 0, C), V("t16", 0, C), scol, OP.not_equal)
     ts(V("mx", 0, 384), V("t16", 0, 384), scol, OP.is_le, BIG, OP.mult)
     ts(sm("s", 2, 3), V("pint", 2, 3), 17.0, OP.mult, scol, OP.add)
-    quant("ql", "sl", 0, 128, V("bt", 0, 512))
     ts(ul("tw", 0, 1), sm("s", 2, 3), 16.0, OP.mult, 511.0, OP.min)
 
     def constants():
@@ -381,19 +411,23 @@ def rank_program(g, core, T, topo):
         const(V("tb0", 0, 2048, 512))
         const(V("tb1", 0, 2048, 512))
         const(V("xrow", 0, 256), 33)
-        for o in (16, 40):
-            iota(V("xrow", o + 4, o + 24), [[4, 5], [0, 4]], 4)
-            iota(V("xrow", o + 48, o + 72), [[4, 6], [0, 4]], 4)
-            const(V("xrow", o + 68, o + 72), 32)
-            iota(V("xrow", o + 97, o + 120), [[1, 23]], 1)
-        iota(V("xrow", 160, 184), [[1, 24]], 1)
-        const(V("xrow", 183, 184), 32)
-        iota(V("xrow", 208, 240), [[4, 8], [0, 4]], 3)
+        for o in (16, 44):
+            iota(V("xrow", o + 1, o + 24), [[1, 23]], 1)
+            iota(V("xrow", o + 68, o + 88), [[4, 5], [0, 4]], 4)
+            const(V("xrow", o + 88, o + 92), 32)
+        const(V("xrow", 40, 41), 32)
+        iota(V("xrow", 144, 174), [[4, 6], [1, 5]], 1)
+        const(V("xrow", 148, 174, 5), 33)
+        const(V("xrow", 172, 173), 32)
+        iota(V("xrow", 176, 206), [[4, 6], [1, 5]])
+        const(V("xrow", 180, 206, 5), 33)
+        const(V("xrow", 176, 177), 33)
+        iota(V("xrow", 208, 232), [[5, 6], [0, 4]], 4)
+        const(V("xrow", 232, 240), 31)
         iota(sm("r", 32, 34), [[1, 2]], int(MAGIC) + C)
         const(V("xr", 0, 256))
         const(V("tc", 0, 512))
         iota(V("idb", 0, S), [[1, S]], OWN - 256)
-        const(V("lrow", 0, 16))
         const(V("step", 0, L))
         const(V("step", L, C), 1)
         const(V("zer", 0, C))
@@ -401,12 +435,14 @@ def rank_program(g, core, T, topo):
         const(V("kk", C, 256))
         const(V("kt0", 0, 1))
         const(V("kt1", 0, 1))
-        iota(sm("m4", 0, 48), [[1, 2], [0, 6], [16, 4]])
+        iota(sm("m4", 0, 56), [[1, 2], [0, 7], [16, 4]])
         iota(sm("n4"), [[4, 24]])
-        const(sm("hz2", 24, 32), 95)
-        const(sm("any", 24, 32))
-        const(sm("rs4"), 1)
-        const(sm("rs4", 0, 24, 4))
+        const(sm("hz", 24, 32), 95)
+        const(sm("sc", 24, 32))
+        const(sm("y16", 24, 28))
+        const(sm("m5", 0, 32), 1)
+        const(sm("m5", 0, 32, 5))
+        const(sm("m5", 4, 32, 5), 2)
         const(V("sq", C, 256))
         const(V("suf", C, C + 1), C)
         const(V("suf", C + 1, 256))
@@ -416,25 +452,24 @@ def rank_program(g, core, T, topo):
             o = V("et", 512 * b, 512 * b + 512)
             run("g", [V("ones", 0, 512)], [o],
                 lambda o=o, b=b: g.affine_select(ap(o), T.ones[:], [[-1, 512]], OP.is_equal, 0.0, b, 4), 1200)
-        ts(sm("yf", 0, 48), sm("k2", 0, 48), scol, OP.add, float(C) / S, OP.mult)
+        ts(sm("yf", 0, 56), sm("k2", 0, 56), scol, OP.add, float(C) / S, OP.mult)
         ts(sm("k240"), sm("k2"), scol, OP.add, float(C), OP.add)
-        ts(sm("yf", 0, 48), sm("yf", 0, 48), UP, OP.add, MAGIC, OP.add)
+        ts(sm("yf", 0, 56), sm("yf", 0, 56), UP, OP.add, MAGIC, OP.add)
         lin(sm("k240m"), sm("k240"), bias=MAGIC)
         ts(ul("qlo", 0, 24), sm("yf"), -MAGIC, OP.add)
         for a in (0, C):
             lin(V("vv", a, a + C), V("rs", 0, C), 0.0, -256.0)
         for b in range(4):
-            lin(V("tbl", 192 + b, 384, 4), sm("yf", 0, 48), bias=-MAGIC)
+            lin(V("tbl", 2 * HI + b, 4 * HI, 4), sm("yf", 0, 56), bias=-MAGIC)
         lin(sm("r", 0, 24), sm("yf", 0, 24))
-        lin(sm("k40", 0, 15), sm("k240", 0, 15), bias=-2 * OFF)
         lin(sm("o16", 0, 2), sm("c", 0, 2), bias=scol)
         lin(sm("o16", 0, 2), sm("o16", 0, 2), 1.0 / 16)
-        lin(sm("o64", 0, 48), sm("m4", 0, 48), bias=scol)
-        lin(sm("o64", 0, 48), sm("o64", 0, 48), 1.0 / 64)
+        lin(sm("o64", 0, 56), sm("m4", 0, 56), bias=scol)
+        lin(sm("o64", 0, 56), sm("o64", 0, 56), 1.0 / 64)
         turned(ul("xc", 0, 16), "xrow", 224, 0.0, "tc")
 
     def leaf_lists():
-        lin(V("xr", 16, 192), IND(sm("r", 0, 64), ul("xc", 0, 11)), bias=-MAGIC)
+        lin(V("xr", 16, 208), IND(sm("r", 0, 64), ul("xc", 0, 12)), bias=-MAGIC)
         turned(ul("xl", 0, 16), "xr", 192, 0.0, "tc")
 
     def ranking(K):
@@ -495,6 +530,7 @@ def rank_program(g, core, T, topo):
         top = OWN + C if t < 2 else 512
         kt, ktn = "kt%d" % (t % 2), "kt%d" % ((t + 1) % 2)
         ch = [(0, cw), (cw, 256 if first else S)]
+        q_t, s_t = "qt%d" % t, "st%d" % t
 
         def gather(c):
             for b in range(4):
@@ -518,10 +554,10 @@ def rank_program(g, core, T, topo):
 
         def qt(c):
             a, z = ch[c]
-            quant("qt", "st", a, z, V("ti", 4 * a, 4 * z))
-            mm(4 * c, "qu2", "su2", 0, "qt", "st", a, z)
+            quant(q_t, s_t, a, z, V("ti", 4 * a, 4 * z))
+            mm(4 * c, "qu2", "su2", 0, q_t, s_t, a, z)
             if first:
-                mm(4 * c + 1, "qu2", "su2", 0, "qt", "st", a, z)
+                mm(4 * c + 1, "qu2", "su2", 0, q_t, s_t, a, z)
                 n = min(z, C) - a
                 tt(V("wm", a, a + n), PS(4 * c, 0, n), V("dm", 0, n), OP.mult)
             lin(V("pp", OWN + a, OWN + z), PS(4 * c + first, 0, z - a))
@@ -563,21 +599,19 @@ def rank_program(g, core, T, topo):
         sp, lp = "sp%d" % t, "lp%d" % t
         tr(V("ptr", 0, 256), V(K[0], K[1], K[1] + 256))
         lin(V(sp, 0, 16), V("ptr", 0, 256, 16))
-        send(T[lp][:], T[sp][:], [V(sp, 0, 16)], "ap%d" % t)
+        p_out = send(T[lp][:], T[sp][:], [V(sp, 0, 16)], "ap%d" % t)
+        n, ql, sl, lo, ll = ch[1][1], "ql%d" % t, "sl%d" % t, "lo%d" % t, "ll%d" % t
+        send(T[ql][:, 0:n].bitcast(dt.uint8), T[q_t][:, 0:n].bitcast(dt.uint8), [V(q_t, 0, n)], "ab%d" % t, [p_out], 1500)
+        send(T[sl][:, 0:n], T[s_t][:, 0:n], [V(s_t, 0, n)], "ab%d" % t, [p_out], 1500)
         rk = ranking(K)
         if not first:
             keys()
         leaf_lists()
 
         W = C + 1
-        o = 128 * t
-        la, lz = 128 + L * t, 128 + L * t + L
 
         def key(j):
             return V("kx", 16 * j + 15, 16 * j + 16)
-
-        def leavers():
-            cp(IND(V("lrow", 16, 16 + C), ul("rk", 0, 15)), ids)
 
         def arrive():
             landed([V(lp, 0, 16)], "ap%d" % t)
@@ -592,12 +626,13 @@ def rank_program(g, core, T, topo):
         def base():
             for a, z, v in rk:
                 lin(sm("gn", a, z), v, -2 * BIG, (2 * L - 1) * BIG)
-            tt(sm("gh", 0, 15), sm("k40", 0, 15), V("spe", 15, C, 16), OP.subtract)
+                lin(sm("gh", a, z), v, bias=C - OFF)
             tt(sm("base", 0, 15), V("spe", 15, C, 16), sm("gn", 0, 15), OP.max)
             tt(sm("base", 0, 15), sm("base", 0, 15), sm("gh", 0, 15), OP.min)
             lin(V("sf2", C, W * NM, W), sm("base", 0, NM), bias=OFF)
-            lin(sm("cap96", 0, NM), sm("base", 0, NM), bias=OFF + L)
-            lin(sm("cap96", NM, 15), sm("base", NM, 15), bias=float(L))
+            lin(sm("b96", 0, 15), sm("base", 0, 15), bias=float(L))
+            tt(sm("cap96", 0, 15), sm("b96", 0, 15), sm("gh", 0, 15), OP.min)
+            lin(sm("cap96", 0, NM), sm("cap96", 0, NM), bias=OFF)
 
         def signs():
             for j in range(NM):
@@ -612,16 +647,7 @@ def rank_program(g, core, T, topo):
                 scan(V("mso", 120 * j, 120 * j + 120), V("mcp", C * j, C * j + 120), V("mcp", C * j + 120, C * j + C),
                      sm("base", NM + j, NM + j + 1), OP.add, OP.add)
 
-        def send_b():
-            for b in range(4):
-                parts("av", t + 1, "bt", b, OWN + ch[1][1], ul("l", 0, 6), 32, 128)
-            quant("qb", "sb", o, o + 128, V("bt", 0, 512))
-            send(T.ql[:, la:lz].bitcast(dt.uint8), T.qb[:, o + 32:o + 128].bitcast(dt.uint8), [V("qb", o, o + 128)],
-                 "ab%d" % t)
-            send(T.sl[:, la:lz], T.sb[:, o + 32:o + 128], [V("sb", o, o + 128)], "ab%d" % t)
-
-        steps = {"leavers": leavers, "arrive": arrive, "stays": stays, "base": base, "signs": signs, "less": less,
-                 "list": lambda: turned(ul("l", 0, 16), "lrow", L, 256.0, "ta"), "B": send_b}
+        steps = {"arrive": arrive, "stays": stays, "base": base, "signs": signs, "less": less}
         for s in AFTER.split():
             steps[s]()
         tt(sm("dd", 0, NM), sm("ta", 0, NM), sm("cap96", 0, NM), OP.min)
@@ -632,51 +658,54 @@ def rank_program(g, core, T, topo):
         lin(V("qrow", 0, C), IND(V("iota", 0, 512), ul("dest", 0, 15)), on="a")
         cp(IND(V("vv", 0, 480), ul("dest", 0, 8)), V(ids[0], 0, 128))
         scan(V("suf", 0, C, -1), V("zer", 0, C), V("qrow", 0, C, -1), float(C), OP.add, OP.min)
-        lin(V("xx", 96, 176), IND(V("suf", 0, 256), ul("xl", 6, 11)), bias=UP)
-        lin(V("xx", 0, 96), IND(V("suf", 0, 256), ul("xl", 0, 6)), bias=UP)
-        cp(IND(V("vv", 0, 480), ul("dest", 8, 15)), V(ids[0], 128, C))
-        lin(V("zz", 0, S), IND(V("suf", 0, 256), ul("qlo", 0, 24)), on="a")
-        lin(V("sxx", 0, 80), IND(V("spb", 0, 256), ul("xl", 6, 11)))
+        SUF = V("suf", 0, 256)
+        lin(sm("xd", 0, 32), IND(SUF, ul("xl", 10, 12)), bias=float(Q1))
+        lin(V("sxx", 0, 32), IND(V("spb", 0, 256), ul("xl", 0, 2)))
+        tt(sm("sc"), V("sxx", 1, 25), V("sxx", 0, 24), OP.subtract)
+        tt(sm("cls", 0, 32), IND(SUF, ul("xl", 0, 2)), sm("sc", 0, 32), OP.add)
+        lin(sm("xa", 0, 64), IND(SUF, ul("xl", 0, 4)))
+        lin(sm("xw", 0, 64), IND(SUF, ul("xl", 4, 8)), bias=UP)
 
-        LO, HI, CL = V("xx", 0, 48), V("xx", 48, 96), V("xx", 96, 144)
-        tt(sm("sc"), V("sxx", 48, 72), V("sxx", 0, 24), OP.subtract)
-        ts(sm("sc13"), sm("sc"), float(Q1), OP.max)
-        tt(sm("cnt"), V("xx", 144, 168), V("xx", 96, 120), OP.subtract)
-        tt(sm("c64", 0, 48), HI, LO, OP.subtract)
-        tt(sm("big"), sm("cnt"), sm("sc13"), OP.is_gt)
-        tt(sm("has"), sm("cnt"), sm("sc"), OP.is_gt)
-        ts(sm("w3"), sm("c64"), float(Q2), OP.is_gt, 192.0, OP.mult)
-        scan(sm("any"), sm("rs4"), sm("big"), 0.0, OP.mult, OP.max)
+        tt(sm("big", 0, 32), IND(SUF, ul("xl", 8, 10)), sm("xd", 0, 32), OP.is_gt)
+        tt(sm("has"), sm("xa", 1, 25), sm("cls"), OP.is_gt)
+        tt(sm("c64", 0, 52), sm("xw", 4, 56), sm("xw", 0, 52), OP.subtract)
+        scan(sm("any", 0, 32), sm("m5", 0, 32), sm("big", 0, 32), 0.0, OP.mult, OP.max)
         tt(sm("hz"), sm("has"), sm("n4"), OP.add)
-        tt(sm("w3"), sm("w3"), sm("big"), OP.mult)
-        tt(sm("hz2"), sm("hz"), sm("has"), OP.add)
-        tt(sm("mr", 0, 32), IND(sm("any", 0, 32), ul("xc", 12, 14)), sm("hz2", 0, 32), OP.add)
-        run("v", [sm("w3")], [sm("f3", 0, 1)],
-            lambda: g.vector.tensor_reduce(ap(sm("f3", 0, 1)), ap(sm("w3")), AxisListType.X, OP.max), 64)
+        ts(sm("w3", 0, 6), sm("c64", 0, 24, 4), float(Q2), OP.is_gt, float(HI), OP.mult)
+        tt(sm("mr", 0, 32), IND(sm("any", 0, 32), ul("xc", 12, 14)), sm("hz", 0, 32), OP.add)
+        tt(sm("w3", 0, 6), sm("w3", 0, 6), sm("any", 4, 30, 5), OP.mult)
         pick(sm("mw", 0, 32), sm("mr", 0, 32), 32)
+        run("v", [sm("w3", 0, 6)], [sm("f3", 0, 1)],
+            lambda: g.vector.tensor_reduce(ap(sm("f3", 0, 1)), ap(sm("w3", 0, 6)), AxisListType.X, OP.max), 64)
         ts(ul("md", 0, 2), sm("mw", 15, 32, 16), sm("f3", 0, 1), OP.add)
+        cp(IND(V("vv", 0, 480), ul("dest", 8, 15)), V(ids[0], 128, C))
+        turned(V(lo, 0, 16), "vv", L, 256.0, "ta", C - 16)
+        send(T[ll][:, 0:6], T[lo][:, 0:6], [V(lo, 0, 6)], "al%d" % t)
+        lin(V("zz", 0, S), IND(SUF, ul("qlo", 0, 24)), on="a")
         pick(V("e1", 0, S), V("zz", 0, S), S)
         pick(V("e2", 0, S), V("zz", 1, S + 1), S)
         lin(V("tbl", 0, 96, 4), V("e1", 15, S, 16))
-        lin(V("tbl", 96, 192, 4), V("e2", 15, S, 16))
-        tt(sm("y64", 0, 48), sm("c64", 0, 48), sm("o64", 0, 48), OP.mult)
-        tt(V("tbl", 1, 192, 4), sm("y64", 0, 48), LO, OP.add)
-        lin(V("tbl", 3, 192, 4), V("tbl", 1, 192, 4))
-        lin(sm("y16", 0, 24), sm("cnt"), sm("o16", 0, 1))
-        lin(sm("y16", 24, 48), sm("cnt"), sm("o16", 1, 2))
-        tt(V("tbl", 2, 192, 4), sm("y16", 0, 48), CL, OP.add)
+        lin(V("tbl", HI, HI + 96, 4), V("e2", 15, S, 16))
+        tt(sm("cnt"), sm("xa", 1, 25), sm("xa", 0, 24), OP.subtract)
+        tt(sm("y64", 0, 52), sm("c64", 0, 52), sm("o64", 0, 52), OP.mult)
+        tt(V("tbl", 2, 208, 4), sm("y64", 0, 52), sm("xw", 0, 52), OP.add)
+        lin(V("tbl", 3, 208, 4), V("tbl", 2, 208, 4))
+        lin(sm("y16", 0, 24), sm("cnt"), sm("o16", 0, 1), UP)
+        lin(sm("y16", 28, 52), sm("cnt"), sm("o16", 1, 2), UP)
+        tt(V("tbl", 1, 208, 4), sm("y16", 0, 52), sm("xa", 0, 52), OP.add)
         act(V("isa", 0, C), V("vv", 0, C), AF.Relu, bias=-255.0, scale=-1.0)
         scan(V("aa", 0, C), V("isa", 0, C), V("zer", 0, C), float(ARR - 257), OP.add, OP.add)
         tt(V("sq", 0, C), V("vv", 0, C), V("aa", 0, C), OP.max)
-        ts(ul("qlo", 0, 32), IND(V("tbl", 0, 288), ul("md", 0, 2)), MAGIC, OP.add, -MAGIC, OP.add)
-        lin(sm("r", 0, 32), IND(V("tbl", 0, 288), ul("md", 0, 2)), bias=MAGIC, on="a")
-        lin(sm("rh", 0, 32), IND(V("tbl", 96, 384), ul("md", 0, 2)), bias=MAGIC, on="a")
-        tt(V("wb", 0, S), IND(V("sq", 0, 256), ul("qlo", 0, 24)), V("dm", 0, S), OP.mult)
-        segsum(V("wb2", 0, S), V("wb", 0, S), S)
+        ts(ul("qlo", 0, 32), IND(V("tbl", 0, 3 * HI), ul("md", 0, 2)), MAGIC, OP.add, -MAGIC, OP.add)
+        lin(sm("r", 0, 32), IND(V("tbl", 0, 3 * HI), ul("md", 0, 2)), bias=MAGIC, on="a")
+        lin(sm("rh", 0, 32), IND(V("tbl", HI, 4 * HI), ul("md", 0, 2)), bias=MAGIC, on="a")
         tt(sm("gap"), sm("rh"), sm("r"), OP.is_le)
         lin(sm("gap"), sm("gap"), BIG)
-        tt(sm("tw"), V("wb2", 15, S, 16), sm("gap"), OP.subtract)
-        ts(ul("to", 0, 24), sm("tw"), 256.0, OP.add)
+        for a, z in TAIL:
+            tt(V("wb", 16 * a, 16 * z), IND(V("sq", 0, 256), ul("qlo", a, z)), V("dm", 16 * a, 16 * z), OP.mult)
+            segsum(V("wb2", 16 * a, 16 * z), V("wb", 16 * a, 16 * z), 16 * (z - a))
+            tt(sm("tw", a, z), V("wb2", 16 * a + 15, 16 * z, 16), sm("gap", a, z), OP.subtract)
+            ts(ul("to", a, z), sm("tw", a, z), 256.0, OP.add)
         if not last:
             tt(sm("d1"), sm("r"), sm("gap"), OP.max)
             tt(sm("d1"), sm("d1"), sm("k240m"), OP.min)
@@ -690,26 +719,28 @@ def rank_program(g, core, T, topo):
             iota(V("idmap", ARR, OWN), [[1, L]], S)
             iota(V("idmap", OWN, 512), [[1, S]])
             quant("qv", "sv", 0, 128, V("vs", 0, 512))
-        landed([V("ql", la, lz), V("sl", la, lz)], "ab%d" % t)
+        landed([V(ql, 0, n), V(sl, 0, n)], "ab%d" % t)
+        landed([V(ll, 0, 6)], "al%d" % t)
         for b in range(4):
-            mm(b, "qe", "se", 128 * b, "ql", "sl", la - 32, lz)
-            lin(TB(t + 1, b, ARR, OWN), PS(b, ARR, OWN), 64.0)
+            mm(b, "qe", "se", 128 * b, ql, sl, 0, n)
+            lin(V("df", 512 * b + OWN, 512 * b + OWN + n), PS(b, 0, n), 64.0, on="a")
+        for b in range(4):
+            lin(TB(t + 1, b, ARR, OWN), IND(V("df", 512 * b, 512 * b + OWN + n), V(ll, 0, 6)))
         if not last:
             const(V("vv", 0, C), -256)
             sk = "sk%d" % t
-            lin(V("arow", 0, L), IND(V("pp", 0, ptop), ul("l", 0, 6)))
+            lin(V("arow", 0, L), IND(V("pp", 0, ptop), V(lo, 0, 6)))
             tr(V("atr", 0, L), V("arow", 0, L))
             lin(V(sk, 0, 6), V("atr", 0, L, 16))
             send(T["lk%d" % t][:], T[sk][:], [V(sk, 0, 6)], "ak%d" % t)
 
-    for c in range(2):
-        a, z = (0, CW) if c == 0 else (CW, S)
+    for c, (a, z) in enumerate(OUTS):
         for b in range(4):
             parts("va", R, "fi", b, 512, ul("to", a // 16, z // 16), a, z)
         quant("qf", "sf", a, z, V("fi", 4 * a, 4 * z))
         mm(c, "qv", "sv", 0, "qf", "sf", a, z)
         lin(V("yo", a, z), PS(c, 0, z - a))
-        store("sa"[c], T.y[:, a:z], T.yo[:, a:z], [V("yo", a, z)], DMA + 4 * (z - a))
+        store("sa"[z == S], T.y[:, a:z], T.yo[:, a:z], [V("yo", a, z)], DMA + 4 * (z - a))
         store("s", T.oc[:, 4 * a:4 * z], T.qf[:, a:z].bitcast(dt.uint8), [V("qf", a, z)], DMA + 4 * (z - a))
     lin(V("olr", 0, S), IND(V("idmap", 0, 512), ul("to", 0, 24)))
     for k in range(4):

@@ -10,11 +10,16 @@ NA = 6
 NM = 6
 ND = 15 - NM
 CW = 256
-WAKE = 160
-DMA = 2600
-GATHER, SCATTER = 1.56, 3.8
-PASSES = 1500
+WAKE = 280
+DMA = 2800
+GATHER = 1.56
+SCATTER = 3.8
+PASSES = 2000
 SEED = 1
+HALVES = [(0, 6), (6, 15)]
+SPLIT = 1
+FLIP = 0.3
+SLACK = 20
 PLAN = []
 OUTS = [(0, 192), (192, 384)]
 LOG = []
@@ -25,7 +30,7 @@ AFTER = "arrive stays base signs less"
 NSC = 1
 SPARE = 300
 HI = 112
-TAIL = [(0, 24)]
+TAIL = [(0, 16), (16, 24)]
 X4, U8, U16, BF, F32 = "float8_e4m3fn_x4", "uint8", "uint16", "bfloat16", "float32"
 
 
@@ -47,11 +52,10 @@ SCRATCH = {
     "nd": _sb(240, BF), "step": _sb(240, BF), "idmap": _sb(512, F32), "xrow": _sb(256, BF), "xr": _sb(256, BF),
     "pint": _sb(8, "int32"), "zer": _sb(240, BF), "ta": _sb(512, BF), "tc": _sb(512, BF), "inv": _sb(288, BF),
     "pp": _sb(512, F32), "kk": _sb(256, F32), "wm": _sb(240, F32), "wf": _sb(240, F32),
-    "ptr": _sb(256, F32), "pax": _sb(256, F32), "prow": _sb(256, F32),
+    "pq": _sb(512, F32), "prow": _sb(240, F32), "qup": _sb(128, X4), "sup": _sb(128, U8),
     "cmp": _sb(240 * (15 - NA), BF), "so": _sb(120 * (15 - NA), BF), "sa": _sb(241 * NA, BF),
     "eq": _sb(240, BF), "ex": _sb(240, BF),
     "lrow": _sb(256, BF), "idb": _sb(384, BF), "wb": _sb(384, BF), "wb2": _sb(384, BF),
-    "arow": _sb(96, F32), "atr": _sb(96, F32), "ax": _sb(96, F32),
     "kt0": _sb(512, F32), "kt1": _sb(512, F32), "krow": _sb(240, F32), "kx": _sb(240, F32),
     "strow": _sb(240, BF), "spb": _sb(256, BF), "spe": _sb(240, BF), "sxx": _sb(80, F32),
     "e1": _sb(384, BF), "e2": _sb(384, BF), "zz": _sb(400, BF),
@@ -62,21 +66,18 @@ SCRATCH = {
     "sm": _sb(64 * 48, F32), "u16": _sb(32 * 16, U16),
 }
 for _t in range(R):
-    SCRATCH["sp%d" % _t] = _sb(16, F32)
-    SCRATCH["lp%d" % _t] = _sb(16, F32)
+    SCRATCH["idl%d" % _t] = _sb(16, U16)
+    SCRATCH["idr%d" % _t] = _sb(16, U16)
     SCRATCH["lo%d" % _t] = _sb(16, U16)
     SCRATCH["ll%d" % _t] = _sb(16, U16)
     for _q, _s in (("qt", "st"), ("ql", "sl")):
         SCRATCH[_q + str(_t)] = _sb(384, X4)
         SCRATCH[_s + str(_t)] = _sb(384, U8)
-for _t in range(R - 1):
-    SCRATCH["sk%d" % _t] = _sb(6, F32)
-    SCRATCH["lk%d" % _t] = _sb(6, F32)
 
 POOLS = {"v": 48, "a": 32, "p": 12, "g": 12}
 LOADS = ["x", "u", "v", "wc", "ws"]
 SEMAPHORES = ([e + str(i) for e in POOLS for i in range(POOLS[e])] + ["ld_" + n for n in LOADS]
-              + [n + str(t) for n in ("ap", "ak", "ab", "al") for t in range(R)] + ["sent", "out_s", "out_a"])
+              + [n + str(t) for n in ("ai", "ab", "al") for t in range(R)] + ["au", "sent", "out_s", "out_a"])
 
 
 def V(name, a, b, step=1):
@@ -166,39 +167,46 @@ def rank_program(g, core, T, topo):
             for d in prog[i][1]:
                 users[d].append(i)
 
-        def lay(seq, back):
-            busy = {e: [] for e in list(Q) + ["-"]}
-            span = {}
+        ways = [[(e, c) for e, (_, c) in p[0].items()] for p in prog]
+        lag = [p[3] for p in prog]
+        ahead = [[(d, lag[d] + WAKE) for d in p[1]] for p in prog]
+        behind = [[(u, lag[i] + WAKE) for u in users[i]] for i in range(n)]
+
+        def lay(seq, links, first, lean):
+            starts, ends = {e: [] for e in list(Q) + ["-"]}, {e: [] for e in list(Q) + ["-"]}
+            st, en, on = [0] * n, [0] * n, [None] * n
             for i in seq:
-                if back:
-                    at = prog[i][3] + max([span[u][1] + WAKE for u in users[i]], default=0)
-                else:
-                    at = max([span[d][1] + prog[d][3] + WAKE for d in prog[i][1]], default=0)
+                at = first[i]
+                for d, w in links[i]:
+                    if en[d] + w > at:
+                        at = en[d] + w
                 best = None
-                for e, (_, c) in prog[i][0].items():
-                    b, k = busy[e], len(busy[e])
-                    while k and b[k - 1][1] > at:
+                for e, c in ways[i]:
+                    s, z = starts[e], ends[e]
+                    k = m = len(z)
+                    while k and z[k - 1] > at:
                         k -= 1
                     a = at
-                    while k < len(b) and b[k][0] < a + c:
-                        a = max(a, b[k][1])
+                    while k < m and s[k] < a + c:
+                        a = z[k] if z[k] > a else a
                         k += 1
-                    late = a + c + (SPARE if e == "v" else 0)
+                    late = a + c + (lean[i] if e == "v" else 0)
                     if best is None or late < best[0]:
-                        best = (late, a + c, a, e, k)
-                late, end, a, e, k = best
-                busy[e].insert(k, (a, end))
-                span[i] = (a, end, e)
-            return span
+                        best = (late, a, a + c, e, k)
+                late, st[i], en[i], e, k = best
+                on[i] = e
+                starts[e].insert(k, st[i])
+                ends[e].insert(k, en[i])
+            return st, en, on
 
-        def close(seq):
-            span = lay(seq, False)
-            back = lay(sorted(range(n), key=lambda i: (-span[i][1] - prog[i][3], -i)), True)
-            span = lay(sorted(range(n), key=lambda i: (-back[i][1], i)), False)
-            return max(span[i][1] + prog[i][3] for i in range(n)), span
+        def close(seq, lean):
+            st, en, on = lay(seq, ahead, [0] * n, lean)
+            st, en, on = lay(sorted(range(n), key=lambda i: (-en[i] - lag[i], -i)), behind, lag, lean)
+            st, en, on = lay(sorted(range(n), key=lambda i: (-en[i], i)), ahead, [0] * n, lean)
+            return max(en[i] + lag[i] for i in range(n)), st, on, lean
 
         if not PLAN:
-            now = best = close(list(range(n)))
+            now = best = close(list(range(n)), [SPARE] * n)
             x = [SEED]
 
             def unit():
@@ -207,16 +215,20 @@ def rank_program(g, core, T, topo):
 
             for k in range(PASSES):
                 a, far, wide = unit() * now[0], (300, 1000, 2500)[k % 3], (2000, 5000, 10000)[k // 3 % 3]
-                at = {}
+                at, lean = list(now[1]), list(now[3])
                 for i in range(n):
-                    s = now[1][i][0]
-                    s += far * (unit() - 0.5) if a <= s < a + wide else 0
-                    at[i] = max([s] + [at[j] for j in prog[i][1]])
-                new = close(sorted(range(n), key=lambda i: (at[i], i)))
-                now = new if new[0] <= now[0] + 30 else now
+                    if a <= at[i] < a + wide:
+                        at[i] += far * (unit() - 0.5)
+                        if len(ways[i]) > 1 and unit() < FLIP:
+                            lean[i] = 1200 * unit() - 300
+                    for d, w in ahead[i]:
+                        if at[d] > at[i]:
+                            at[i] = at[d]
+                new = close(sorted(range(n), key=lambda i: (at[i], i)), lean)
+                now = new if new[0] <= now[0] + SLACK else now
                 best = new if new[0] < best[0] else best
             LOG.append(best[0])
-            PLAN.extend((i, best[1][i][2]) for i in sorted(range(n), key=lambda i: (best[1][i][0], i)))
+            PLAN.extend((i, best[2][i]) for i in sorted(range(n), key=lambda i: (best[1][i], i)))
         return PLAN
 
     def wait(e, i):
@@ -432,7 +444,6 @@ def rank_program(g, core, T, topo):
         const(V("step", L, C), 1)
         const(V("zer", 0, C))
         const(V("spb", 0, 256), -int(OFF))
-        const(V("kk", C, 256))
         const(V("kt0", 0, 1))
         const(V("kt1", 0, 1))
         iota(sm("m4", 0, 56), [[1, 2], [0, 7], [16, 4]])
@@ -511,12 +522,16 @@ def rank_program(g, core, T, topo):
     run("v", [V("qu", 0, 128), ul("c16", 0, 8)], [V("qu2", 0, 128)], lambda: g.vector.tensor_copy(
         T.qu2[:, 0:128].bitcast(dt.uint32), T.qu[:, 0:128].bitcast(dt.uint32).indirect(ap(ul("c16", 0, 8)))), 260)
     act(V("su2", 0, 128), IND(V("su", 0, 128), ul("c16", 0, 8)))
+    send(T.qup[:].bitcast(dt.uint8), T.qu2[:].bitcast(dt.uint8), [V("qu2", 0, 128)], "au")
+    send(T.sup[:], T.su2[:], [V("su2", 0, 128)], "au")
+    landed([V("qup", 0, 128), V("sup", 0, 128)], "au")
     quant("qx", "sx", 0, C, V("xs", 0, 960))
     mm(0, "qu2", "su2", 0, "qx", "sx", 0, C)
     mm(1, "qu2", "su2", 0, "qx", "sx", 0, C)
-    tt(V("wm", 0, C), PS(0, 0, C), V("dm", 0, C), OP.mult)
     act(V("pp", OWN, OWN + C), PS(1, 0, C))
-    segsum(V("wf", 0, C), V("wm", 0, C), C)
+    for a, z in HALVES:
+        tt(V("wm", 16 * a, 16 * z), PS(0, 16 * a, 16 * z), V("dm", 16 * a, 16 * z), OP.mult)
+        segsum(V("wf", 16 * a, 16 * z), V("wm", 16 * a, 16 * z), 16 * (z - a))
     ranking(V("pp", OWN, OWN + C))
     constants()
     cp(IND(V("inv", 16, 16 + C), ul("rk", 0, 15)), V("iota", 0, C))
@@ -530,7 +545,7 @@ def rank_program(g, core, T, topo):
         top = OWN + C if t < 2 else 512
         kt, ktn = "kt%d" % (t % 2), "kt%d" % ((t + 1) % 2)
         ch = [(0, cw), (cw, 256 if first else S)]
-        q_t, s_t = "qt%d" % t, "st%d" % t
+        q_t, s_t, IDS = "qt%d" % t, "st%d" % t, V("idl%d" % t, 0, 15)
 
         def gather(c):
             for b in range(4):
@@ -568,19 +583,16 @@ def rank_program(g, core, T, topo):
                     z = a + 24 // NSC
                     cp(IND(V("srw", 0, 624), ul("d2", a, z)), V("idb", 16 * a, 16 * z))
                 pick(V("srx", 0, C), V("srw", 0, C), C)
-                ts(ul("ids", 0, 15), V("srx", 15, C, 16), 256.0, OP.add)
+                ts(IDS, V("srx", 15, C, 16), 256.0, OP.add)
+                send(T["idr%d" % t][:, 0:15], ap(IDS), [IDS], "ai%d" % t)
 
         def keys():
             if first:
                 lin(V(kt, OWN, OWN + C), IND(V("pp", 0, OWN + C), ul("to", 0, 15)))
                 pick(V("kx", 0, C), V(kt, OWN, OWN + C), C)
             else:
-                lk = "lk%d" % (t - 1)
-                landed([V(lk, 0, 6)], "ak%d" % (t - 1))
-                lin(V("ax", 0, L), IND(V(lk, 0, 6), ul("c", 0, 6)))
-                tr(V(ktn, ARR, OWN), V("ax", 0, L))
                 lin(V(kt, OWN, 512), IND(V(ktn, 0, top), ul("to", 0, 24)))
-                lin(V("krow", 0, C), IND(V(kt, 0, 512), ul("ids", 0, 15)))
+                lin(V("krow", 0, C), IND(V(kt, 0, 512), IDS))
                 pick(V("kx", 0, C), V("krow", 0, C), C)
 
         if first:
@@ -589,20 +601,21 @@ def rank_program(g, core, T, topo):
         for s in LAYER.split():
             steps[s[0]](int(s[1:] or 0))
         if first:
-            K, ids, ptop = V("pp", OWN, OWN + C), V("idb", 0, C), OWN + C
+            K, ids = V("pp", OWN, OWN + C), V("idb", 0, C)
         else:
-            tt(V("wm", 0, C), IND(V("pp", 0, 512), ul("ids", 0, 15)), V("dm", 0, C), OP.mult)
-            lin(V("kk", 0, C), IND(V("pp", 0, 512), ul("ids", 0, 15)), on=ENG["kk"])
-            K, ids, ptop = V("kk", 0, C), V("srw", 0, C), 512
-        segsum(V("wf", 0, C), V("wm", 0, C), C)
+            for a, z in HALVES:
+                P, lst = V("pp", 0, OWN + (cw if 16 * z + S - C <= cw else S)), V(IDS[0], a, z)
+                tt(V("wm", 16 * a, 16 * z), IND(P, lst), V("dm", 16 * a, 16 * z), OP.mult)
+                lin(V("kk", 16 * a, 16 * z), IND(P, lst), on=ENG["kk"])
+            K, ids = V("kk", 0, C), V("srw", 0, C)
+        for a, z in ([(0, 8), (8, 15)] if first else HALVES):
+            segsum(V("wf", 16 * a, 16 * z), V("wm", 16 * a, 16 * z), 16 * (z - a))
 
-        sp, lp = "sp%d" % t, "lp%d" % t
-        tr(V("ptr", 0, 256), V(K[0], K[1], K[1] + 256))
-        lin(V(sp, 0, 16), V("ptr", 0, 256, 16))
-        p_out = send(T[lp][:], T[sp][:], [V(sp, 0, 16)], "ap%d" % t)
         n, ql, sl, lo, ll = ch[1][1], "ql%d" % t, "sl%d" % t, "lo%d" % t, "ll%d" % t
-        send(T[ql][:, 0:n].bitcast(dt.uint8), T[q_t][:, 0:n].bitcast(dt.uint8), [V(q_t, 0, n)], "ab%d" % t, [p_out], 1500)
-        send(T[sl][:, 0:n], T[s_t][:, 0:n], [V(s_t, 0, n)], "ab%d" % t, [p_out], 1500)
+        for a, z in (ch if SPLIT else [(0, n)]):
+            send(T[ql][:, a:z].bitcast(dt.uint8), T[q_t][:, a:z].bitcast(dt.uint8), [V(q_t, a, z)], "ab%d" % t,
+                 more=4 * (z - a))
+            send(T[sl][:, a:z], T[s_t][:, a:z], [V(s_t, a, z)], "ab%d" % t, more=4 * (z - a))
         rk = ranking(K)
         if not first:
             keys()
@@ -614,9 +627,14 @@ def rank_program(g, core, T, topo):
             return V("kx", 16 * j + 15, 16 * j + 16)
 
         def arrive():
-            landed([V(lp, 0, 16)], "ap%d" % t)
-            lin(V("pax", 0, 256), IND(V(lp, 0, 16), ul("c", 0, 16)))
-            tr(V("prow", 0, 256), V("pax", 0, 256))
+            landed([V(ql, 0, n), V(sl, 0, n)], "ab%d" % t)
+            mm(6, "qup", "sup", 0, ql, sl, 0, n)
+            lin(V("pq", OWN, OWN + n), PS(6, 0, n))
+            if not first:
+                landed([V("idr%d" % t, 0, 16)], "ai%d" % t)
+                lin(V("prow", 0, C), IND(V("pq", 0, 512), V("idr%d" % t, 0, 15)))
+
+        PR = V("pq", OWN, OWN + C) if first else V("prow", 0, C)
 
         def stays():
             lin(V("strow", 0, C), IND(V("step", 0, C), ul("rk", 0, 15)))
@@ -636,13 +654,13 @@ def rank_program(g, core, T, topo):
 
         def signs():
             for j in range(NM):
-                act(V("sf2", W * j, W * j + C), V("prow", 0, C), AF.Sign, bias=key(j), scale=-1.0)
+                act(V("sf2", W * j, W * j + C), PR, AF.Sign, bias=key(j), scale=-1.0)
             for j in range(NM):
                 act(V("sf2", W * j, W * j + W), V("sf2", W * j, W * j + W), AF.Relu, accum=sm("ta", j, j + 1))
 
         def less():
             for j in range(ND):
-                ts(V("mcp", C * j, C * j + C), V("prow", 0, C), key(NM + j), OP.is_lt)
+                ts(V("mcp", C * j, C * j + C), PR, key(NM + j), OP.is_lt)
             for j in range(ND):
                 scan(V("mso", 120 * j, 120 * j + 120), V("mcp", C * j, C * j + 120), V("mcp", C * j + 120, C * j + C),
                      sm("base", NM + j, NM + j + 1), OP.add, OP.add)
@@ -719,7 +737,6 @@ def rank_program(g, core, T, topo):
             iota(V("idmap", ARR, OWN), [[1, L]], S)
             iota(V("idmap", OWN, 512), [[1, S]])
             quant("qv", "sv", 0, 128, V("vs", 0, 512))
-        landed([V(ql, 0, n), V(sl, 0, n)], "ab%d" % t)
         landed([V(ll, 0, 6)], "al%d" % t)
         for b in range(4):
             mm(b, "qe", "se", 128 * b, ql, sl, 0, n)
@@ -728,11 +745,7 @@ def rank_program(g, core, T, topo):
             lin(TB(t + 1, b, ARR, OWN), IND(V("df", 512 * b, 512 * b + OWN + n), V(ll, 0, 6)))
         if not last:
             const(V("vv", 0, C), -256)
-            sk = "sk%d" % t
-            lin(V("arow", 0, L), IND(V("pp", 0, ptop), V(lo, 0, 6)))
-            tr(V("atr", 0, L), V("arow", 0, L))
-            lin(V(sk, 0, 6), V("atr", 0, L, 16))
-            send(T["lk%d" % t][:], T[sk][:], [V(sk, 0, 6)], "ak%d" % t)
+            lin(V(kt, ARR, OWN), IND(V("pq", 0, OWN + n), V(ll, 0, 6)))
 
     for c, (a, z) in enumerate(OUTS):
         for b in range(4):

@@ -7,30 +7,48 @@ MAGIC = 12582912.0
 UP = 0.4921875
 OFF = 200.0
 NA = 6
-NM = 6
+NM = 5
 ND = 15 - NM
 CW = 256
-WAKE = 280
-DMA = 2800
-GATHER = 1.56
-SCATTER = 3.8
-PASSES = 2000
-SEED = 1
+WAKE = 265
+DMA = 2400
+GATHER = 1.75
+SCATTER = 4.4
+PASSES = 1700
+SEED = 4
+VFIX = 2
+LONG = 100
+HOLD = 1750
+AMIN = 64
+CALL = 450
+FIRST = 5500
+ISSUE = 150
+SLOW = 1.4
+MIX = 0.4
+LD = 1650
+BYTE = 0.8
+AFIX = 4
+PE = 1.55
+XP = [(0, 128), (128, 240)]
+REST = []
+CUT = [1, 1, 1, 5]
+VH = [(0, 8), (8, 15)]
 HALVES = [(0, 6), (6, 15)]
-SPLIT = 1
+HP = [(0, 6), (6, 15)]
 FLIP = 0.3
-SLACK = 20
+SLACK = 30
 PLAN = []
-OUTS = [(0, 192), (192, 384)]
+OUTS = [(0, 256), (256, 384)]
 LOG = []
 HOOK = []
-LAYER = "s g0 q0 g1 f0 q1 a0 f1 a1 t0 t1"
-ENG = dict(g0="va", g1="va", f0="v", f1="v", t0="a", t1="a", kk="a")
+LAYER = "s g0 q0 g1 q1 f0 g2 a0 f1 q2 a1 f2 a2 t0 t1"
+CF = [(0, 128), (128, 256), (256, 384)]
+ENG = dict(g0="va", g1="va", g2="va", f0="v", f1="v", f2="v", t0="a", t1="a", t2="a", kk="a")
 AFTER = "arrive stays base signs less"
 NSC = 1
 SPARE = 300
 HI = 112
-TAIL = [(0, 16), (16, 24)]
+TAIL = [(0, 8), (8, 24)]
 X4, U8, U16, BF, F32 = "float8_e4m3fn_x4", "uint8", "uint16", "bfloat16", "float32"
 
 
@@ -41,10 +59,10 @@ def _sb(n, d):
 SCRATCH = {
     "ps": ("psum", [128, 4096], F32),
     "xs": _sb(960, BF), "us": _sb(512, BF), "vs": _sb(512, BF),
-    "qx": _sb(240, X4), "sx": _sb(240, U8), "qu": _sb(128, X4), "su": _sb(128, U8),
+    "qx": _sb(512, X4), "sx": _sb(512, U8), "qu": _sb(128, X4), "su": _sb(128, U8),
     "qu2": _sb(128, X4), "su2": _sb(128, U8), "qv": _sb(128, X4), "sv": _sb(128, U8),
     "qw": _sb(512, X4), "sw": _sb(512, U8), "qe": _sb(512, X4), "se": _sb(512, U8),
-    "ones": _sb(512, BF), "et": _sb(2048, BF), "tb0": _sb(2048, BF), "tb1": _sb(2048, BF),
+    "one": _sb(256, BF), "ones": _sb(512, BF), "et": _sb(2048, BF), "tb0": _sb(2048, BF), "tb1": _sb(2048, BF),
     "fi": _sb(1536, BF), "f64": _sb(1536, BF), "ti": _sb(1536, BF), "df": _sb(2048, BF),
     "qf": _sb(384, X4), "sf": _sb(384, U8),
     "yo": _sb(384, F32), "olr": _sb(384, F32),
@@ -59,7 +77,7 @@ SCRATCH = {
     "kt0": _sb(512, F32), "kt1": _sb(512, F32), "krow": _sb(240, F32), "kx": _sb(240, F32),
     "strow": _sb(240, BF), "spb": _sb(256, BF), "spe": _sb(240, BF), "sxx": _sb(80, F32),
     "e1": _sb(384, BF), "e2": _sb(384, BF), "zz": _sb(400, BF),
-    "mso": _sb(120 * ND, BF), "mcp": _sb(240 * ND, BF), "sf2": _sb(241 * NM, F32),
+    "mso": _sb(120 * ND, BF), "mcp": _sb(240 * ND, BF), "sf2": _sb(240 * NM, BF),
     "vv": _sb(480, BF), "isa": _sb(240, BF), "aa": _sb(240, BF), "sq": _sb(256, BF),
     "qrow": _sb(240, BF), "suf": _sb(256, BF), "tbl": _sb(448, F32),
     "srw": _sb(624, BF), "srx": _sb(240, BF),
@@ -74,10 +92,9 @@ for _t in range(R):
         SCRATCH[_q + str(_t)] = _sb(384, X4)
         SCRATCH[_s + str(_t)] = _sb(384, U8)
 
-POOLS = {"v": 48, "a": 32, "p": 12, "g": 12}
-LOADS = ["x", "u", "v", "wc", "ws"]
-SEMAPHORES = ([e + str(i) for e in POOLS for i in range(POOLS[e])] + ["ld_" + n for n in LOADS]
-              + [n + str(t) for n in ("ai", "ab", "al") for t in range(R)] + ["au", "sent", "out_s", "out_a"])
+LOADS = ["x0", "x1", "u", "v", "wc", "ws"]
+SEMAPHORES = (["done_" + e for e in "vapg"] + ["ld_" + n for n in LOADS]
+              + [n + str(t) for n in ("ai", "ab0", "ab1", "al") for t in range(R)] + ["au", "sent", "out_s", "out_a"])
 
 
 def V(name, a, b, step=1):
@@ -102,8 +119,10 @@ def rank_program(g, core, T, topo):
     prog = []
     ops = {}
     known = {e: 0 for e in Q}
-    count = {e: [] for e in POOLS}
+    count = {e: 0 for e in Q}
+    mine = {e: 0 for e in Q}
     acc = {}
+    slow = []
     waited = {}
 
     def clash(a, b):
@@ -127,12 +146,15 @@ def rank_program(g, core, T, topo):
 
     def note(ways, reads, writes, kind="", lag=0, more=()):
         deps = set(more)
-        use = [(v, v[0] == "ps") for v in flat(reads)] + [(v, True) for v in flat(writes)]
+        use = [(v, False) for v in flat(reads)] + [(v, True) for v in flat(writes)]
         for v, w in use:
             for (u, uw, i) in acc.get(v[0], []):
-                if (w or uw) and clash(u, v):
+                other = v[0] == "ps" and len(set(ways) | set(prog[i][0])) > 1
+                if (w or uw or other) and clash(u, v):
                     deps.add(i)
         i = len(prog)
+        by_list = any(w is False and SCRATCH[v[0]][2] == U16 for v, w in use)
+        slow.append(1.0 if kind or "p" in ways else SLOW * (1.15 if by_list else 1.0))
         prog.append(({e: (c, int(n)) for e, (c, n) in ways.items()}, deps, kind, lag))
         for v, w in use:
             lst = acc.setdefault(v[0], [])
@@ -153,7 +175,7 @@ def rank_program(g, core, T, topo):
             return 60 + GATHER * n
         if rate is None:
             rate = 0.5 if e == "v" and all(SCRATCH[v[0]][2] in (BF, U16) for v in vs if size(v) > 1) else 1.0
-        return max(64, rate * n)
+        return max(64 if e == "v" else AMIN, rate * n) + (VFIX if e == "v" else 0)
 
     def run(e, reads, writes, call, cost):
         note({e: (call, cost)}, reads, writes)
@@ -173,7 +195,7 @@ def rank_program(g, core, T, topo):
         behind = [[(u, lag[i] + WAKE) for u in users[i]] for i in range(n)]
 
         def lay(seq, links, first, lean):
-            starts, ends = {e: [] for e in list(Q) + ["-"]}, {e: [] for e in list(Q) + ["-"]}
+            starts, ends = {e: [] for e in "vapgsd-"}, {e: [] for e in "vapgsd-"}
             st, en, on = [0] * n, [0] * n, [None] * n
             for i in seq:
                 at = first[i]
@@ -203,7 +225,15 @@ def rank_program(g, core, T, topo):
             st, en, on = lay(seq, ahead, [0] * n, lean)
             st, en, on = lay(sorted(range(n), key=lambda i: (-en[i] - lag[i], -i)), behind, lag, lean)
             st, en, on = lay(sorted(range(n), key=lambda i: (-en[i], i)), ahead, [0] * n, lean)
-            return max(en[i] + lag[i] for i in range(n)), st, on, lean
+            free, e2 = {}, [0] * n
+            for i in sorted(range(n), key=lambda i: (st[i], i)):
+                at = free.get(on[i], 0)
+                for d, w in ahead[i]:
+                    if e2[d] + w > at:
+                        at = e2[d] + w
+                e2[i] = free[on[i]] = at + (en[i] - st[i]) * slow[i]
+            end = max(en[i] + lag[i] for i in range(n))
+            return (end + MIX * max(e2[i] + lag[i] for i in range(n))) / (1 + 1.3 * MIX), st, on, lean
 
         if not PLAN:
             now = best = close(list(range(n)), [SPARE] * n)
@@ -215,7 +245,8 @@ def rank_program(g, core, T, topo):
 
             for k in range(PASSES):
                 a, far, wide = unit() * now[0], (300, 1000, 2500)[k % 3], (2000, 5000, 10000)[k // 3 % 3]
-                at, lean = list(now[1]), list(now[3])
+                a -= wide / 2
+                at, lean = list(now[1]), [-10 ** 6 if e == "v" else 10 ** 6 for e in now[2]]
                 for i in range(n):
                     if a <= at[i] < a + wide:
                         at[i] += far * (unit() - 0.5)
@@ -225,7 +256,7 @@ def rank_program(g, core, T, topo):
                         if at[d] > at[i]:
                             at[i] = at[d]
                 new = close(sorted(range(n), key=lambda i: (at[i], i)), lean)
-                now = new if new[0] <= now[0] + SLACK else now
+                now = new if new[0] <= now[0] + SLACK * unit() else now
                 best = new if new[0] < best[0] else best
             LOG.append(best[0])
             PLAN.extend((i, best[2][i]) for i in sorted(range(n), key=lambda i: (best[1][i], i)))
@@ -241,19 +272,18 @@ def rank_program(g, core, T, topo):
         for i, e in order():
             place[i] = len(place)
             ways, deps, kind, lag = prog[i]
-            if e == "-":
-                ops[i] = (kind[0], kind[1], 0)
+            if e in "d-":
+                if kind[1]:
+                    ops[i] = (kind[0], kind[1], 0)
                 continue
-            if not kind:
-                n, k = len(count[e]), POOLS[e]
-                deps = set(deps) | set([count[e][n - k]] if n >= k else [])
             for d in sorted(deps, key=place.get, reverse=True):
                 if d in ops and not known[e] >> d & 1:
                     wait(e, d)
             if not kind:
-                ways[e][0]().then_inc(T.sem[e + str(n % k)], 1)
-                ops[i] = (e + str(n % k), n // k + 1, known[e])
-                count[e].append(i)
+                ways[e][0]().then_inc(T.sem["done_" + e], 1)
+                count[e] += 1
+                ops[i] = ("done_" + e, count[e], known[e] | mine[e])
+                mine[e] |= 1 << i
             else:
                 ways[e][0]()
                 if kind[1]:
@@ -306,7 +336,7 @@ def rank_program(g, core, T, topo):
         if accum is not None:
             kw["accum_out"] = ap(accum)
         return (lambda: g.scalar.activation(ap(out), ap(in_), func, **kw),
-                cycles("a", out, [in_]) + (24 if accum else 0))
+                cycles("a", out, [in_]) + (24 if accum else 0) + AFIX)
 
     def act(out, in_, func=AF.Copy, bias=None, scale=None, accum=None):
         note({"a": act_way(out, in_, func, bias, scale, accum)}, [in_, bias, scale], [out, accum])
@@ -324,33 +354,42 @@ def rank_program(g, core, T, topo):
         o = V("ps", 512 * bank, 512 * bank + b - a)
         w, wsc, x, xsc = V(wq, wa, wa + 128), V(ws, wa, wa + 128), V(xq, a, b), V(xs, a, b)
         run("p", [w, wsc, x, xsc], [o],
-            lambda: g.tensor.matmul_mx(ap(o), ap(w), ap(wsc), ap(x), ap(xsc), True, True), 1.2 * (b - a + 16))
+            lambda: g.tensor.matmul_mx(ap(o), ap(w), ap(wsc), ap(x), ap(xsc), True, True), PE * (b - a + 16))
 
     def iota(out, pattern, base=0, cm=0):
         run("g", [], [out], lambda: g.iota(ap(out), pattern, base, cm, allow_small_or_imprecise_dtypes=True),
             150 + 2 * size(out))
 
     def const(out, c=0):
-        iota(out, [[0, len(range(out[1], out[2], out[3]))]], c)
+        n, one = size(out), V("one", 0, size(out))
+        if n < LONG:
+            return iota(out, [[0, n]], c)
+        note({"a": act_way(out, one, scale=float(c)),
+              "g": (lambda: g.iota(ap(out), [[0, n]], c, 0, allow_small_or_imprecise_dtypes=True), 150 + 2 * n)},
+             [one], [out])
 
-    def load(e, name, out, dst, src, lag, more=()):
-        return note({e: (lambda: Q[e].dma_start(dst, src).then_inc(T.sem["ld_" + name], 16), 50)}, [], [out],
-                    ("ld_" + name, 16), lag, more)
+    def moved(i, row, writes=(), kind=("", 0)):
+        return note({"d": (None, BYTE * row)}, [], writes, kind, 0, [i])
+
+    def load(e, name, out, dst, src, row, more=()):
+        i = note({e: (lambda: Q[e].dma_start(dst, src).then_inc(T.sem["ld_" + name], 16),
+                      HOLD if e == "a" else ISSUE)}, [], [], ("", 0), LD - (HOLD - ISSUE if e == "a" else 0), more)
+        return moved(i, row, [out], ("ld_" + name, 16))
 
     total = {"sent": 0, "out_s": 0, "out_a": 0}
 
-    def store(e, dst, src, reads, lag=DMA):
-        note({e: (lambda: Q[e].dma_start(dst, src).then_inc(T.sem["out_" + e], 16), 50)}, reads, [], ("out", 0), lag)
+    def store(e, dst, src, reads, row):
+        moved(note({e: (lambda: Q[e].dma_start(dst, src).then_inc(T.sem["out_" + e], 16), ISSUE)}, reads, [],
+                   ("", 0), LD), row)
         total["out_" + e] += 16
 
     sends = {}
 
-    def send(dst, src, reads, sem, behind=(), more=0):
+    def send(dst, src, reads, sem, row):
         i = note({"g": (lambda: g.remote_dma(dst, src, T.sem[sem], T.sem.sent, pid, rid, mask),
-                        330 if sends else 330 + DMA)}, reads, [], ("sent", 0), DMA + more, behind)
-        sends.setdefault(sem, []).append(i)
+                        CALL if sends else FIRST)}, reads, [], ("", 0), DMA)
+        sends.setdefault(sem, []).append(moved(i, row))
         total["sent"] += neng
-        return i
 
     def landed(writes, sem):
         note({"-": (None, 0)}, [], writes, (sem, len(sends[sem]) * neng), -WAKE, sends[sem])
@@ -386,19 +425,21 @@ def rank_program(g, core, T, topo):
         tr(V(via, 256, 256 + min(n + 32, 256)), V(row, o, o + min(n + 32, 256)))
         ts(out, IND(V(via, 0, 512), ul("tw", 0, 1)), more, OP.add)
 
-    load("a", "u", V("us", 0, 512), T.us[:], T.u[:], 2700)
-    x_in = load("s", "x", V("xs", 0, 960), T.xs[:], T.x[:], 3500)
-    load("s", "wc", V("qw", 0, 512), T.qw[:].bitcast(dt.uint8), T.wc[:], 3500, [x_in])
-    load("s", "ws", V("sw", 0, 512), T.sw[:], T.ws[:], 3500, [x_in])
-    load("s", "v", V("vs", 0, 512), T.vs[:], T.v[:], 4000, [x_in])
+    load("a", "u", V("us", 0, 512), T.us[:], T.u[:], 1024)
+    for c, (a, z) in enumerate(XP):
+        x_in = load("s", "x%d" % c, V("xs", 4 * a, 4 * z), T.xs[:, 4 * a:4 * z], T.x[:, 4 * a:4 * z], 8 * (z - a))
+    load("s", "wc", V("qw", 0, 512), T.qw[:].bitcast(dt.uint8), T.wc[:], 2048, [x_in])
+    load("s", "ws", V("sw", 0, 512), T.sw[:], T.ws[:], 512, [x_in])
+    load("s", "v", V("vs", 0, 512), T.vs[:], T.v[:], 1024, [x_in])
 
     scol = sm("s", 0, 1)
     run("g", [], [V("pint", 0, 1)], lambda: g.iota(T.pint[:, 0:1], [[0, 1]], 0, 1), 150)
     iota(sm("c", 0, 32), [[1, 32]])
     iota(sm("k2", 0, 56), [[1, 2], [16, 28]])
+    fill(V("one", 0, 256), 1.0)
     fill(V("rs", 0, 384), 1.0)
-    fill(sm("beta", 0, 16), -1.0)
-    fill(sm("ra", 0, 16), 0.0)
+    iota(V("ones", 0, 512), [[0, 512]], 1)
+    const(sm("ra", 0, 16))
     ts(V("pint", 1, 2), V("pint", 0, 1), 15, OP.bitwise_and)
     fill(V("rs", 0, 384, 16), 0.0)
     ts(V("pint", 2, 3), V("pint", 0, 1), 4, OP.logical_shift_right)
@@ -409,7 +450,7 @@ def rank_program(g, core, T, topo):
     ts(ul("lw", 0, 16), sm("c", 0, 16), 16.0, OP.mult, 15.0, OP.add)
     cp(ul("c", 0, 16), sm("c", 0, 16))
     ts(V("pint", 2, 3), V("pint", 2, 3), 1, OP.bitwise_and)
-    ts(sm("beta", 0, NA), sm("c", 0, NA), 16.0, OP.mult, -1.0, OP.add)
+    iota(V("sa", C, (C + 1) * NA, C + 1), [[16, NA]])
     ts(V("dm", 0, 384), V("t16", 0, 384), scol, OP.is_equal)
     ts(V("nd", 0, C), V("t16", 0, C), scol, OP.not_equal)
     ts(V("mx", 0, 384), V("t16", 0, 384), scol, OP.is_le, BIG, OP.mult)
@@ -437,9 +478,10 @@ def rank_program(g, core, T, topo):
         iota(V("xrow", 208, 232), [[5, 6], [0, 4]], 4)
         const(V("xrow", 232, 240), 31)
         iota(sm("r", 32, 34), [[1, 2]], int(MAGIC) + C)
-        const(V("xr", 0, 256))
-        const(V("tc", 0, 512))
-        iota(V("idb", 0, S), [[1, S]], OWN - 256)
+        const(V("xr", 0, 16))
+        const(V("xr", 208, 224))
+        const(V("tc", 192, 256))
+        lin(V("idb", 0, S), V("iota", 0, S), bias=OWN - 256.0, on="a")
         const(V("step", 0, L))
         const(V("step", L, C), 1)
         const(V("zer", 0, C))
@@ -458,32 +500,31 @@ def rank_program(g, core, T, topo):
         const(V("suf", C, C + 1), C)
         const(V("suf", C + 1, 256))
         const(V("zz", S, 400), C)
-        const(V("ones", 0, 512), 1)
         for b in range(4):
             o = V("et", 512 * b, 512 * b + 512)
             run("g", [V("ones", 0, 512)], [o],
                 lambda o=o, b=b: g.affine_select(ap(o), T.ones[:], [[-1, 512]], OP.is_equal, 0.0, b, 4), 1200)
         ts(sm("yf", 0, 56), sm("k2", 0, 56), scol, OP.add, float(C) / S, OP.mult)
-        ts(sm("k240"), sm("k2"), scol, OP.add, float(C), OP.add)
+        lin(sm("k240m"), sm("k2"), bias=scol, on="a")
+        lin(sm("k240m"), sm("k240m"), bias=MAGIC + C, on="a")
         ts(sm("yf", 0, 56), sm("yf", 0, 56), UP, OP.add, MAGIC, OP.add)
-        lin(sm("k240m"), sm("k240"), bias=MAGIC)
         ts(ul("qlo", 0, 24), sm("yf"), -MAGIC, OP.add)
-        for a in (0, C):
-            lin(V("vv", a, a + C), V("rs", 0, C), 0.0, -256.0)
+        for a, z in ((0, C), (C, 352)):
+            const(V("vv", a, z), -256)
         for b in range(4):
-            lin(V("tbl", 2 * HI + b, 4 * HI, 4), sm("yf", 0, 56), bias=-MAGIC)
-        lin(sm("r", 0, 24), sm("yf", 0, 24))
-        lin(sm("o16", 0, 2), sm("c", 0, 2), bias=scol)
-        lin(sm("o16", 0, 2), sm("o16", 0, 2), 1.0 / 16)
-        lin(sm("o64", 0, 56), sm("m4", 0, 56), bias=scol)
-        lin(sm("o64", 0, 56), sm("o64", 0, 56), 1.0 / 64)
+            lin(V("tbl", 2 * HI + b, 4 * HI, 4), sm("yf", 0, 56), bias=-MAGIC, on="a")
+        lin(sm("r", 0, 24), sm("yf", 0, 24), on="a")
+        lin(sm("o16", 0, 2), sm("c", 0, 2), bias=scol, on="a")
+        lin(sm("o16", 0, 2), sm("o16", 0, 2), 1.0 / 16, on="a")
+        lin(sm("o64", 0, 56), sm("m4", 0, 56), bias=scol, on="a")
+        lin(sm("o64", 0, 56), sm("o64", 0, 56), 1.0 / 64, on="a")
         turned(ul("xc", 0, 16), "xrow", 224, 0.0, "tc")
 
     def leaf_lists():
         lin(V("xr", 16, 208), IND(sm("r", 0, 64), ul("xc", 0, 12)), bias=-MAGIC)
         turned(ul("xl", 0, 16), "xr", 192, 0.0, "tc")
 
-    def ranking(K):
+    def ranking(K, cut):
         def k(a, b):
             return V(K[0], K[1] + a, K[1] + b)
 
@@ -493,16 +534,17 @@ def rank_program(g, core, T, topo):
         W = C + 1
         tt(V("eq", 0, C), IND(V("wf", 0, C), ul("lw", 0, 15)), k(0, C), OP.is_equal)
         scan(V("ex", 0, C, -1), V("nd", 0, C, -1), V("eq", 0, C, -1), 0.0, OP.mult, OP.add)
-        tt(sm("eb", 0, 15), V("ex", 0, C, 16), sm("beta", 0, 15), OP.add)
         for j in range(NA - 1, -1, -1):
-            act(V("sa", W * j, W * j + C), k(0, C), AF.Sign, bias=w(j), scale=-1.0)
+            for a, z in ((0, cut), (cut, C)) if cut else ((0, C),):
+                act(V("sa", W * j + a, W * j + z), k(a, z), AF.Sign, bias=w(j), scale=-1.0)
         for j in range(NA - 1, 0, -1):
             act(V("sa", W * j, W * j + 16 * j), V("sa", W * j, W * j + 16 * j), AF.Relu, scale=-1.0,
                 accum=sm("ra", j, j + 1))
-        tt(V("sa", C, W * NA, W), sm("eb", 0, NA), sm("ra", 0, NA), OP.subtract)
-        for j in range(NA):
-            o = W * j
-            act(V("sa", o + 16 * j, o + W), V("sa", o + 16 * j, o + W), AF.Relu, accum=sm("rb", j, j + 1))
+        for j in range(NA - 1, -1, -1):
+            o, z = W * j + 16 * j, W * j + W
+            act(V("sa", o, z), V("sa", o, z), AF.Relu, accum=sm("rb", j, j + 1))
+        tt(sm("eb", 0, NA), V("ex", 0, 16 * NA, 16), sm("ra", 0, NA), OP.subtract)
+        tt(sm("rb", 0, NA), sm("rb", 0, NA), sm("eb", 0, NA), OP.add)
         for j in range(NA, 15):
             o = C * (j - NA)
             ts(V("cmp", o, o + 16 * j), k(0, 16 * j), w(j), OP.is_le)
@@ -510,9 +552,9 @@ def rank_program(g, core, T, topo):
         for j in range(NA, 15):
             o = C * (j - NA)
             scan(V("so", o // 2, o // 2 + 120), V("cmp", o, o + 120), V("cmp", o + 120, o + C),
-                 sm("eb", j, j + 1), OP.add, OP.add)
-        cp(ul("rk", NA, 15), V("so", 119, 120 * (15 - NA), 120))
-        cp(ul("rk", 0, NA), sm("rb", 0, NA))
+                 V("ex", 16 * j, 16 * j + 1), OP.add, OP.add)
+        ts(ul("rk", NA, 15), V("so", 119, 120 * (15 - NA), 120), -1.0, OP.add)
+        ts(ul("rk", 0, NA), sm("rb", 0, NA), -1.0, OP.add)
         return [(0, NA, sm("rb", 0, NA)), (NA, 15, V("so", 119, 120 * (15 - NA), 120))]
 
     def parts(e, t, out, b, top, lst, a, z):
@@ -522,17 +564,18 @@ def rank_program(g, core, T, topo):
     run("v", [V("qu", 0, 128), ul("c16", 0, 8)], [V("qu2", 0, 128)], lambda: g.vector.tensor_copy(
         T.qu2[:, 0:128].bitcast(dt.uint32), T.qu[:, 0:128].bitcast(dt.uint32).indirect(ap(ul("c16", 0, 8)))), 260)
     act(V("su2", 0, 128), IND(V("su", 0, 128), ul("c16", 0, 8)))
-    send(T.qup[:].bitcast(dt.uint8), T.qu2[:].bitcast(dt.uint8), [V("qu2", 0, 128)], "au")
-    send(T.sup[:], T.su2[:], [V("su2", 0, 128)], "au")
+    send(T.qup[:].bitcast(dt.uint8), T.qu2[:].bitcast(dt.uint8), [V("qu2", 0, 128)], "au", 512)
+    send(T.sup[:], T.su2[:], [V("su2", 0, 128)], "au", 128)
     landed([V("qup", 0, 128), V("sup", 0, 128)], "au")
-    quant("qx", "sx", 0, C, V("xs", 0, 960))
-    mm(0, "qu2", "su2", 0, "qx", "sx", 0, C)
-    mm(1, "qu2", "su2", 0, "qx", "sx", 0, C)
-    act(V("pp", OWN, OWN + C), PS(1, 0, C))
-    for a, z in HALVES:
-        tt(V("wm", 16 * a, 16 * z), PS(0, 16 * a, 16 * z), V("dm", 16 * a, 16 * z), OP.mult)
-        segsum(V("wf", 16 * a, 16 * z), V("wm", 16 * a, 16 * z), 16 * (z - a))
-    ranking(V("pp", OWN, OWN + C))
+    for c, (a, z) in enumerate(XP):
+        o, n = min(a, C - 128), max(z - a, 128)
+        quant("qx", "sx", 256 * c, 256 * c + n, V("xs", 4 * o, 4 * (o + n)))
+        mm(2 * c, "qu2", "su2", 0, "qx", "sx", 256 * c, 256 * c + n)
+        mm(2 * c + 1, "qu2", "su2", 0, "qx", "sx", 256 * c, 256 * c + n)
+        tt(V("wm", a, z), PS(2 * c, a - o, z - o), V("dm", a, z), OP.mult)
+        act(V("pp", OWN + a, OWN + z), PS(2 * c + 1, a - o, z - o))
+        segsum(V("wf", a, z), V("wm", a, z), z - a)
+    ranking(V("pp", OWN, OWN + C), 128 * CUT[0])
     constants()
     cp(IND(V("inv", 16, 16 + C), ul("rk", 0, 15)), V("iota", 0, C))
     turned(ul("to", 0, 16), "inv", 256, float(OWN), "ta")
@@ -545,37 +588,39 @@ def rank_program(g, core, T, topo):
         top = OWN + C if t < 2 else 512
         kt, ktn = "kt%d" % (t % 2), "kt%d" % ((t + 1) % 2)
         ch = [(0, cw), (cw, 256 if first else S)]
+        cf = ch if first else CF
         q_t, s_t, IDS = "qt%d" % t, "st%d" % t, V("idl%d" % t, 0, 15)
 
         def gather(c):
             for b in range(4):
-                parts(ENG["g%d" % c], t, "fi", b, top, ul("to", ch[c][0] // 16, ch[c][1] // 16), *ch[c])
+                parts(ENG["g%d" % c], t, "fi", b, top, ul("to", cf[c][0] // 16, cf[c][1] // 16), *cf[c])
 
         def qf(c):
-            a, z = ch[c]
+            a, z = cf[c]
             quant("qf", "sf", a, z, V("fi", 4 * a, 4 * z))
             for b in range(4):
-                mm(4 * c + b, "qw", "sw", 128 * b, "qf", "sf", a, z)
+                mm(4 * (c % 2) + b, "qw", "sw", 128 * b, "qf", "sf", a, z)
 
         def f64(c):
-            a, z = ch[c]
+            a, z = cf[c]
             lin(V("f64", 4 * a, 4 * z), V("fi", 4 * a, 4 * z), 64.0, on=ENG["f%d" % c])
 
         def add(c):
-            a, z = ch[c]
+            a, z = cf[c]
             for b in range(4):
-                tt(TB(t + 1, b, OWN + a, OWN + z), PS(4 * c + b, 0, z - a), V("f64", 4 * a + b, 4 * z, 4), OP.add)
+                tt(TB(t + 1, b, OWN + a, OWN + z), PS(4 * (c % 2) + b, 0, z - a), V("f64", 4 * a + b, 4 * z, 4), OP.add)
                 lin(V("ti", 4 * a + b, 4 * z, 4), TB(t + 1, b, OWN + a, OWN + z), 0.015625, on=ENG["t%d" % c])
 
         def qt(c):
             a, z = ch[c]
+            k = 4 * c if len(cf) == 2 else 4 + c
             quant(q_t, s_t, a, z, V("ti", 4 * a, 4 * z))
-            mm(4 * c, "qu2", "su2", 0, q_t, s_t, a, z)
+            mm(k, "qu2", "su2", 0, q_t, s_t, a, z)
             if first:
-                mm(4 * c + 1, "qu2", "su2", 0, q_t, s_t, a, z)
+                mm(k + 1, "qu2", "su2", 0, q_t, s_t, a, z)
                 n = min(z, C) - a
-                tt(V("wm", a, a + n), PS(4 * c, 0, n), V("dm", 0, n), OP.mult)
-            lin(V("pp", OWN + a, OWN + z), PS(4 * c + first, 0, z - a))
+                tt(V("wm", a, a + n), PS(k, 0, n), V("dm", 0, n), OP.mult)
+            lin(V("pp", OWN + a, OWN + z), PS(k + first, 0, z - a))
 
         def held(c):
             if not first:
@@ -584,7 +629,7 @@ def rank_program(g, core, T, topo):
                     cp(IND(V("srw", 0, 624), ul("d2", a, z)), V("idb", 16 * a, 16 * z))
                 pick(V("srx", 0, C), V("srw", 0, C), C)
                 ts(IDS, V("srx", 15, C, 16), 256.0, OP.add)
-                send(T["idr%d" % t][:, 0:15], ap(IDS), [IDS], "ai%d" % t)
+                send(T["idr%d" % t][:, 0:15], ap(IDS), [IDS], "ai%d" % t, 100)
 
         def keys():
             if first:
@@ -599,7 +644,8 @@ def rank_program(g, core, T, topo):
             keys()
         steps = {"g": gather, "q": qf, "f": f64, "a": add, "t": qt, "s": held}
         for s in LAYER.split():
-            steps[s[0]](int(s[1:] or 0))
+            if int(s[1:] or 0) < len(cf):
+                steps[s[0]](int(s[1:] or 0))
         if first:
             K, ids = V("pp", OWN, OWN + C), V("idb", 0, C)
         else:
@@ -612,11 +658,12 @@ def rank_program(g, core, T, topo):
             segsum(V("wf", 16 * a, 16 * z), V("wm", 16 * a, 16 * z), 16 * (z - a))
 
         n, ql, sl, lo, ll = ch[1][1], "ql%d" % t, "sl%d" % t, "lo%d" % t, "ll%d" % t
-        for a, z in (ch if SPLIT else [(0, n)]):
-            send(T[ql][:, a:z].bitcast(dt.uint8), T[q_t][:, a:z].bitcast(dt.uint8), [V(q_t, a, z)], "ab%d" % t,
-                 more=4 * (z - a))
-            send(T[sl][:, a:z], T[s_t][:, a:z], [V(s_t, a, z)], "ab%d" % t, more=4 * (z - a))
-        rk = ranking(K)
+        for c, (a, z) in enumerate(ch):
+            send(T[ql][:, a:z].bitcast(dt.uint8), T[q_t][:, a:z].bitcast(dt.uint8), [V(q_t, a, z)], "ab%d%d" % (c, t),
+                 4 * (z - a))
+            send(T[sl][:, a:z], T[s_t][:, a:z], [V(s_t, a, z)], "ab%d%d" % (c, t), z - a)
+        cut = 128 if first else 96
+        rk = ranking(K, cut * CUT[1])
         if not first:
             keys()
         leaf_lists()
@@ -627,12 +674,15 @@ def rank_program(g, core, T, topo):
             return V("kx", 16 * j + 15, 16 * j + 16)
 
         def arrive():
-            landed([V(ql, 0, n), V(sl, 0, n)], "ab%d" % t)
-            mm(6, "qup", "sup", 0, ql, sl, 0, n)
-            lin(V("pq", OWN, OWN + n), PS(6, 0, n))
+            for c, (a, z) in enumerate(ch):
+                landed([V(ql, a, z), V(sl, a, z)], "ab%d%d" % (c, t))
+                mm(6 + c, "qup", "sup", 0, ql, sl, a, z)
+                lin(V("pq", OWN + a, OWN + z), PS(6 + c, 0, z - a))
             if not first:
                 landed([V("idr%d" % t, 0, 16)], "ai%d" % t)
-                lin(V("prow", 0, C), IND(V("pq", 0, 512), V("idr%d" % t, 0, 15)))
+                for a, z in HP:
+                    lin(V("prow", 16 * a, 16 * z), IND(V("pq", 0, OWN + (cw if 16 * z + S - C <= cw else S)),
+                                                       V("idr%d" % t, a, z)))
 
         PR = V("pq", OWN, OWN + C) if first else V("prow", 0, C)
 
@@ -643,24 +693,25 @@ def rank_program(g, core, T, topo):
 
         def base():
             for a, z, v in rk:
-                lin(sm("gn", a, z), v, -2 * BIG, (2 * L - 1) * BIG)
-                lin(sm("gh", a, z), v, bias=C - OFF)
-            tt(sm("base", 0, 15), V("spe", 15, C, 16), sm("gn", 0, 15), OP.max)
-            tt(sm("base", 0, 15), sm("base", 0, 15), sm("gh", 0, 15), OP.min)
-            lin(V("sf2", C, W * NM, W), sm("base", 0, NM), bias=OFF)
-            lin(sm("b96", 0, 15), sm("base", 0, 15), bias=float(L))
-            tt(sm("cap96", 0, 15), sm("b96", 0, 15), sm("gh", 0, 15), OP.min)
-            lin(sm("cap96", 0, NM), sm("cap96", 0, NM), bias=OFF)
+                lin(sm("gn", a, z), v, -2 * BIG, (2 * L + 1) * BIG)
+                lin(sm("gh", a, z), v, bias=C - 1 - OFF)
+            tt(sm("gh", 0, 15), sm("gh", 0, 15), sm("gn", 0, 15), OP.min)
+            tt(sm("base", 0, 15), V("spe", 15, C, 16), sm("gh", 0, 15), OP.max)
+            lin(sm("b96", 0, 15), V("spe", 15, C, 16), bias=float(L))
+            tt(sm("cap96", 0, 15), sm("b96", 0, 15), sm("gh", 0, 15), OP.max)
 
         def signs():
             for j in range(NM):
-                act(V("sf2", W * j, W * j + C), PR, AF.Sign, bias=key(j), scale=-1.0)
+                for a, z in ((0, cut), (cut, C)) if CUT[2] else ((0, C),):
+                    act(V("sf2", C * j + a, C * j + z), V(PR[0], PR[1] + a, PR[1] + z), AF.Sign, bias=key(j), scale=-1.0)
             for j in range(NM):
-                act(V("sf2", W * j, W * j + W), V("sf2", W * j, W * j + W), AF.Relu, accum=sm("ta", j, j + 1))
+                act(V("sf2", C * j, C * j + C), V("sf2", C * j, C * j + C), AF.Relu, accum=sm("ta", j, j + 1))
+            tt(sm("ta", 0, NM), sm("ta", 0, NM), sm("base", 0, NM), OP.add)
 
         def less():
             for j in range(ND):
-                ts(V("mcp", C * j, C * j + C), PR, key(NM + j), OP.is_lt)
+                for a, z in ((0, cut), (cut, C)) if j < CUT[3] else ((0, C),):
+                    ts(V("mcp", C * j + a, C * j + z), V(PR[0], PR[1] + a, PR[1] + z), key(NM + j), OP.is_lt)
             for j in range(ND):
                 scan(V("mso", 120 * j, 120 * j + 120), V("mcp", C * j, C * j + 120), V("mcp", C * j + 120, C * j + C),
                      sm("base", NM + j, NM + j + 1), OP.add, OP.add)
@@ -670,11 +721,13 @@ def rank_program(g, core, T, topo):
             steps[s]()
         tt(sm("dd", 0, NM), sm("ta", 0, NM), sm("cap96", 0, NM), OP.min)
         tt(sm("dd", NM, 15), V("mso", 119, 120 * ND, 120), sm("cap96", NM, 15), OP.min)
-        cp(ul("dest", 0, NM), sm("dd", 0, NM))
-        ts(ul("dest", NM, 15), sm("dd", NM, 15), OFF, OP.add)
+        ts(ul("dest", 0, 15), sm("dd", 0, 15), OFF, OP.add)
 
         lin(V("qrow", 0, C), IND(V("iota", 0, 512), ul("dest", 0, 15)), on="a")
-        cp(IND(V("vv", 0, 480), ul("dest", 0, 8)), V(ids[0], 0, 128))
+        for a, z in VH:
+            cp(IND(V("vv", 0, 480), ul("dest", a, z)), V(ids[0], 16 * a, 16 * z))
+        turned(V(lo, 0, 16), "vv", L, 256.0, "ta", C - 16)
+        send(T[ll][:, 0:6], T[lo][:, 0:6], [V(lo, 0, 6)], "al%d" % t, 100)
         scan(V("suf", 0, C, -1), V("zer", 0, C), V("qrow", 0, C, -1), float(C), OP.add, OP.min)
         SUF = V("suf", 0, 256)
         lin(sm("xd", 0, 32), IND(SUF, ul("xl", 10, 12)), bias=float(Q1))
@@ -696,9 +749,6 @@ def rank_program(g, core, T, topo):
         run("v", [sm("w3", 0, 6)], [sm("f3", 0, 1)],
             lambda: g.vector.tensor_reduce(ap(sm("f3", 0, 1)), ap(sm("w3", 0, 6)), AxisListType.X, OP.max), 64)
         ts(ul("md", 0, 2), sm("mw", 15, 32, 16), sm("f3", 0, 1), OP.add)
-        cp(IND(V("vv", 0, 480), ul("dest", 8, 15)), V(ids[0], 128, C))
-        turned(V(lo, 0, 16), "vv", L, 256.0, "ta", C - 16)
-        send(T[ll][:, 0:6], T[lo][:, 0:6], [V(lo, 0, 6)], "al%d" % t)
         lin(V("zz", 0, S), IND(SUF, ul("qlo", 0, 24)), on="a")
         pick(V("e1", 0, S), V("zz", 0, S), S)
         pick(V("e2", 0, S), V("zz", 1, S + 1), S)
@@ -711,14 +761,15 @@ def rank_program(g, core, T, topo):
         lin(sm("y16", 0, 24), sm("cnt"), sm("o16", 0, 1), UP)
         lin(sm("y16", 28, 52), sm("cnt"), sm("o16", 1, 2), UP)
         tt(V("tbl", 1, 208, 4), sm("y16", 0, 52), sm("xa", 0, 52), OP.add)
-        act(V("isa", 0, C), V("vv", 0, C), AF.Relu, bias=-255.0, scale=-1.0)
+        note({"a": act_way(V("isa", 0, C), V("vv", 0, C), AF.Relu, -255.0, -1.0),
+              "v": ts_way(V("isa", 0, C), V("vv", 0, C), -255.5, OP.is_lt)}, [V("vv", 0, C)], [V("isa", 0, C)])
         scan(V("aa", 0, C), V("isa", 0, C), V("zer", 0, C), float(ARR - 257), OP.add, OP.add)
-        tt(V("sq", 0, C), V("vv", 0, C), V("aa", 0, C), OP.max)
+        scan(V("sq", 0, C, -1), V("aa", 0, C, -1), V("vv", 0, C, -1), BIG, OP.min, OP.max)
         ts(ul("qlo", 0, 32), IND(V("tbl", 0, 3 * HI), ul("md", 0, 2)), MAGIC, OP.add, -MAGIC, OP.add)
         lin(sm("r", 0, 32), IND(V("tbl", 0, 3 * HI), ul("md", 0, 2)), bias=MAGIC, on="a")
         lin(sm("rh", 0, 32), IND(V("tbl", HI, 4 * HI), ul("md", 0, 2)), bias=MAGIC, on="a")
         tt(sm("gap"), sm("rh"), sm("r"), OP.is_le)
-        lin(sm("gap"), sm("gap"), BIG)
+        tt(sm("gap"), sm("gap"), sm("k240m"), OP.mult)
         for a, z in TAIL:
             tt(V("wb", 16 * a, 16 * z), IND(V("sq", 0, 256), ul("qlo", a, z)), V("dm", 16 * a, 16 * z), OP.mult)
             segsum(V("wb2", 16 * a, 16 * z), V("wb", 16 * a, 16 * z), 16 * (z - a))
@@ -726,13 +777,11 @@ def rank_program(g, core, T, topo):
             ts(ul("to", a, z), sm("tw", a, z), 256.0, OP.add)
         if not last:
             tt(sm("d1"), sm("r"), sm("gap"), OP.max)
-            tt(sm("d1"), sm("d1"), sm("k240m"), OP.min)
             ts(ul("d2", 0, 24), sm("d1"), -MAGIC, OP.add)
 
         if first:
             quant("qe", "se", 0, 256, V("et", 0, 1024))
             quant("qe", "se", 256, 512, V("et", 1024, 2048))
-            const(V("srw", 0, 624))
             const(V("idmap", 0, ARR), -1)
             iota(V("idmap", ARR, OWN), [[1, L]], S)
             iota(V("idmap", OWN, 512), [[1, S]])
@@ -744,7 +793,7 @@ def rank_program(g, core, T, topo):
         for b in range(4):
             lin(TB(t + 1, b, ARR, OWN), IND(V("df", 512 * b, 512 * b + OWN + n), V(ll, 0, 6)))
         if not last:
-            const(V("vv", 0, C), -256)
+            iota(V("vv", 0, C), [[0, C]], -256)
             lin(V(kt, ARR, OWN), IND(V("pq", 0, OWN + n), V(ll, 0, 6)))
 
     for c, (a, z) in enumerate(OUTS):
@@ -753,12 +802,12 @@ def rank_program(g, core, T, topo):
         quant("qf", "sf", a, z, V("fi", 4 * a, 4 * z))
         mm(c, "qv", "sv", 0, "qf", "sf", a, z)
         lin(V("yo", a, z), PS(c, 0, z - a))
-        store("sa"[z == S], T.y[:, a:z], T.yo[:, a:z], [V("yo", a, z)], DMA + 4 * (z - a))
-        store("s", T.oc[:, 4 * a:4 * z], T.qf[:, a:z].bitcast(dt.uint8), [V("qf", a, z)], DMA + 4 * (z - a))
+        store("sa"[z == S], T.y[:, a:z], T.yo[:, a:z], [V("yo", a, z)], 4 * (z - a))
+        store("s", T.oc[:, 4 * a:4 * z], T.qf[:, a:z].bitcast(dt.uint8), [V("qf", a, z)], 4 * (z - a))
     lin(V("olr", 0, S), IND(V("idmap", 0, 512), ul("to", 0, 24)))
     for k in range(4):
-        store("s", T.osc[4 * k:4 * k + 4, :], T.sf[32 * k:32 * k + 4, :], [V("sf", 0, S)])
-    store("a", T.ol[:], T.olr[0:128:16, :], [V("olr", 0, S)])
+        store("s", T.osc[4 * k:4 * k + 4, :], T.sf[32 * k:32 * k + 4, :], [V("sf", 0, S)], 50)
+    store("a", T.ol[:], T.olr[0:128:16, :], [V("olr", 0, S)], 150)
 
     issue()
     lastval = {}

from concourse.mybir import dt, AluOpType, AxisListType, ActivationFunctionType

S, C, L, Q1, Q2, R = 384, 240, 96, 13, 46, 3
ARR, OWN = 32, 128
BIG = 2.0 ** 90
MAGIC = 12582912.0
UP = 0.4921875
OFF = 200.0
NA = 6
NM = 5
ND = 15 - NM
CW = 256
WAKE = 265
DMA = 2400
GATHER = 1.75
SCATTER = 4.4
PASSES = 1700
SEED = 4
VFIX = 2
LONG = 100
HOLD = 1750
AMIN = 64
CALL = 450
FIRST = 5500
ISSUE = 150
SLOW = 1.4
MIX = 0.4
LD = 1650
BYTE = 0.8
AFIX = 4
PE = 1.55
XP = [(0, 128), (128, 240)]
REST = []
CUT = [1, 1, 1, 5]
VH = [(0, 8), (8, 15)]
HALVES = [(0, 6), (6, 15)]
HP = [(0, 6), (6, 15)]
FLIP = 0.3
SLACK = 30
PLAN = []
OUTS = [(0, 256), (256, 384)]
LOG = []
HOOK = []
LAYER = "s g0 q0 g1 q1 f0 g2 a0 f1 q2 a1 f2 a2 t0 t1"
CF = [(0, 128), (128, 256), (256, 384)]
ENG = dict(g0="va", g1="va", g2="va", f0="v", f1="v", f2="v", t0="a", t1="a", t2="a", kk="a")
AFTER = "arrive stays base signs less"
NSC = 1
SPARE = 300
HI = 112
TAIL = [(0, 8), (8, 24)]
X4, U8, U16, BF, F32 = "float8_e4m3fn_x4", "uint8", "uint16", "bfloat16", "float32"


def _sb(n, d):
    return ("sbuf", [128, n], d)


SCRATCH = {
    "ps": ("psum", [128, 4096], F32),
    "xs": _sb(960, BF), "us": _sb(512, BF), "vs": _sb(512, BF),
    "qx": _sb(512, X4), "sx": _sb(512, U8), "qu": _sb(128, X4), "su": _sb(128, U8),
    "qu2": _sb(128, X4), "su2": _sb(128, U8), "qv": _sb(128, X4), "sv": _sb(128, U8),
    "qw": _sb(512, X4), "sw": _sb(512, U8), "qe": _sb(512, X4), "se": _sb(512, U8),
    "one": _sb(256, BF), "ones": _sb(512, BF), "et": _sb(2048, BF), "tb0": _sb(2048, BF), "tb1": _sb(2048, BF),
    "fi": _sb(1536, BF), "f64": _sb(1536, BF), "ti": _sb(1536, BF), "df": _sb(2048, BF),
    "qf": _sb(384, X4), "sf": _sb(384, U8),
    "yo": _sb(384, F32), "olr": _sb(384, F32),
    "iota": _sb(512, F32), "t16": _sb(384, BF), "dm": _sb(384, BF), "mx": _sb(384, BF), "rs": _sb(384, BF),
    "nd": _sb(240, BF), "step": _sb(240, BF), "idmap": _sb(512, F32), "xrow": _sb(256, BF), "xr": _sb(256, BF),
    "pint": _sb(8, "int32"), "zer": _sb(240, BF), "ta": _sb(512, BF), "tc": _sb(512, BF), "inv": _sb(288, BF),
    "pp": _sb(512, F32), "kk": _sb(256, F32), "wm": _sb(240, F32), "wf": _sb(240, F32),
    "pq": _sb(512, F32), "prow": _sb(240, F32), "qup": _sb(128, X4), "sup": _sb(128, U8),
    "cmp": _sb(240 * (15 - NA), BF), "so": _sb(120 * (15 - NA), BF), "sa": _sb(241 * NA, BF),
    "eq": _sb(240, BF), "ex": _sb(240, BF),
    "lrow": _sb(256, BF), "idb": _sb(384, BF), "wb": _sb(384, BF), "wb2": _sb(384, BF),
    "kt0": _sb(512, F32), "kt1": _sb(512, F32), "krow": _sb(240, F32), "kx": _sb(240, F32),
    "strow": _sb(240, BF), "spb": _sb(256, BF), "spe": _sb(240, BF), "sxx": _sb(80, F32),
    "e1": _sb(384, BF), "e2": _sb(384, BF), "zz": _sb(400, BF),
    "mso": _sb(120 * ND, BF), "mcp": _sb(240 * ND, BF), "sf2": _sb(240 * NM, BF),
    "vv": _sb(480, BF), "isa": _sb(240, BF), "aa": _sb(240, BF), "sq": _sb(256, BF),
    "qrow": _sb(240, BF), "suf": _sb(256, BF), "tbl": _sb(448, F32),
    "srw": _sb(624, BF), "srx": _sb(240, BF),
    "sm": _sb(64 * 48, F32), "u16": _sb(32 * 16, U16),
}
for _t in range(R):
    SCRATCH["idl%d" % _t] = _sb(16, U16)
    SCRATCH["idr%d" % _t] = _sb(16, U16)
    SCRATCH["lo%d" % _t] = _sb(16, U16)
    SCRATCH["ll%d" % _t] = _sb(16, U16)
    for _q, _s in (("qt", "st"), ("ql", "sl")):
        SCRATCH[_q + str(_t)] = _sb(384, X4)
        SCRATCH[_s + str(_t)] = _sb(384, U8)

LOADS = ["x0", "x1", "u", "v", "wc", "ws"]
SEMAPHORES = (["done_" + e for e in "vapg"] + ["ld_" + n for n in LOADS]
              + [n + str(t) for n in ("ai", "ab0", "ab1", "al") for t in range(R)] + ["au", "sent", "out_s", "out_a"])


def V(name, a, b, step=1):
    return (name, a, b, step)


def IND(win, off):
    return ("*", win, off)


def rank_program(g, core, T, topo):
    rank = T.rank_of(core)
    if rank is None:
        return
    nxt = T.cores[(rank + 1) % len(T.cores)]
    rid, pid = topo.addr(nxt)[0], topo.addr(nxt)[1]
    mask = topo.mask(core, nxt)
    neng = len(topo.engines(core, nxt))
    OP, AF = AluOpType, ActivationFunctionType
    Q = {"v": g.vector, "a": g.scalar, "p": g.tensor, "g": g, "s": g.sync}

    prog = []
    ops = {}
    known = {e: 0 for e in Q}
    count = {e: 0 for e in Q}
    mine = {e: 0 for e in Q}
    acc = {}
    slow = []
    waited = {}

    def clash(a, b):
        if a[0] == "ps":
            return a[1] // 512 <= (b[2] - 1) // 512 and b[1] // 512 <= (a[2] - 1) // 512
        if a[2] <= b[1] or b[2] <= a[1]:
            return False
        if a[3] > 1 and a[3] == b[3]:
            return (a[1] - b[1]) % a[3] == 0
        if a[3] > 1 >= b[3] or b[3] > 1 >= a[3]:
            s, r = (a, b) if a[3] > 1 else (b, a)
            return any(r[1] <= c < r[2] for c in range(s[1], s[2], s[3]))
        return True

    def flat(vs):
        o = []
        for v in vs:
            if isinstance(v, tuple):
                o += [v[1], v[2]] if v[0] == "*" else [v]
        return o

    def note(ways, reads, writes, kind="", lag=0, more=()):
        deps = set(more)
        use = [(v, False) for v in flat(reads)] + [(v, True) for v in flat(writes)]
        for v, w in use:
            for (u, uw, i) in acc.get(v[0], []):
                other = v[0] == "ps" and len(set(ways) | set(prog[i][0])) > 1
                if (w or uw or other) and clash(u, v):
                    deps.add(i)
        i = len(prog)
        by_list = any(w is False and SCRATCH[v[0]][2] == U16 for v, w in use)
        slow.append(1.0 if kind or "p" in ways else SLOW * (1.15 if by_list else 1.0))
        prog.append(({e: (c, int(n)) for e, (c, n) in ways.items()}, deps, kind, lag))
        for v, w in use:
            lst = acc.setdefault(v[0], [])
            if w and abs(v[3]) == 1:
                lst[:] = [r for r in lst if not (r[0][1] >= v[1] and r[0][2] <= v[2])]
            lst.append((v, w, i))
        return i

    def size(v):
        return 16 * size(v[2]) if v[0] == "*" else len(range(v[1], v[2], abs(v[3])))

    def cycles(e, out, ins, rate=None):
        vs = [v for v in [out] + ins if isinstance(v, tuple)]
        n = max(size(v) for v in vs)
        if out[0] == "*":
            return 60 + SCATTER * n
        if any(v[0] == "*" for v in vs):
            return 60 + GATHER * n
        if rate is None:
            rate = 0.5 if e == "v" and all(SCRATCH[v[0]][2] in (BF, U16) for v in vs if size(v) > 1) else 1.0
        return max(64 if e == "v" else AMIN, rate * n) + (VFIX if e == "v" else 0)

    def run(e, reads, writes, call, cost):
        note({e: (call, cost)}, reads, writes)

    def order():
        n = len(prog)
        if HOOK:
            return HOOK[0](prog)
        users = [[] for _ in range(n)]
        for i in range(n):
            for d in prog[i][1]:
                users[d].append(i)

        ways = [[(e, c) for e, (_, c) in p[0].items()] for p in prog]
        lag = [p[3] for p in prog]
        ahead = [[(d, lag[d] + WAKE) for d in p[1]] for p in prog]
        behind = [[(u, lag[i] + WAKE) for u in users[i]] for i in range(n)]

        def lay(seq, links, first, lean):
            starts, ends = {e: [] for e in "vapgsd-"}, {e: [] for e in "vapgsd-"}
            st, en, on = [0] * n, [0] * n, [None] * n
            for i in seq:
                at = first[i]
                for d, w in links[i]:
                    if en[d] + w > at:
                        at = en[d] + w
                best = None
                for e, c in ways[i]:
                    s, z = starts[e], ends[e]
                    k = m = len(z)
                    while k and z[k - 1] > at:
                        k -= 1
                    a = at
                    while k < m and s[k] < a + c:
                        a = z[k] if z[k] > a else a
                        k += 1
                    late = a + c + (lean[i] if e == "v" else 0)
                    if best is None or late < best[0]:
                        best = (late, a, a + c, e, k)
                late, st[i], en[i], e, k = best
                on[i] = e
                starts[e].insert(k, st[i])
                ends[e].insert(k, en[i])
            return st, en, on

        def close(seq, lean):
            st, en, on = lay(seq, ahead, [0] * n, lean)
            st, en, on = lay(sorted(range(n), key=lambda i: (-en[i] - lag[i], -i)), behind, lag, lean)
            st, en, on = lay(sorted(range(n), key=lambda i: (-en[i], i)), ahead, [0] * n, lean)
            free, e2 = {}, [0] * n
            for i in sorted(range(n), key=lambda i: (st[i], i)):
                at = free.get(on[i], 0)
                for d, w in ahead[i]:
                    if e2[d] + w > at:
                        at = e2[d] + w
                e2[i] = free[on[i]] = at + (en[i] - st[i]) * slow[i]
            end = max(en[i] + lag[i] for i in range(n))
            return (end + MIX * max(e2[i] + lag[i] for i in range(n))) / (1 + 1.3 * MIX), st, on, lean

        if not PLAN:
            now = best = close(list(range(n)), [SPARE] * n)
            x = [SEED]

            def unit():
                x[0] = (x[0] * 1103515245 + 12345) % 2 ** 31
                return x[0] / 2 ** 31

            for k in range(PASSES):
                a, far, wide = unit() * now[0], (300, 1000, 2500)[k % 3], (2000, 5000, 10000)[k // 3 % 3]
                a -= wide / 2
                at, lean = list(now[1]), [-10 ** 6 if e == "v" else 10 ** 6 for e in now[2]]
                for i in range(n):
                    if a <= at[i] < a + wide:
                        at[i] += far * (unit() - 0.5)
                        if len(ways[i]) > 1 and unit() < FLIP:
                            lean[i] = 1200 * unit() - 300
                    for d, w in ahead[i]:
                        if at[d] > at[i]:
                            at[i] = at[d]
                new = close(sorted(range(n), key=lambda i: (at[i], i)), lean)
                now = new if new[0] <= now[0] + SLACK * unit() else now
                best = new if new[0] < best[0] else best
            LOG.append(best[0])
            PLAN.extend((i, best[2][i]) for i in sorted(range(n), key=lambda i: (best[1][i], i)))
        return PLAN

    def wait(e, i):
        Q[e].wait_ge(T.sem[ops[i][0]], ops[i][1])
        waited[ops[i][0]] = max(waited.get(ops[i][0], 0), ops[i][1])
        known[e] |= ops[i][2] | (1 << i)

    def issue():
        place = {}
        for i, e in order():
            place[i] = len(place)
            ways, deps, kind, lag = prog[i]
            if e in "d-":
                if kind[1]:
                    ops[i] = (kind[0], kind[1], 0)
                continue
            for d in sorted(deps, key=place.get, reverse=True):
                if d in ops and not known[e] >> d & 1:
                    wait(e, d)
            if not kind:
                ways[e][0]().then_inc(T.sem["done_" + e], 1)
                count[e] += 1
                ops[i] = ("done_" + e, count[e], known[e] | mine[e])
                mine[e] |= 1 << i
            else:
                ways[e][0]()
                if kind[1]:
                    ops[i] = (kind[0], kind[1], known[e])

    def ap(v):
        if not isinstance(v, tuple):
            return v
        if v[0] == "*":
            return ap(v[1]).indirect(ap(v[2]))
        if v[3] == -1:
            return T[v[0]][:, v[2] - 1:(v[1] - 1 if v[1] else None):-1]
        return T[v[0]][:, v[1]:v[2]] if v[3] == 1 else T[v[0]][:, v[1]:v[2]:v[3]]

    def cp(out, in_):
        r, w = ([out[2]], [out[1]]) if out[0] == "*" else ([], [out])
        run("v", r + [in_], w, lambda: g.vector.tensor_copy(ap(out), ap(in_)), cycles("v", out, [in_]))

    def tt(out, a, b, op):
        run("v", [a, b], [out], lambda: g.vector.tensor_tensor(ap(out), ap(a), ap(b), op),
            cycles("v", out, [a, b], 1.0 if "ps" in (a[0], b[0]) else 2.0))

    def ts_way(out, a, s1, op0, s2=None, op1=None):
        more = (None, op0) if s2 is None else (ap(s2), op0, op1)
        return lambda: g.vector.tensor_scalar(ap(out), ap(a), ap(s1), *more), cycles("v", out, [a])

    def ts(out, a, s1, op0, s2=None, op1=None):
        note({"v": ts_way(out, a, s1, op0, s2, op1)}, [a, s1, s2], [out])

    def scan(out, d0, d1, init, op0, op1):
        run("v", [d0, d1, init], [out],
            lambda: g.vector.tensor_tensor_scan(ap(out), ap(d0), ap(d1), ap(init), op0, op1), cycles("v", out, [d0, d1]))

    def fill(out, c):
        run("v", [], [out], lambda: g.vector.memset(ap(out), c), cycles("v", out, []))

    def tr(out, in_):
        run("v", [in_], [out], lambda: g.vector.transpose(ap(out), ap(in_)), cycles("v", out, [in_]))

    def quant(q, s, a, b, in_):
        run("v", [in_], [V(q, a, b), V(s, a, b)],
            lambda: g.vector.quantize_mx(ap(V(q, a, b)), ap(V(s, a, b)), ap(in_)), 14 + (b - a))

    def act_way(out, in_, func=AF.Copy, bias=None, scale=None, accum=None):
        kw = {}
        if bias is not None:
            kw["bias"] = ap(bias)
        if scale is not None:
            kw["scale"] = ap(scale)
        if accum is not None:
            kw["accum_out"] = ap(accum)
        return (lambda: g.scalar.activation(ap(out), ap(in_), func, **kw),
                cycles("a", out, [in_]) + (24 if accum else 0) + AFIX)

    def act(out, in_, func=AF.Copy, bias=None, scale=None, accum=None):
        note({"a": act_way(out, in_, func, bias, scale, accum)}, [in_, bias, scale], [out, accum])

    def lin(out, in_, scale=1.0, bias=None, on="av"):
        ways = {}
        for e in on:
            if e == "a":
                ways[e] = act_way(out, in_, AF.Copy if bias is None else AF.Identity, bias, scale)
            else:
                ways[e] = ts_way(out, in_, scale, OP.mult, bias, None if bias is None else OP.add)
        note(ways, [in_, bias, scale], [out])

    def mm(bank, wq, ws, wa, xq, xs, a, b):
        o = V("ps", 512 * bank, 512 * bank + b - a)
        w, wsc, x, xsc = V(wq, wa, wa + 128), V(ws, wa, wa + 128), V(xq, a, b), V(xs, a, b)
        run("p", [w, wsc, x, xsc], [o],
            lambda: g.tensor.matmul_mx(ap(o), ap(w), ap(wsc), ap(x), ap(xsc), True, True), PE * (b - a + 16))

    def iota(out, pattern, base=0, cm=0):
        run("g", [], [out], lambda: g.iota(ap(out), pattern, base, cm, allow_small_or_imprecise_dtypes=True),
            150 + 2 * size(out))

    def const(out, c=0):
        n, one = size(out), V("one", 0, size(out))
        if n < LONG:
            return iota(out, [[0, n]], c)
        note({"a": act_way(out, one, scale=float(c)),
              "g": (lambda: g.iota(ap(out), [[0, n]], c, 0, allow_small_or_imprecise_dtypes=True), 150 + 2 * n)},
             [one], [out])

    def moved(i, row, writes=(), kind=("", 0)):
        return note({"d": (None, BYTE * row)}, [], writes, kind, 0, [i])

    def load(e, name, out, dst, src, row, more=()):
        i = note({e: (lambda: Q[e].dma_start(dst, src).then_inc(T.sem["ld_" + name], 16),
                      HOLD if e == "a" else ISSUE)}, [], [], ("", 0), LD - (HOLD - ISSUE if e == "a" else 0), more)
        return moved(i, row, [out], ("ld_" + name, 16))

    total = {"sent": 0, "out_s": 0, "out_a": 0}

    def store(e, dst, src, reads, row):
        moved(note({e: (lambda: Q[e].dma_start(dst, src).then_inc(T.sem["out_" + e], 16), ISSUE)}, reads, [],
                   ("", 0), LD), row)
        total["out_" + e] += 16

    sends = {}

    def send(dst, src, reads, sem, row):
        i = note({"g": (lambda: g.remote_dma(dst, src, T.sem[sem], T.sem.sent, pid, rid, mask),
                        CALL if sends else FIRST)}, reads, [], ("", 0), DMA)
        sends.setdefault(sem, []).append(moved(i, row))
        total["sent"] += neng

    def landed(writes, sem):
        note({"-": (None, 0)}, [], writes, (sem, len(sends[sem]) * neng), -WAKE, sends[sem])

    def PS(bank, a, b):
        return V("ps", 512 * bank + a, 512 * bank + b)

    def TB(t, b, a, e):
        return V("tb%d" % (t % 2), 512 * b + a, 512 * b + e)

    slots = {}

    def sm(name, a=0, b=24, step=1):
        o = 64 * slots.setdefault(name, len(slots))
        assert len(slots) <= 48
        return V("sm", o + a, o + b, step)

    lists = {}

    def ul(name, a, b):
        o = 32 * lists.setdefault(name, len(lists))
        assert len(lists) <= 16
        return V("u16", o + a, o + b)

    def pick(out, row, n):
        scan(out, V("mx", 0, n), row, 0.0, OP.add, OP.min)

    def segsum(out, row, n):
        scan(out, V("rs", 0, n), row, 0.0, OP.mult, OP.add)

    def turned(out, row, n, more, via, o=0):
        tr(V(via, 0, n), V(row, o + 16, o + 16 + n))
        tr(V(via, 256, 256 + min(n + 32, 256)), V(row, o, o + min(n + 32, 256)))
        ts(out, IND(V(via, 0, 512), ul("tw", 0, 1)), more, OP.add)

    load("a", "u", V("us", 0, 512), T.us[:], T.u[:], 1024)
    for c, (a, z) in enumerate(XP):
        x_in = load("s", "x%d" % c, V("xs", 4 * a, 4 * z), T.xs[:, 4 * a:4 * z], T.x[:, 4 * a:4 * z], 8 * (z - a))
    load("s", "wc", V("qw", 0, 512), T.qw[:].bitcast(dt.uint8), T.wc[:], 2048, [x_in])
    load("s", "ws", V("sw", 0, 512), T.sw[:], T.ws[:], 512, [x_in])
    load("s", "v", V("vs", 0, 512), T.vs[:], T.v[:], 1024, [x_in])

    scol = sm("s", 0, 1)
    run("g", [], [V("pint", 0, 1)], lambda: g.iota(T.pint[:, 0:1], [[0, 1]], 0, 1), 150)
    iota(sm("c", 0, 32), [[1, 32]])
    iota(sm("k2", 0, 56), [[1, 2], [16, 28]])
    fill(V("one", 0, 256), 1.0)
    fill(V("rs", 0, 384), 1.0)
    iota(V("ones", 0, 512), [[0, 512]], 1)
    const(sm("ra", 0, 16))
    ts(V("pint", 1, 2), V("pint", 0, 1), 15, OP.bitwise_and)
    fill(V("rs", 0, 384, 16), 0.0)
    ts(V("pint", 2, 3), V("pint", 0, 1), 4, OP.logical_shift_right)
    ts(ul("c16", 0, 8), sm("c", 0, 8), 16.0, OP.mult)
    segsum(V("t16", 0, 384), V("rs", 0, 384), 384)
    cp(scol, V("pint", 1, 2))
    tt(V("pint", 2, 3), V("pint", 2, 3), V("pint", 0, 1), OP.add)
    ts(ul("lw", 0, 16), sm("c", 0, 16), 16.0, OP.mult, 15.0, OP.add)
    cp(ul("c", 0, 16), sm("c", 0, 16))
    ts(V("pint", 2, 3), V("pint", 2, 3), 1, OP.bitwise_and)
    iota(V("sa", C, (C + 1) * NA, C + 1), [[16, NA]])
    ts(V("dm", 0, 384), V("t16", 0, 384), scol, OP.is_equal)
    ts(V("nd", 0, C), V("t16", 0, C), scol, OP.not_equal)
    ts(V("mx", 0, 384), V("t16", 0, 384), scol, OP.is_le, BIG, OP.mult)
    ts(sm("s", 2, 3), V("pint", 2, 3), 17.0, OP.mult, scol, OP.add)
    ts(ul("tw", 0, 1), sm("s", 2, 3), 16.0, OP.mult, 511.0, OP.min)

    def constants():
        const(V("inv", 0, 16))
        const(V("inv", 16 + C, 288))
        iota(V("iota", 0, 512), [[1, 512]])
        const(V("tb0", 0, 2048, 512))
        const(V("tb1", 0, 2048, 512))
        const(V("xrow", 0, 256), 33)
        for o in (16, 44):
            iota(V("xrow", o + 1, o + 24), [[1, 23]], 1)
            iota(V("xrow", o + 68, o + 88), [[4, 5], [0, 4]], 4)
            const(V("xrow", o + 88, o + 92), 32)
        const(V("xrow", 40, 41), 32)
        iota(V("xrow", 144, 174), [[4, 6], [1, 5]], 1)
        const(V("xrow", 148, 174, 5), 33)
        const(V("xrow", 172, 173), 32)
        iota(V("xrow", 176, 206), [[4, 6], [1, 5]])
        const(V("xrow", 180, 206, 5), 33)
        const(V("xrow", 176, 177), 33)
        iota(V("xrow", 208, 232), [[5, 6], [0, 4]], 4)
        const(V("xrow", 232, 240), 31)
        iota(sm("r", 32, 34), [[1, 2]], int(MAGIC) + C)
        const(V("xr", 0, 16))
        const(V("xr", 208, 224))
        const(V("tc", 192, 256))
        lin(V("idb", 0, S), V("iota", 0, S), bias=OWN - 256.0, on="a")
        const(V("step", 0, L))
        const(V("step", L, C), 1)
        const(V("zer", 0, C))
        const(V("spb", 0, 256), -int(OFF))
        const(V("kt0", 0, 1))
        const(V("kt1", 0, 1))
        iota(sm("m4", 0, 56), [[1, 2], [0, 7], [16, 4]])
        iota(sm("n4"), [[4, 24]])
        const(sm("hz", 24, 32), 95)
        const(sm("sc", 24, 32))
        const(sm("y16", 24, 28))
        const(sm("m5", 0, 32), 1)
        const(sm("m5", 0, 32, 5))
        const(sm("m5", 4, 32, 5), 2)
        const(V("sq", C, 256))
        const(V("suf", C, C + 1), C)
        const(V("suf", C + 1, 256))
        const(V("zz", S, 400), C)
        for b in range(4):
            o = V("et", 512 * b, 512 * b + 512)
            run("g", [V("ones", 0, 512)], [o],
                lambda o=o, b=b: g.affine_select(ap(o), T.ones[:], [[-1, 512]], OP.is_equal, 0.0, b, 4), 1200)
        ts(sm("yf", 0, 56), sm("k2", 0, 56), scol, OP.add, float(C) / S, OP.mult)
        lin(sm("k240m"), sm("k2"), bias=scol, on="a")
        lin(sm("k240m"), sm("k240m"), bias=MAGIC + C, on="a")
        ts(sm("yf", 0, 56), sm("yf", 0, 56), UP, OP.add, MAGIC, OP.add)
        ts(ul("qlo", 0, 24), sm("yf"), -MAGIC, OP.add)
        for a, z in ((0, C), (C, 352)):
            const(V("vv", a, z), -256)
        for b in range(4):
            lin(V("tbl", 2 * HI + b, 4 * HI, 4), sm("yf", 0, 56), bias=-MAGIC, on="a")
        lin(sm("r", 0, 24), sm("yf", 0, 24), on="a")
        lin(sm("o16", 0, 2), sm("c", 0, 2), bias=scol, on="a")
        lin(sm("o16", 0, 2), sm("o16", 0, 2), 1.0 / 16, on="a")
        lin(sm("o64", 0, 56), sm("m4", 0, 56), bias=scol, on="a")
        lin(sm("o64", 0, 56), sm("o64", 0, 56), 1.0 / 64, on="a")
        turned(ul("xc", 0, 16), "xrow", 224, 0.0, "tc")

    def leaf_lists():
        lin(V("xr", 16, 208), IND(sm("r", 0, 64), ul("xc", 0, 12)), bias=-MAGIC)
        turned(ul("xl", 0, 16), "xr", 192, 0.0, "tc")

    def ranking(K, cut):
        def k(a, b):
            return V(K[0], K[1] + a, K[1] + b)

        def w(j):
            return V("wf", 16 * j + 15, 16 * j + 16)

        W = C + 1
        tt(V("eq", 0, C), IND(V("wf", 0, C), ul("lw", 0, 15)), k(0, C), OP.is_equal)
        scan(V("ex", 0, C, -1), V("nd", 0, C, -1), V("eq", 0, C, -1), 0.0, OP.mult, OP.add)
        for j in range(NA - 1, -1, -1):
            for a, z in ((0, cut), (cut, C)) if cut else ((0, C),):
                act(V("sa", W * j + a, W * j + z), k(a, z), AF.Sign, bias=w(j), scale=-1.0)
        for j in range(NA - 1, 0, -1):
            act(V("sa", W * j, W * j + 16 * j), V("sa", W * j, W * j + 16 * j), AF.Relu, scale=-1.0,
                accum=sm("ra", j, j + 1))
        for j in range(NA - 1, -1, -1):
            o, z = W * j + 16 * j, W * j + W
            act(V("sa", o, z), V("sa", o, z), AF.Relu, accum=sm("rb", j, j + 1))
        tt(sm("eb", 0, NA), V("ex", 0, 16 * NA, 16), sm("ra", 0, NA), OP.subtract)
        tt(sm("rb", 0, NA), sm("rb", 0, NA), sm("eb", 0, NA), OP.add)
        for j in range(NA, 15):
            o = C * (j - NA)
            ts(V("cmp", o, o + 16 * j), k(0, 16 * j), w(j), OP.is_le)
            ts(V("cmp", o + 16 * j, o + C), k(16 * j, C), w(j), OP.is_lt)
        for j in range(NA, 15):
            o = C * (j - NA)
            scan(V("so", o // 2, o // 2 + 120), V("cmp", o, o + 120), V("cmp", o + 120, o + C),
                 V("ex", 16 * j, 16 * j + 1), OP.add, OP.add)
        ts(ul("rk", NA, 15), V("so", 119, 120 * (15 - NA), 120), -1.0, OP.add)
        ts(ul("rk", 0, NA), sm("rb", 0, NA), -1.0, OP.add)
        return [(0, NA, sm("rb", 0, NA)), (NA, 15, V("so", 119, 120 * (15 - NA), 120))]

    def parts(e, t, out, b, top, lst, a, z):
        lin(V(out, 4 * a + b, 4 * z, 4), IND(TB(t, b, 0, top), lst), 0.015625, on=e)

    quant("qu", "su", 0, 128, V("us", 0, 512))
    run("v", [V("qu", 0, 128), ul("c16", 0, 8)], [V("qu2", 0, 128)], lambda: g.vector.tensor_copy(
        T.qu2[:, 0:128].bitcast(dt.uint32), T.qu[:, 0:128].bitcast(dt.uint32).indirect(ap(ul("c16", 0, 8)))), 260)
    act(V("su2", 0, 128), IND(V("su", 0, 128), ul("c16", 0, 8)))
    send(T.qup[:].bitcast(dt.uint8), T.qu2[:].bitcast(dt.uint8), [V("qu2", 0, 128)], "au", 512)
    send(T.sup[:], T.su2[:], [V("su2", 0, 128)], "au", 128)
    landed([V("qup", 0, 128), V("sup", 0, 128)], "au")
    for c, (a, z) in enumerate(XP):
        o, n = min(a, C - 128), max(z - a, 128)
        quant("qx", "sx", 256 * c, 256 * c + n, V("xs", 4 * o, 4 * (o + n)))
        mm(2 * c, "qu2", "su2", 0, "qx", "sx", 256 * c, 256 * c + n)
        mm(2 * c + 1, "qu2", "su2", 0, "qx", "sx", 256 * c, 256 * c + n)
        tt(V("wm", a, z), PS(2 * c, a - o, z - o), V("dm", a, z), OP.mult)
        act(V("pp", OWN + a, OWN + z), PS(2 * c + 1, a - o, z - o))
        segsum(V("wf", a, z), V("wm", a, z), z - a)
    ranking(V("pp", OWN, OWN + C), 128 * CUT[0])
    constants()
    cp(IND(V("inv", 16, 16 + C), ul("rk", 0, 15)), V("iota", 0, C))
    turned(ul("to", 0, 16), "inv", 256, float(OWN), "ta")
    for b in range(4):
        lin(TB(0, b, OWN, OWN + C), V("xs", b, 960, 4), 64.0)

    for t in range(R):
        first, last = t == 0, t == R - 1
        cw = 128 if first else CW
        top = OWN + C if t < 2 else 512
        kt, ktn = "kt%d" % (t % 2), "kt%d" % ((t + 1) % 2)
        ch = [(0, cw), (cw, 256 if first else S)]
        cf = ch if first else CF
        q_t, s_t, IDS = "qt%d" % t, "st%d" % t, V("idl%d" % t, 0, 15)

        def gather(c):
            for b in range(4):
                parts(ENG["g%d" % c], t, "fi", b, top, ul("to", cf[c][0] // 16, cf[c][1] // 16), *cf[c])

        def qf(c):
            a, z = cf[c]
            quant("qf", "sf", a, z, V("fi", 4 * a, 4 * z))
            for b in range(4):
                mm(4 * (c % 2) + b, "qw", "sw", 128 * b, "qf", "sf", a, z)

        def f64(c):
            a, z = cf[c]
            lin(V("f64", 4 * a, 4 * z), V("fi", 4 * a, 4 * z), 64.0, on=ENG["f%d" % c])

        def add(c):
            a, z = cf[c]
            for b in range(4):
                tt(TB(t + 1, b, OWN + a, OWN + z), PS(4 * (c % 2) + b, 0, z - a), V("f64", 4 * a + b, 4 * z, 4), OP.add)
                lin(V("ti", 4 * a + b, 4 * z, 4), TB(t + 1, b, OWN + a, OWN + z), 0.015625, on=ENG["t%d" % c])

        def qt(c):
            a, z = ch[c]
            k = 4 * c if len(cf) == 2 else 4 + c
            quant(q_t, s_t, a, z, V("ti", 4 * a, 4 * z))
            mm(k, "qu2", "su2", 0, q_t, s_t, a, z)
            if first:
                mm(k + 1, "qu2", "su2", 0, q_t, s_t, a, z)
                n = min(z, C) - a
                tt(V("wm", a, a + n), PS(k, 0, n), V("dm", 0, n), OP.mult)
            lin(V("pp", OWN + a, OWN + z), PS(k + first, 0, z - a))

        def held(c):
            if not first:
                for a in range(0, 24, 24 // NSC):
                    z = a + 24 // NSC
                    cp(IND(V("srw", 0, 624), ul("d2", a, z)), V("idb", 16 * a, 16 * z))
                pick(V("srx", 0, C), V("srw", 0, C), C)
                ts(IDS, V("srx", 15, C, 16), 256.0, OP.add)
                send(T["idr%d" % t][:, 0:15], ap(IDS), [IDS], "ai%d" % t, 100)

        def keys():
            if first:
                lin(V(kt, OWN, OWN + C), IND(V("pp", 0, OWN + C), ul("to", 0, 15)))
                pick(V("kx", 0, C), V(kt, OWN, OWN + C), C)
            else:
                lin(V(kt, OWN, 512), IND(V(ktn, 0, top), ul("to", 0, 24)))
                lin(V("krow", 0, C), IND(V(kt, 0, 512), IDS))
                pick(V("kx", 0, C), V("krow", 0, C), C)

        if first:
            keys()
        steps = {"g": gather, "q": qf, "f": f64, "a": add, "t": qt, "s": held}
        for s in LAYER.split():
            if int(s[1:] or 0) < len(cf):
                steps[s[0]](int(s[1:] or 0))
        if first:
            K, ids = V("pp", OWN, OWN + C), V("idb", 0, C)
        else:
            for a, z in HALVES:
                P, lst = V("pp", 0, OWN + (cw if 16 * z + S - C <= cw else S)), V(IDS[0], a, z)
                tt(V("wm", 16 * a, 16 * z), IND(P, lst), V("dm", 16 * a, 16 * z), OP.mult)
                lin(V("kk", 16 * a, 16 * z), IND(P, lst), on=ENG["kk"])
            K, ids = V("kk", 0, C), V("srw", 0, C)
        for a, z in ([(0, 8), (8, 15)] if first else HALVES):
            segsum(V("wf", 16 * a, 16 * z), V("wm", 16 * a, 16 * z), 16 * (z - a))

        n, ql, sl, lo, ll = ch[1][1], "ql%d" % t, "sl%d" % t, "lo%d" % t, "ll%d" % t
        for c, (a, z) in enumerate(ch):
            send(T[ql][:, a:z].bitcast(dt.uint8), T[q_t][:, a:z].bitcast(dt.uint8), [V(q_t, a, z)], "ab%d%d" % (c, t),
                 4 * (z - a))
            send(T[sl][:, a:z], T[s_t][:, a:z], [V(s_t, a, z)], "ab%d%d" % (c, t), z - a)
        cut = 128 if first else 96
        rk = ranking(K, cut * CUT[1])
        if not first:
            keys()
        leaf_lists()

        W = C + 1

        def key(j):
            return V("kx", 16 * j + 15, 16 * j + 16)

        def arrive():
            for c, (a, z) in enumerate(ch):
                landed([V(ql, a, z), V(sl, a, z)], "ab%d%d" % (c, t))
                mm(6 + c, "qup", "sup", 0, ql, sl, a, z)
                lin(V("pq", OWN + a, OWN + z), PS(6 + c, 0, z - a))
            if not first:
                landed([V("idr%d" % t, 0, 16)], "ai%d" % t)
                for a, z in HP:
                    lin(V("prow", 16 * a, 16 * z), IND(V("pq", 0, OWN + (cw if 16 * z + S - C <= cw else S)),
                                                       V("idr%d" % t, a, z)))

        PR = V("pq", OWN, OWN + C) if first else V("prow", 0, C)

        def stays():
            lin(V("strow", 0, C), IND(V("step", 0, C), ul("rk", 0, 15)))
            scan(V("spb", 1, C + 1), V("strow", 0, C), V("zer", 0, C), -OFF, OP.add, OP.add)
            pick(V("spe", 0, C), V("spb", 0, C), C)

        def base():
            for a, z, v in rk:
                lin(sm("gn", a, z), v, -2 * BIG, (2 * L + 1) * BIG)
                lin(sm("gh", a, z), v, bias=C - 1 - OFF)
            tt(sm("gh", 0, 15), sm("gh", 0, 15), sm("gn", 0, 15), OP.min)
            tt(sm("base", 0, 15), V("spe", 15, C, 16), sm("gh", 0, 15), OP.max)
            lin(sm("b96", 0, 15), V("spe", 15, C, 16), bias=float(L))
            tt(sm("cap96", 0, 15), sm("b96", 0, 15), sm("gh", 0, 15), OP.max)

        def signs():
            for j in range(NM):
                for a, z in ((0, cut), (cut, C)) if CUT[2] else ((0, C),):
                    act(V("sf2", C * j + a, C * j + z), V(PR[0], PR[1] + a, PR[1] + z), AF.Sign, bias=key(j), scale=-1.0)
            for j in range(NM):
                act(V("sf2", C * j, C * j + C), V("sf2", C * j, C * j + C), AF.Relu, accum=sm("ta", j, j + 1))
            tt(sm("ta", 0, NM), sm("ta", 0, NM), sm("base", 0, NM), OP.add)

        def less():
            for j in range(ND):
                for a, z in ((0, cut), (cut, C)) if j < CUT[3] else ((0, C),):
                    ts(V("mcp", C * j + a, C * j + z), V(PR[0], PR[1] + a, PR[1] + z), key(NM + j), OP.is_lt)
            for j in range(ND):
                scan(V("mso", 120 * j, 120 * j + 120), V("mcp", C * j, C * j + 120), V("mcp", C * j + 120, C * j + C),
                     sm("base", NM + j, NM + j + 1), OP.add, OP.add)

        steps = {"arrive": arrive, "stays": stays, "base": base, "signs": signs, "less": less}
        for s in AFTER.split():
            steps[s]()
        tt(sm("dd", 0, NM), sm("ta", 0, NM), sm("cap96", 0, NM), OP.min)
        tt(sm("dd", NM, 15), V("mso", 119, 120 * ND, 120), sm("cap96", NM, 15), OP.min)
        ts(ul("dest", 0, 15), sm("dd", 0, 15), OFF, OP.add)

        lin(V("qrow", 0, C), IND(V("iota", 0, 512), ul("dest", 0, 15)), on="a")
        for a, z in VH:
            cp(IND(V("vv", 0, 480), ul("dest", a, z)), V(ids[0], 16 * a, 16 * z))
        turned(V(lo, 0, 16), "vv", L, 256.0, "ta", C - 16)
        send(T[ll][:, 0:6], T[lo][:, 0:6], [V(lo, 0, 6)], "al%d" % t, 100)
        scan(V("suf", 0, C, -1), V("zer", 0, C), V("qrow", 0, C, -1), float(C), OP.add, OP.min)
        SUF = V("suf", 0, 256)
        lin(sm("xd", 0, 32), IND(SUF, ul("xl", 10, 12)), bias=float(Q1))
        lin(V("sxx", 0, 32), IND(V("spb", 0, 256), ul("xl", 0, 2)))
        tt(sm("sc"), V("sxx", 1, 25), V("sxx", 0, 24), OP.subtract)
        tt(sm("cls", 0, 32), IND(SUF, ul("xl", 0, 2)), sm("sc", 0, 32), OP.add)
        lin(sm("xa", 0, 64), IND(SUF, ul("xl", 0, 4)))
        lin(sm("xw", 0, 64), IND(SUF, ul("xl", 4, 8)), bias=UP)

        tt(sm("big", 0, 32), IND(SUF, ul("xl", 8, 10)), sm("xd", 0, 32), OP.is_gt)
        tt(sm("has"), sm("xa", 1, 25), sm("cls"), OP.is_gt)
        tt(sm("c64", 0, 52), sm("xw", 4, 56), sm("xw", 0, 52), OP.subtract)
        scan(sm("any", 0, 32), sm("m5", 0, 32), sm("big", 0, 32), 0.0, OP.mult, OP.max)
        tt(sm("hz"), sm("has"), sm("n4"), OP.add)
        ts(sm("w3", 0, 6), sm("c64", 0, 24, 4), float(Q2), OP.is_gt, float(HI), OP.mult)
        tt(sm("mr", 0, 32), IND(sm("any", 0, 32), ul("xc", 12, 14)), sm("hz", 0, 32), OP.add)
        tt(sm("w3", 0, 6), sm("w3", 0, 6), sm("any", 4, 30, 5), OP.mult)
        pick(sm("mw", 0, 32), sm("mr", 0, 32), 32)
        run("v", [sm("w3", 0, 6)], [sm("f3", 0, 1)],
            lambda: g.vector.tensor_reduce(ap(sm("f3", 0, 1)), ap(sm("w3", 0, 6)), AxisListType.X, OP.max), 64)
        ts(ul("md", 0, 2), sm("mw", 15, 32, 16), sm("f3", 0, 1), OP.add)
        lin(V("zz", 0, S), IND(SUF, ul("qlo", 0, 24)), on="a")
        pick(V("e1", 0, S), V("zz", 0, S), S)
        pick(V("e2", 0, S), V("zz", 1, S + 1), S)
        lin(V("tbl", 0, 96, 4), V("e1", 15, S, 16))
        lin(V("tbl", HI, HI + 96, 4), V("e2", 15, S, 16))
        tt(sm("cnt"), sm("xa", 1, 25), sm("xa", 0, 24), OP.subtract)
        tt(sm("y64", 0, 52), sm("c64", 0, 52), sm("o64", 0, 52), OP.mult)
        tt(V("tbl", 2, 208, 4), sm("y64", 0, 52), sm("xw", 0, 52), OP.add)
        lin(V("tbl", 3, 208, 4), V("tbl", 2, 208, 4))
        lin(sm("y16", 0, 24), sm("cnt"), sm("o16", 0, 1), UP)
        lin(sm("y16", 28, 52), sm("cnt"), sm("o16", 1, 2), UP)
        tt(V("tbl", 1, 208, 4), sm("y16", 0, 52), sm("xa", 0, 52), OP.add)
        note({"a": act_way(V("isa", 0, C), V("vv", 0, C), AF.Relu, -255.0, -1.0),
              "v": ts_way(V("isa", 0, C), V("vv", 0, C), -255.5, OP.is_lt)}, [V("vv", 0, C)], [V("isa", 0, C)])
        scan(V("aa", 0, C), V("isa", 0, C), V("zer", 0, C), float(ARR - 257), OP.add, OP.add)
        scan(V("sq", 0, C, -1), V("aa", 0, C, -1), V("vv", 0, C, -1), BIG, OP.min, OP.max)
        ts(ul("qlo", 0, 32), IND(V("tbl", 0, 3 * HI), ul("md", 0, 2)), MAGIC, OP.add, -MAGIC, OP.add)
        lin(sm("r", 0, 32), IND(V("tbl", 0, 3 * HI), ul("md", 0, 2)), bias=MAGIC, on="a")
        lin(sm("rh", 0, 32), IND(V("tbl", HI, 4 * HI), ul("md", 0, 2)), bias=MAGIC, on="a")
        tt(sm("gap"), sm("rh"), sm("r"), OP.is_le)
        tt(sm("gap"), sm("gap"), sm("k240m"), OP.mult)
        for a, z in TAIL:
            tt(V("wb", 16 * a, 16 * z), IND(V("sq", 0, 256), ul("qlo", a, z)), V("dm", 16 * a, 16 * z), OP.mult)
            segsum(V("wb2", 16 * a, 16 * z), V("wb", 16 * a, 16 * z), 16 * (z - a))
            tt(sm("tw", a, z), V("wb2", 16 * a + 15, 16 * z, 16), sm("gap", a, z), OP.subtract)
            ts(ul("to", a, z), sm("tw", a, z), 256.0, OP.add)
        if not last:
            tt(sm("d1"), sm("r"), sm("gap"), OP.max)
            ts(ul("d2", 0, 24), sm("d1"), -MAGIC, OP.add)

        if first:
            quant("qe", "se", 0, 256, V("et", 0, 1024))
            quant("qe", "se", 256, 512, V("et", 1024, 2048))
            const(V("idmap", 0, ARR), -1)
            iota(V("idmap", ARR, OWN), [[1, L]], S)
            iota(V("idmap", OWN, 512), [[1, S]])
            quant("qv", "sv", 0, 128, V("vs", 0, 512))
        landed([V(ll, 0, 6)], "al%d" % t)
        for b in range(4):
            mm(b, "qe", "se", 128 * b, ql, sl, 0, n)
            lin(V("df", 512 * b + OWN, 512 * b + OWN + n), PS(b, 0, n), 64.0, on="a")
        for b in range(4):
            lin(TB(t + 1, b, ARR, OWN), IND(V("df", 512 * b, 512 * b + OWN + n), V(ll, 0, 6)))
        if not last:
            iota(V("vv", 0, C), [[0, C]], -256)
            lin(V(kt, ARR, OWN), IND(V("pq", 0, OWN + n), V(ll, 0, 6)))

    for c, (a, z) in enumerate(OUTS):
        for b in range(4):
            parts("va", R, "fi", b, 512, ul("to", a // 16, z // 16), a, z)
        quant("qf", "sf", a, z, V("fi", 4 * a, 4 * z))
        mm(c, "qv", "sv", 0, "qf", "sf", a, z)
        lin(V("yo", a, z), PS(c, 0, z - a))
        store("sa"[z == S], T.y[:, a:z], T.yo[:, a:z], [V("yo", a, z)], 4 * (z - a))
        store("s", T.oc[:, 4 * a:4 * z], T.qf[:, a:z].bitcast(dt.uint8), [V("qf", a, z)], 4 * (z - a))
    lin(V("olr", 0, S), IND(V("idmap", 0, 512), ul("to", 0, 24)))
    for k in range(4):
        store("s", T.osc[4 * k:4 * k + 4, :], T.sf[32 * k:32 * k + 4, :], [V("sf", 0, S)], 50)
    store("a", T.ol[:], T.olr[0:128:16, :], [V("olr", 0, S)], 150)

    issue()
    lastval = {}
    for sem, val, seen in ops.values():
        lastval[sem] = max(lastval.get(sem, 0), val)
    for sem in lastval:
        if waited.get(sem, 0) < lastval[sem]:
            g.wait_ge(T.sem[sem], lastval[sem])
    for sem in total:
        g.wait_ge(T.sem[sem], total[sem])
